import numpy as np, ml_dtypes
CORES = [16,18,20,22]
N = 4
BF = ml_dtypes.bfloat16
def entries(a):
    return np.ascontiguousarray(a.T).reshape(-1)
def table(e):
    return np.ascontiguousarray(np.reshape(e, (-1, 16)).T).astype(np.int32)
def f(rng, *shape):
    return (rng.standard_normal(shape, dtype=np.float32) * np.exp2(rng.integers(-2, 3, shape[:-1] + (1,)))).astype(BF)
def wide(rng, *shape):
    v = f(rng, *shape).astype(np.float32); k = shape[:-2] + (1, shape[-1])
    return (v * np.exp2(rng.integers(-6, 7, k)) * (rng.random(k) > 0.0625)).astype(BF)
R, S1, S2, CAPP = 4096, 512, 512, 32
T1, T2 = 0, 100
def orders(rng):
    return np.stack([rng.permutation(R) for r in range(N)])
def values(rng, order, n1, m, lo):
    v = rng.integers(-60, 1, (N, R))
    for r in range(N):
        v[r, order[r, :n1[r]]] = rng.integers(1, 5, n1[r]); v[r, order[r, :m[r]]] = rng.integers(lo[r], 256, m[r])
    x = f(rng, N, 16, R); x[:, 0] = v.astype(np.float32).astype(BF); return x
def some(rng, order, n1, m, *shape):
    top = np.array([m, n1, R])[rng.integers(0, 3, shape)]
    return order[(rng.random(shape) * top).astype(np.int64)]
def ghosts(rng, r, *shape):
    return R + ((r + 1 + rng.integers(0, N - 1, shape)) % N) * CAPP + rng.integers(0, CAPP, shape)
def draw(rng, order, n1, m, lo):
    x = values(rng, order, n1, m, lo); nb = []; bd = []
    for r in range(N):
        nb.append(np.where(rng.random((6, R)) < 0.7, some(rng, order[r], n1[r], m[r], 6, R), ghosts(rng, r, 6, R)))
        bd.append(table(some(rng, order[r], n1[r], m[r], N * CAPP)))
    return {"x": x, "nb": np.stack(nb).astype(np.int32), "bd": np.stack(bd)}
def setup_inputs(rng):
    return draw(rng, orders(rng), rng.integers(3 * S1 // 4, S1 + 1, N), np.full(N, S2 // 8), np.full(N, 40))
def setup_inputs_full(rng):
    order = orders(rng); a = int(rng.integers(0, N)); order[a] = np.arange(R); order[(a + 1) % N] = np.arange(R)[::-1]
    return draw(rng, order, np.full(N, S1), np.full(N, S2 // 8), np.full(N, 200))
def setup_inputs_ties(rng):
    order = orders(rng); n1 = rng.integers(3 * S1 // 4, S1 + 1, N); m = S2 // 8
    d = draw(rng, order, n1, np.full(N, m), np.full(N, 40)); x, nb = d["x"], d["nb"]; bd = []
    for r in range(N):
        h = order[r, :m]; c = order[r, n1[r]:]
        x[r, 0, h] = rng.integers(99, 102, m).astype(np.float32).astype(BF); x[r, 0, c] = rng.integers(-1, 1, len(c)).astype(np.float32).astype(BF)
        nb[r][:, h] = np.where(rng.random((6, m)) < 0.5, h[rng.integers(0, m, (6, m))], ghosts(rng, r, 6, m))
        nb[r][:, h[0]] = h[0]; x[r, 0, h[0]] = 100; nb[r][:, h[1]] = h[1]; x[r, 0, h[1]] = 101
        bd.append(table(h[rng.integers(0, m, N * CAPP)]))
    d["bd"] = np.stack(bd); return d
def setup_inputs_thin(rng):
    order = orders(rng); n1 = rng.integers(3 * S1 // 4, S1 + 1, N); m = np.minimum(S2 // 4, n1)
    d = draw(rng, order, n1, m, np.full(N, 40)); x, nb, bd = d["x"], d["nb"], d["bd"]; first = int(rng.integers(0, 6))
    for r in range(N):
        k = int(m[r]); h = order[r, :k]; c = order[r, n1[r]:]
        x[r, 0, h] = rng.integers(101, 104, k).astype(np.float32).astype(BF)
        nb[r][:, h] = np.where(rng.random((6, k)) < 0.5, h[rng.integers(0, k, (6, k))], ghosts(rng, r, 6, k))
        nb[r][(first + r) % 6, h] = c[rng.integers(0, len(c), k)]
        bd[r] = table(h[rng.integers(0, k, N * CAPP)])
    return d
def setup_inputs_far(rng):
    order = orders(rng); n1 = rng.integers(3 * S1 // 4, S1 + 1, N); m = np.full(N, S2 // 8); lo = np.full(N, 40); a = int(rng.integers(0, N)); b = (a + 1) % N; s = int(rng.integers(1, N))
    n1[a] = S1 // 8; m[a] = S2 // 64; lo[a] = 200
    d = draw(rng, order, n1, m, lo); nb, bd = d["nb"], d["bd"]
    for r in range(N):
        if r != a: nb[r] = R + ((r + s) % N) * CAPP + rng.integers(0, CAPP, (6, R))
        top = np.where(rng.random(N * CAPP) < 0.5, m[r], n1[r]); e = (rng.random(N * CAPP) * top).astype(np.int64)
        if r == a: e = rng.integers(n1[a], R, N * CAPP)
        if r == b: e = rng.integers(0, m[b], N * CAPP)
        bd[r] = table(order[r][e])
    return d
def setup_inputs_spread(rng):
    d = setup_inputs(rng); d["x"][:, 1:] = wide(rng, N, 16, R)[:, 1:]; return d
def grow(x, nb, bd):
    v = np.concatenate([a.astype(np.float64).T for a in x])
    w = np.stack([entries(a) for a in bd]).astype(np.int64).reshape(N, N, CAPP); near = []
    for r in range(N):
        ext = np.concatenate([r * R + np.arange(R), (R * np.arange(N)[:, None] + w[:, r]).reshape(-1)])
        near.append(ext[nb[r]].T)
    near = np.concatenate(near)
    p = np.flatnonzero(v[:, 0] > T1); number = np.full(N * R, -1); number[p] = np.arange(len(p)); kids = []
    for o in range(8):
        c = v[p].copy()
        for d in range(3): c += 0.125 * (v[near[p, 2 * d + (o >> d & 1)]] - v[p])
        kids.append(c)
    return v, near, p, number, np.stack(kids)
def check_inputs(d):
    bad = []; x = d["x"].astype(np.float32); nb, bd = d["nb"], d["bd"]
    if not np.isfinite(x).all() or not (np.abs(x) <= 65536).all(): bad.append("x finite and of size at most 65536")
    elif (x[:, 0] != np.floor(x[:, 0])).any() or (np.abs(x[:, 0]) > 256).any(): bad.append("x channel 0")
    own = (nb - R) // CAPP == np.arange(N)[:, None, None]
    if (nb < 0).any() or (nb >= R + N * CAPP).any() or own.any(): bad.append("nb")
    if (bd < 0).any() or (bd >= R).any(): bad.append("bd")
    if bad: return bad
    v, near, p, number, c1 = grow(d["x"], nb, bd); q = p // R
    if (np.bincount(q, minlength=N) > S1).any(): bad.append("splits of level 1")
    if (np.bincount(q[np.nonzero(c1[:, :, 0] > T2)[1]], minlength=N) > S2).any(): bad.append("splits of level 2")
    return bad
def reference(x, nb, bd):
    v, near, p, number, c1 = grow(x, nb, bd)
    O, S = np.nonzero(c1[:, :, 0] > T2)
    number2 = np.full(c1.shape[:2], -1); number2[O, S] = np.arange(len(O)); mid = c1[O, S]; val = {}; fine = {}
    for d in range(3):
        for b in range(2):
            m = near[p[S], 2 * d + b]; t = np.where((O >> d & 1) != b, S, number[m]); o = O ^ (1 << d)
            val[d, b] = np.where((t >= 0)[:, None], c1[o, t], v[m]); fine[d, b] = np.where(t >= 0, number2[o, t], -1)
    c2 = []
    for o in range(8):
        c = mid.copy()
        for d in range(3): c += 0.125 * (val[d, o >> d & 1] - mid)
        c2.append(c)
    c2 = np.stack(c2); z = 0.25 * c2
    for o in range(8):
        for d in range(3):
            b = o >> d & 1; other = c2[o ^ (1 << d)]; u = fine[d, b]
            z[o] += 0.125 * (other + np.where((u >= 0)[:, None], other[u], val[d, b]))
    y1 = np.zeros((N, 8, 16, S1)); y2 = np.zeros((N, 8, 16, S2))
    for r in range(N):
        a = c1[:, p // R == r]; y1[r, :, :, :a.shape[1]] = a.transpose(0, 2, 1)
        a = z[:, p[S] // R == r]; y2[r, :, :, :a.shape[1]] = a.transpose(0, 2, 1)
    return {"y1": y1.reshape(N, 128, S1).astype(np.float32), "y2": y2.reshape(N, 128, S2).astype(np.float32)}

@@ -1,0 +1,625 @@
+from concourse.bass import DstId, RemoteDMATransfer
+from concourse.mybir import AluOpType, ActivationFunctionType
+
+F32, BF, F16, I32, U16 = "float32", "bfloat16", "float16", "int32", "uint16"
+ZC = 4224
+ST = 608
+ROOT = 16 + 8 * ST
+DUM = 5632
+BIG = 16384
+
+SB = {
+    "xw": (4240, BF), "xn": (512, BF), "x0": (512, BF), "d1": (512, I32), "bdi": (8, I32), "bdk": (32, I32),
+    "bdf": (32, F16), "bdu": (32, U16), "mka": (128, BF), "xa": (128, BF), "rx": (128, BF),
+    "i8": (8, F32), "w1": (8192, F32), "w2": (8192, F32), "gw": (640, BF), "gb": (128, BF), "gg": (96, BF),
+    "onesb": (512, BF), "onesf": (128, F32), "b1": (144, BF), "b2": (144, BF), "pi": (4, I32), "pk": (8, I32),
+    "col": (24, F32), "iog": (128, BF), "iom": (128, BF), "bo": (128, BF), "prev": (128, BF), "rf": (128, BF),
+    "ident": (128, BF), "tri0": (128, BF), "tri": (128, BF), "k64": (32, BF), "dc": (32, F16), "i16": (16, F32),
+    "pa0": (128, BF), "pa1": (128, BF), "n2h": (32, F16), "offh": (32, F16), "io8": (8, I32),
+    "ee": (256, BF), "c1": (136, F32), "c4": (136, F32), "c2": (136, BF), "c3": (136, BF), "sel": (192, F32),
+    "obi": (8, I32), "obt": (8, F32), "m8": (32, F32), "lj": (8, U16), "wc": (128, F32), "wz": (128, F32),
+    "wm": (128, F32), "wo": (1024, BF), "bc": (128, BF), "rt": (128, BF), "pm": (256, F32), "urow": (128, F32),
+    "ios": (512, F32), "nr": (512, F32), "jb": (8, F32), "cc": (8, F32), "nw": (272, F32), "nw2": (344, F32),
+    "n2w": (40, F32), "nf": (64, BF), "sc": (80, BF), "nd": (64, F16), "off": (64, U16), "offf": (32, F32),
+    "sw": (320, F32), "sb": (32, F32), "l1u": (32, U16), "l2u": (32, U16), "li": (32, I32), "lcr": (64, I32),
+    "lcu": (64, U16), "li2": (32, I32), "lcr2": (64, I32), "lcu2": (64, U16), "bi": (8, I32), "bcr": (16, I32),
+    "bcu": (16, U16), "mk": (640, BF), "tm": (640, F16), "mk2": (512, BF), "tm2": (512, F16), "mkb": (128, BF),
+    "tmb": (128, F16), "nb1": (8, F32), "nb2": (8, F32), "lbu": (8, U16), "nbb": (8, F16), "l8u": (64, U16),
+    "lfu": (96, U16), "d2": (512, F32), "t1": (ROOT + 512, F32), "v": (512, F32), "sg": (512, BF),
+    "vs": (512, F32), "win": (1296, F32), "cb": (1024, F32), "gd": (1536, F32), "yo": (512, F32),
+}
+SCRATCH = {k: ("sbuf", [128, v[0]], v[1]) for k, v in SB.items()}
+PSUM = ["pa", "pb", "pc", "pd", "p0", "p1", "p2", "pz"]
+for _p in PSUM:
+    SCRATCH[_p] = ("psum", [128, 512], F32)
+SEMAPHORES = ["cv", "ca", "ct", "cg", "lx0", "lbd", "lnb", "lxn", "lx", "oy1", "oy2", "arra", "arrb", "arrc", "sent"]
+ENG_SEM = {"v": "cv", "a": "ca", "t": "ct", "g": "cg"}
+POOL = ("pool", 0, 1, 1, 0, 128, 1)
+GAP = 0.11
+VEC = 0.00104
+PE = 0.00052
+TRIES = 3000
+SLACK = 0.1
+PLANS = {}
+
+
+def A(name, c0=0, c1=None, cs=1, p0=0, p1=128, ps=1):
+    if c1 is None:
+        c1 = SB[name][0] if name in SB else 512
+    return (name, c0, c1, cs, p0, p1, ps)
+
+
+def overlap(a, b):
+    if a[0] != b[0] or a[1] >= b[2] or b[1] >= a[2] or a[4] >= b[5] or b[4] >= a[5]:
+        return False
+    return not (a[3] == b[3] and (a[1] - b[1]) % a[3])
+
+
+def conflict(o, p):
+    if p["sem"] and p["sem"] == o["sem"]:
+        return False
+    if o["names"].isdisjoint(p["names"]):
+        return False
+    if any(overlap(a, b) for a in o["w"] for b in p["w"] + p["r"]) or any(overlap(a, b) for a in o["r"] for b in p["w"]):
+        return True
+    return (p["e"] != o["e"] or o["e"] in "t*") and not o["banks"].isdisjoint(p["banks"])
+
+
+def unfenced(o, p):
+    return p["e"] == "t" and o["e"] == "t" and p["tile"] == o["tile"]
+
+
+def arrange(ops):
+    n = len(ops)
+    pred = [[j for j in range(i) if conflict(ops[i], ops[j]) or j in ops[i]["after"]] for i in range(n)]
+    level = [o["c"] + o["lat"] + o["pri"] for o in ops]
+    for i in range(n - 1, -1, -1):
+        for j in pred[i]:
+            level[j] = max(level[j], ops[j]["c"] + ops[j]["lat"] + ops[j]["pri"] + level[i] + GAP)
+    succ = [[] for _ in range(n)]
+    for i in range(n):
+        for j in pred[i]:
+            succ[j].append(i)
+
+    def sweep(key, before, behind, back):
+        busy = {}
+        start, end, pick = [0.0] * n, [0.0] * n, [None] * n
+        left = [len(p) for p in before]
+        ready = [i for i in range(n) if not left[i]]
+        while ready:
+            i = max(ready, key=lambda x: key[x])
+            ready.remove(i)
+            o = ops[i]
+            t0 = max([end[j] + (0.0 if unfenced(o, ops[j]) else GAP) for j in before[i]] + [0.0])
+            t0 += o["lat"] if back else 0.0
+            top = None
+            for e, f, c in o["alt"]:
+                t = t0
+                for a, b in busy.setdefault(e, []):
+                    if t + c <= a:
+                        break
+                    if b > t:
+                        t = b
+                if top is None or t + c < top[0]:
+                    top = (t + c, t, e)
+            start[i], end[i], pick[i] = top[1], top[0] + (0.0 if back else o["lat"]), top[2]
+            if top[2] != "-":
+                busy[top[2]].append((top[1], top[0]))
+                busy[top[2]].sort()
+            for k in behind[i]:
+                left[k] -= 1
+                if not left[k]:
+                    ready.append(k)
+        return start, end, pick
+
+    seed = [12345]
+
+    def rand():
+        seed[0] = (seed[0] * 1103515245 + 12345) % 2147483648
+        return seed[0] / 2147483648
+
+    name = str(pred)
+    if name not in PLANS:
+        best = None
+        key = level
+        for trial in range(TRIES):
+            start, end, pick = sweep(key, pred, succ, False)
+            score = max(end) + 0.001 * sum(end) / n
+            if best is None or score <= best[0] + SLACK * rand() * (1 - trial / TRIES):
+                best = (score, start)
+                if name not in PLANS or score < PLANS[name][0]:
+                    PLANS[name] = (score, start, pick)
+            if trial % 8 == 0:
+                key = [x + o["pri"] for x, o in zip(sweep(end, succ, pred, True)[1], ops)]
+            else:
+                key = [o["pri"] - x for x, o in zip(best[1], ops)]
+                for _ in range(1 + trial % 12):
+                    key[int(rand() * n)] += 3.0 * (rand() - 0.4)
+    score, start, pick = PLANS[name]
+    for o, e in zip(ops, pick):
+        o["e"], o["f"] = [x[:2] for x in o["alt"] if x[0] == e][0]
+    return [ops[i] for i in sorted(range(n), key=lambda x: (start[x], x))]
+
+
+def emit(g, T, ops):
+    queue = {"v": g.vector, "a": g.scalar, "t": g.tensor, "g": g, "s": g.sync}
+    n = len(ops)
+    total = {}
+    for o in ops:
+        if o["sem"]:
+            total[o["sem"]] = total.get(o["sem"], 0) + o["inc"]
+    known = {e: {} for e in queue}
+    clock = [{} for _ in range(n)]
+    waits = [[] for _ in range(n)]
+    needed = set()
+    for i, o in enumerate(ops):
+        e = o["e"]
+        if e == "-":
+            continue
+        dep = {}
+        for j in range(i):
+            p = ops[j]
+            if not unfenced(o, p) and conflict(o, p):
+                dep[p["sem"] or p["e"]] = j
+        k = known[e]
+        for src, j in sorted(dep.items(), key=lambda t: -t[1]):
+            if k.get(src, -1) >= j:
+                continue
+            waits[i].append(j)
+            needed.add(j)
+            k[src] = n if ops[j]["sem"] else j
+            for s2, j2 in clock[j].items():
+                if k.get(s2, -1) < j2:
+                    k[s2] = j2
+        clock[i] = dict(k)
+    count = {}
+    value = {}
+    for i, o in enumerate(ops):
+        if not o["sem"] and i in needed:
+            count[o["e"]] = count.get(o["e"], 0) + 1
+            value[i] = count[o["e"]]
+    for i, o in enumerate(ops):
+        if o["e"] == "-":
+            continue
+        q = queue[o["e"]]
+        for j in waits[i]:
+            if ops[j]["sem"]:
+                q.wait_ge(T.sem[ops[j]["sem"]], total[ops[j]["sem"]])
+            else:
+                q.wait_ge(T.sem[ENG_SEM[ops[j]["e"]]], value[j])
+        ins = o["f"](q)
+        if o["dma"]:
+            ins.then_inc(T.sem[o["sem"]], 16)
+        elif i in value:
+            ins.then_inc(T.sem[ENG_SEM[o["e"]]], 1)
+    return total
+
+
+def rank_program(g, core, T, topo):
+    rank = T.rank_of(core)
+    if rank is None:
+        return
+    cores = list(T.cores)
+    peers = [q for q in range(len(cores)) if q != rank]
+    Op, Fn = AluOpType, ActivationFunctionType
+    ops = []
+
+    def ap(r):
+        if r[0] == "ind":
+            return ap(r[1]).indirect(ap(r[2]))
+        return T[r[0]][r[4]:r[5]:r[6], r[1]:r[2]:r[3]]
+
+    def width(r):
+        return len(range(r[1], r[2], r[3]))
+
+    def add(e, f, w, r, c, sem=None, inc=0, dma=False, lat=0.0, pri=0.0, after=(), alt=None, tile=None):
+        ww, rr = [], []
+        for x in r:
+            if isinstance(x, tuple):
+                rr += [x[1], x[2]] if x[0] == "ind" else [x]
+        for x in w:
+            if x[0] == "ind":
+                ww.append(x[1])
+                rr.append(x[2])
+            else:
+                ww.append(x)
+        names = set(x[0] for x in ww + rr)
+        ops.append({"e": e, "f": f, "w": ww, "r": rr, "sem": sem, "inc": inc, "dma": dma, "c": c, "lat": lat,
+                    "pri": pri, "after": after, "names": names, "banks": names & set(PSUM), "tile": tile,
+                    "alt": alt or [(e, f, c)]})
+        return len(ops) - 1
+
+    def narrow(r):
+        return r[0] in SB and SB[r[0]][1] in (BF, F16, U16)
+
+    def cost(o, i, cyc=1.0):
+        if o[0] == "ind":
+            return 0.06 + 16 * width(o[2]) * 3.8 * VEC
+        if i[0] == "ind":
+            return 0.06 + 16 * width(i[2]) * 1.56 * VEC
+        return max(64, width(o) * cyc) * VEC
+
+    def half(o, i):
+        return cost(o, i, 0.5 if narrow(o) and narrow(i) else 1.0)
+
+    def sc(s):
+        return ap(s) if isinstance(s, tuple) else s
+
+    def ind(win, off):
+        return ("ind", win, off)
+
+    def memset(o, c):
+        add("v", lambda q: q.memset(ap(o), c), [o], [], half(o, o))
+
+    def copy(o, i):
+        add("v", lambda q: q.tensor_copy(ap(o), ap(i)), [o], [i], half(o, i))
+
+    def ts(o, i, s1, op0, s2=None, op1=None):
+        if op1 is None:
+            add("v", lambda q: q.tensor_scalar(ap(o), ap(i), sc(s1), None, op0), [o], [i, s1], half(o, i))
+        else:
+            add("v", lambda q: q.tensor_scalar(ap(o), ap(i), sc(s1), sc(s2), op0, op1), [o], [i, s1, s2], half(o, i))
+
+    def tt(o, a, b, op):
+        add("v", lambda q: q.tensor_tensor(ap(o), ap(a), ap(b), op), [o], [a, b],
+            cost(o, a, 1.0 if a[0] in PSUM or b[0] in PSUM else 2.0))
+
+    def scan(o, a, b, op0, op1, first=0.0):
+        add("v", lambda q: q.tensor_tensor_scan(ap(o), ap(a), ap(b), sc(first), op0, op1), [o], [a, b, first], half(o, a))
+
+    def aff(o, i, scale=None, bias=None, e="*"):
+        kw = {}
+        if bias is not None:
+            kw["bias"] = bias
+        if scale is not None:
+            kw["scale"] = scale
+
+        def on_a(q):
+            return q.activation(ap(o), ap(i), Fn.Identity if kw else Fn.Copy, **{k: sc(x) for k, x in kw.items()})
+
+        def on_v(q):
+            if not kw:
+                return q.tensor_copy(ap(o), ap(i))
+            if scale is None:
+                return q.tensor_scalar(ap(o), ap(i), sc(bias), None, Op.add)
+            if bias is None:
+                return q.tensor_scalar(ap(o), ap(i), sc(scale), None, Op.mult)
+            return q.tensor_scalar(ap(o), ap(i), sc(scale), sc(bias), Op.mult, Op.add)
+        alt = [x for x in (("a", on_a, cost(o, i) + 0.015), ("v", on_v, half(o, i))) if e in ("*", x[0])]
+        add(e, alt[0][1], [o], [i, scale, bias], alt[0][2], alt=alt)
+
+    def fill(o, c):
+        src = A("onesb", 0, width(o), 1, o[4], o[5])
+        alt = [("a", lambda q: q.activation(ap(o), ap(src), Fn.Identity, scale=float(c)), cost(o, o) + 0.015),
+               ("v", lambda q: q.memset(ap(o), c), half(o, o))]
+        add("*", alt[0][1], [o], [src], alt[0][2], alt=alt)
+
+    def mm(o, l, r, start=True, stop=True):
+        add("t", lambda q: q.matmul(ap(o), ap(l), ap(r), start, stop), [o], [l, r],
+            max(64, width(r)) * PE * (4 if SB[l[0]][1] == F32 else 1), tile=(l[4], l[5]))
+
+    def iota(o, pat, base, cm, pri=0.0):
+        kw = {} if SB[o[0]][1] == I32 else {"allow_small_or_imprecise_dtypes": True}
+        add("g", lambda q: q.iota(ap(o), pat, base, cm, **kw), [o], [], 0.16 + width(o) * 2 * VEC, pri=pri)
+
+    def asel(o, i, pat, cmp, base, cm):
+        add("g", lambda q: q.affine_select(ap(o), ap(i), pat, cmp, 0.0, base, cm), [o], [i],
+            0.21 + width(o) * 2 * VEC)
+
+    def load(e, o, src, sem, lat, pri, after=()):
+        return add(e, lambda q: q.dma_start(ap(o), src), [o], [], 0.06, sem, 16, True, lat, pri, after)
+
+    def store(e, dst, i, sem):
+        add(e, lambda q: q.dma_start(dst, ap(i)), [], [i], 0.06, sem, 16, True, 2.2)
+
+    def slot(at, q):
+        return q if q < at else q - 1
+
+    def fused(src_of, dst_of, sem, turn, c):
+        tr = []
+        n = 0
+        for q in peers:
+            en = topo.engines(core, cores[q])
+            w = len(en) // 4
+            j = slot(rank, q) + turn
+            rid, pid = topo.addr(cores[q])[:2]
+            tr.append(RemoteDMATransfer(dst_ids=[DstId(rid=rid, pnc=pid)],
+                                        dma_engine_mask=sum(1 << e for e in en[j * w:(j + 1) * w]),
+                                        remote_sem=T.sem[sem], src=ap(src_of(q)), dst=ap(dst_of(q))))
+            n += w
+        return add("g", lambda x: x.remote_dma_fused(tr, local_sem=T.sem.sent), [], [src_of(q) for q in peers], c,
+                   "sent", n, lat=2.3)
+
+    def arrive(regions, sem, div, after):
+        n = sum(len(topo.engines(cores[q], core)) // div for q in peers)
+        add("-", None, regions, [], 0.0, sem, n, after=after)
+
+    def wrap8(o, c, src, n, p0=0, p1=128):
+        for b in range(8):
+            mm(o, A(c, 7 - b, 135 - b, 1, p0, p1), A(src[0], src[1] + b, src[1] + n, 8, p0, p1), b == 0, b == 7)
+
+    def spread(o_of, src):
+        for gr in range(8):
+            a, h = gr // 2, gr % 2
+            mm(o_of(gr), A("ee", 128 * h, 128 * h + 128, 1, 32 * a, 32 * a + 32),
+               A(src[0], src[1], src[2], 1, 32 * a, 32 * a + 32))
+
+    (rcol, kcol, hcol, c8col, g8col, pcol, r4col, h0col, ccol, b1col, sbcol, k6col, zc0, zc, nrc, tcol,
+     bias2) = [A("col", i, i + 1) for i in range(17)]
+
+    def number(lv, second):
+        c = 32 * lv
+        nf, nd = A("nf", c, c + 32), A("nd", c, c + 32)
+        s0 = 40 * lv
+        ts(nf, A("pa", 32 + c, 64 + c), 100.0 * lv, Op.is_le)
+        scan(A("sc", s0 + 1, s0 + 33), A("onesb", 0, 32), nf, Op.add, Op.subtract)
+        tt(nd, nf, A("dc"), Op.mult)
+        p1, pc = A("pb", 64 * lv, 64 * lv + 32), A("pb", 64 * lv + 32, 64 * lv + 33)
+        mm(p1, A("tri"), nf, True, False)
+        mm(p1, A("bo"), A("sc", s0, s0 + 32), False, False)
+        mm(p1, A("ident"), nd, False, True)
+        mm(pc, A("prev"), A("sc", s0 + 32, s0 + 33))
+        ts(A("off", c, c + 32), p1, pc, Op.add, rcol, Op.add)
+        ts(second, p1, pc, Op.add, rcol, Op.add)
+
+    iota(A("pi", 0, 1), [[0, 1]], 0, 1, 200.0)
+    first = len(ops)
+    iota(A("d1"), [[1, 512]], -192, 32, 50.0)
+    load("s", A("x0", p1=8), T.x[0, :], "lx0", 1.9, 90.0)
+    load("a", A("bdi", p1=16), T.bd[:, :], "lbd", 1.9, 90.0)
+    load("s", A("xn"), T.x[:, :], "lxn", 2.4, 80.0)
+    for k in range(6):
+        load("sa"[k % 2], A("d1", 0, 512, 1, k, 128, 16), T.nb[k, :], "lnb", 2.1, 40.0)
+    for k in range(8):
+        load("s", A("xw", 0, 4096, 1, 16 * k, 16 * k + 16), T.x[:, :], "lx", 4.5, 70.0 if k < 2 else 0.0,
+             () if k < 2 else (first,))
+
+    memset(A("onesb"), 1.0)
+    fill(A("pa0"), 1.0)
+    fill(A("pa0", 0, 128, 16), 0.0)
+    fill(A("pa1"), 0.0)
+    fill(A("pa1", 0, 128, 16), 1.0)
+    scan(A("iom"), A("onesb", 0, 128), A("pa0"), Op.add, Op.mult)
+    scan(A("iog"), A("pa1"), A("onesb", 0, 128), Op.add, Op.mult, -1.0)
+    fill(A("k64"), 64.0)
+    fill(A("w1", 0, 512), 0.0)
+    iota(A("w2", 0, 512), [[0, 512]], 0, 0)
+    fill(A("sc"), 0.0)
+    fill(A("sel"), -65536.0)
+    fill(A("xw", ZC, 4240), 0.0)
+    fill(A("xw", 4096 + 32 * rank, 4128 + 32 * rank), 0.0)
+    fill(A("onesf"), 1.0)
+    for c in ("c1", "c2", "c3", "c4", "b1", "b2"):
+        fill(A(c), 0.0)
+    fill(A("nw", 264, 272), 8000.0)
+    fill(A("n2w", 32, 40), 512.0)
+    fill(A("t1", 0, 16), 0.0)
+    fill(A("nw2", 0, 8), 512.0)
+    fill(A("nw2", 304, 344), 512.0)
+    fill(A("win", 512, 528), 0.0)
+    ts(A("pk", 0, 1), A("pi", 0, 1), 15, Op.bitwise_and)
+    ts(A("pk", 1, 2), A("pi", 0, 1), 4, Op.logical_shift_right)
+    ts(A("pk", 2, 3), A("pi", 0, 1), 4, Op.logical_shift_right, 1, Op.bitwise_and)
+    ts(A("pk", 3, 4), A("pi", 0, 1), 3, Op.logical_shift_right)
+    ts(A("pk", 4, 5), A("pi", 0, 1), 7, Op.bitwise_and)
+    copy(A("col", 0, 5), A("pk", 0, 5))
+    copy(pcol, A("pi", 0, 1))
+    ts(A("b1", 15, 128, 16), A("iom", 0, 8), pcol, Op.is_equal)
+    ts(A("bo"), A("iog"), kcol, Op.is_equal)
+    asel(A("prev"), A("onesb", 0, 128), [[16, 8], [0, 16]], Op.is_gt, 0, -1)
+    ts(A("tri0"), A("iog"), kcol, Op.is_equal, -1.0, Op.mult)
+    ts(A("rf"), A("iom"), rcol, Op.is_equal)
+    aff(r4col, rcol, 4.0, DUM - 64.0)
+    asel(A("tri"), A("tri0"), [[1, 128]], Op.is_gt, 0, -1)
+    asel(A("ident"), A("onesb", 0, 128), [[1, 128]], Op.is_equal, 0, -1)
+    scan(A("dc"), A("k64"), A("onesb", 0, 32), Op.add, Op.mult, r4col)
+    aff(h0col, hcol, -1.0, 1.0)
+    aff(A("ee", 0, 128), A("rf"), h0col)
+    aff(A("ee", 128, 256), A("rf"), hcol)
+    ts(A("i16"), A("iom", 0, 16), rcol, Op.is_equal)
+    ts(A("i8"), A("iom", 0, 8), g8col, Op.is_equal)
+    ts(A("rx"), A("iom"), c8col, Op.is_equal)
+    ts(ccol, A("i16", 6, 7), A("i16", 7, 8), Op.subtract, ZC / 32.0, Op.mult)
+    aff(A("c1", 7, 128, 16), A("i16", 0, 8), None, ccol)
+    aff(A("c1", 15, 128, 16), A("i16", 0, 8), None, ccol)
+    copy(A("io8"), A("iom", 0, 8))
+    memset(A("obi", p0=96), 2)
+    for d in range(3):
+        ts(A("obi", p0=32 * d, p1=32 * d + 32), A("io8", p0=32 * d, p1=32 * d + 32), d, Op.logical_shift_right,
+           1, Op.bitwise_and)
+    fill(A("urow", p1=1), 16.0)
+    for q in range(7):
+        st, base = [4 * ST, 2 * ST, ST], 16
+        if q < 6:
+            d, b = q // 2, q % 2
+            base += st[2 - d] + (0 if b else BIG)
+            st[2 - d] = -st[2 - d] + (BIG if b else -BIG)
+        iota(A("urow", q, 128, 16, 0, 1), [[st[0], 2], [st[1], 2], [st[2], 2]], base, 0)
+    iota(A("ios"), [[1, 512]], 0, 0)
+    ts(b1col, rcol, 8.0, Op.is_lt, 98304.0, Op.mult)
+    aff(sbcol, b1col, 1.0 / 3)
+    aff(A("sel", 1, 192, 2), A("sel", 0, 192, 2), None, b1col)
+    ts(A("obt"), A("obi"), hcol, Op.is_equal)
+    ts(k6col, kcol, 6.0, Op.is_equal, 0.625, Op.mult)
+    aff(A("m8", 0, 8), A("obt"), 0.125, k6col)
+    aff(A("jb"), A("iom", 0, 8), 16.0, rcol)
+    aff(A("b2", 15, 128, 16), A("m8", 0, 8), A("i16", 0, 1))
+    for o in range(8):
+        aff(A("wo", 128 * o, 128 * o + 128), A("rf"), A("m8", o, o + 1))
+    aff(A("nw", 256, 258 + 2 * rank), A("jb", 0, 2 + 2 * rank), None, 512.0)
+    if rank < 3:
+        aff(A("nw", 258 + 2 * rank, 264), A("jb", 2 + 2 * rank, 8), None, 480.0)
+    ts(A("rt"), A("iom"), kcol, Op.is_equal, -1.0, Op.mult)
+    aff(A("c2", 7, 128, 8), A("bo", 0, 128, 8))
+    asel(A("pm", 0, 128), A("onesf"), [[-32, 4], [16, 2], [-1, 16]], Op.is_equal, -16, 1)
+    asel(A("pm", 128, 256), A("onesf"), [[-64, 2], [32, 2], [-1, 32]], Op.is_equal, -32, 1)
+    aff(A("c4", 7, 128, 16), A("i16", 0, 8), -1.0)
+    aff(A("c4", 15, 128, 16), A("i16", 0, 8), -1.0)
+    aff(A("cc"), A("iom", 0, 8), 128.0, rcol)
+    for o in range(8):
+        aff(A("pd", 38 * o + 32, 38 * o + 38), A("cc", 0, 6), None, 528.0 + 16 * o, "a")
+    copy(A("lj"), A("iom", 0, 8))
+    aff(A("m8", 8, 16), A("m8", 0, 8), 0.125)
+    aff(A("bc"), A("bo"), A("i16", 0, 1))
+    ts(zc0, kcol, 6.0, Op.is_lt, 1.0 / 64, Op.mult)
+    aff(zc, k6col, 0.625, zc0)
+    aff(A("m8", 24, 32), A("obt"), 1.0 / 16)
+    aff(A("m8", 16, 24), A("obt"), 7.0 / 64, zc)
+    tt(A("wc"), ind(A("m8", 8, 16), A("lj")), A("rf"), Op.mult)
+    tt(A("wz"), ind(A("m8", 16, 24), A("lj")), A("rf"), Op.mult)
+    tt(A("wm"), ind(A("m8", 24, 32), A("lj")), A("rf"), Op.mult)
+    aff(A("c3", 7, 128, 16), A("obt"), -1.0, 1.0)
+    aff(A("c3", 15, 128, 16), A("obt"), -1.0, 1.0)
+
+    for r in range(16):
+        mm(A("pa", 32, 64), A("b1", 15 - r, 143 - r, 1, 0, 8), A("x0", r, 512, 16, 0, 8), r == 0, r == 15)
+    number(0, A("offh"))
+    mm(A("pb", 100, 101), A("urow", p1=1), A("onesf", 0, 1, 1, 0, 1))
+    ts(nrc, A("pb", 100, 101), float(ROOT), Op.min, -1.0, Op.mult)
+    ts(tcol, A("pb", 100, 101), float(ROOT), Op.is_gt, 2.0 * BIG, Op.mult)
+    ts(bias2, tcol, A("pb", 100, 101), Op.subtract, float(BIG), Op.subtract)
+    aff(A("nr"), A("ios"), -1.0, nrc)
+
+    bdi = A("bdi", p1=16)
+    for h, (o0, s0, o1, s1) in enumerate(((Op.bitwise_and, 511, Op.logical_shift_right, 9),
+                                          (Op.logical_shift_right, 4, Op.bitwise_and, 15))):
+        ts(A("bdk", 16 * h, 16 * h + 8, p1=16), bdi, s0, o0)
+        ts(A("bdk", 16 * h + 8, 16 * h + 16, p1=16), bdi, s1, o1)
+        copy(A("bdf", 16 * h, 16 * h + 16, p1=16), A("bdk", 16 * h, 16 * h + 16, p1=16))
+    mm(A("pz", 0, 16), A("ee", 0, 128, 1, 0, 16), A("bdf", 0, 16, p1=16))
+    copy(A("bdu", 0, 16), A("pz", 0, 16))
+    aff(A("mka"), ind(A("i8"), A("bdu", 8, 16)))
+    tt(A("xa"), ind(A("xn"), A("bdu", 0, 8)), A("mka"), Op.mult)
+    mm(A("pz", 128, 256), A("rx"), A("xa"))
+    aff(A("gw", 512, 640), A("pz", 128, 256))
+    sa = fused(lambda q: A("gw", 512 + 32 * q, 544 + 32 * q),
+               lambda q: A("xw", 4096 + 32 * rank, 4128 + 32 * rank), "arra", 0, 2.6)
+    arrive([A("xw", 4096 + 32 * q, 4128 + 32 * q) for q in peers], "arra", 4, (sa,))
+    mm(A("pz", 16, 32), A("ee", 0, 128, 1, 0, 16), A("bdf", 16, 32, p1=16))
+    copy(A("bdu", 16, 32), A("pz", 16, 32))
+    banks = ["p0", "p1", "p2"]
+
+    copy(ind(A("w1"), A("off", 0, 32)), A("d1"))
+    spread(lambda gr: A("pc", 64 + 32 * gr, 96 + 32 * gr), A("offh"))
+    aff(A("nw", 0, 256), A("pc", 64, 320))
+    wrap8(A("pc", 0, 64), "c1", A("w1"), 512)
+    scan(A("sw", 0, 64), A("sel", 0, 64), A("pc", 0, 64), Op.add, Op.max)
+    ts(A("l1u"), A("sw", 1, 64, 2), sbcol, Op.subtract, float(ZC), Op.add)
+    ts(A("li"), A("sw", 1, 64, 2), sbcol, Op.subtract, float(ZC), Op.add)
+    for h in range(2):
+        aff(A("gw", 256 * h, 256 * h + 256), ind(A("xw"), A("l1u", 16 * h, 16 * h + 16)))
+    ts(A("lcr", 32, 64), A("li"), 15, Op.bitwise_and)
+    ts(A("lcr", 0, 32), A("li"), 4, Op.logical_shift_right)
+    copy(A("lcu"), A("lcr"))
+
+    aff(A("mk", 512, 640), ind(A("i16"), A("bdu", 24, 32)))
+    tt(A("tm", 512, 640), ind(A("nw"), A("bdu", 16, 24)), A("mk", 512, 640), Op.mult)
+    wrap8(A("pz", 256, 272), "c2", A("tm", 512, 640), 128)
+    scan(A("sb", 0, 16), A("sel", 0, 16), A("pz", 256, 272), Op.add, Op.max)
+    ts(A("nb1"), A("sb", 1, 16, 2), sbcol, Op.subtract, 512.0, Op.subtract)
+    tt(A("nb2"), A("nb1"), A("jb"), Op.min)
+    ts(A("lbu"), A("nb2"), 512.0, Op.add)
+    ts(A("bi"), A("nb1"), 0.0, Op.min, 512.0, Op.add)
+    ts(A("bcr", 8, 16), A("bi"), 15, Op.bitwise_and)
+    ts(A("bcr", 0, 8), A("bi"), 4, Op.logical_shift_right)
+    copy(A("bcu"), A("bcr"))
+    aff(A("mkb"), ind(A("i16"), A("bcu", 8, 16)))
+    aff(A("gb"), ind(A("gw"), A("lbu")))
+    sb = fused(lambda q: A("gb", 32 * q, 32 * q + 32),
+               lambda q: A("gg", 32 * slot(q, rank), 32 * slot(q, rank) + 32), "arrb", 1, 0.5)
+    arrive([A("gg")], "arrb", 4, (sb,))
+
+    for r in range(16):
+        mm(A("pa", 64, 96), A("b2", 15 - r, 143 - r), A("gw", r, 512, 16), r == 0, r == 15)
+    number(1, A("offf"))
+    for h in range(2):
+        c = (256 * h, 256 * h + 256)
+        aff(A("mk", *c), ind(A("i16"), A("lcu", 32 + 16 * h, 48 + 16 * h)))
+        tt(A("tm", *c), ind(A("nw"), A("lcu", 16 * h, 16 * h + 16)), A("mk", *c), Op.mult)
+        bank = A(("pz", "pc")[h], 0, 256)
+        mm(bank, A("rt"), A("tm", *c))
+        aff(A("d2", *c), bank, None, bias2)
+    tt(ind(A("w2"), A("off", 32, 64)), A("d2"), A("nr"), Op.max)
+    ts(A("n2w", 0, 32), A("offf"), 512.0, Op.min)
+    ts(A("n2h"), A("offf"), 512.0, Op.min)
+    spread(lambda gr: A("pd", 38 * gr, 38 * gr + 32), A("n2h"))
+    wrap8(A("pc", 320, 384), "c4", A("w2"), 512)
+    scan(A("sw", 64, 128), A("sel", 0, 64), A("pc", 320, 384), Op.add, Op.max)
+    ts(A("l2u"), A("sw", 65, 128, 2), sbcol, Op.subtract)
+    ts(A("li2"), A("sw", 65, 128, 2), sbcol, Op.subtract)
+
+    asel(A("t1", ROOT, ROOT + 512), A("gw", 0, 512), [[0, 512]], Op.is_ge, 0, 0)
+    for o in range(8):
+        mm(A(banks[o % 3]), A("wo", 128 * o, 128 * o + 128), A("gw", 0, 512))
+        aff(A("t1", 16 + ST * o, 528 + ST * o), A(banks[o % 3]))
+        store("s", T.y1[16 * o:16 * o + 16, :], A("t1", 16 + ST * o, 528 + ST * o, 1, 16 * o, 16 * o + 16), "oy1")
+    for o in range(8):
+        mm(A(("pz", "pb")[o // 4], 128 + 96 * (o % 4), 224 + 96 * (o % 4)), A("wo", 128 * o, 128 * o + 128), A("gg"))
+    for o in range(8):
+        aff(A("t1", 528 + ST * o, 624 + ST * o), A(("pz", "pb")[o // 4], 128 + 96 * (o % 4), 224 + 96 * (o % 4)))
+
+    tt(A("tmb"), ind(A("n2w"), A("bcu", 0, 8)), A("mkb"), Op.mult)
+    wrap8(A("pa", 144, 160), "c2", A("tmb"), 128)
+    scan(A("sb", 16, 32), A("sel", 0, 16), A("pa", 144, 160), Op.add, Op.max)
+    ts(A("nbb"), A("sb", 17, 32, 2), sbcol, Op.subtract)
+    spread(lambda gr: A("pa", 192 + gr, 256, 8), A("nbb", 0, 8))
+    copy(A("l8u"), A("pa", 192, 256))
+
+    for h in range(2):
+        c = (256 * h, 256 * h + 256)
+        aff(A("v", *c), ind(A("t1"), A("l2u", 16 * h, 16 * h + 16)))
+        mm(A(banks[h], 0, 256), A("wc"), A("v", *c))
+        aff(A("win", *c), A(banks[h], 0, 256))
+
+    order = sorted(peers, key=lambda q: topo.die(cores[q]) == topo.die(core))
+    sent = []
+    for i, q in enumerate(order):
+        o = A("cb", 256 * q, 256 * q + 256)
+        for h in range(2):
+            aff(A("cb", 256 * q + 128 * h, 256 * q + 128 * h + 128),
+                ind(A("win", 0, 528), A("l8u", 16 * q + 8 * h, 16 * q + 8 * h + 8)))
+        rid, pid = topo.addr(cores[q])[:2]
+        s = slot(q, rank)
+        m = topo.mask(core, cores[q])
+        sent.append(add("g", lambda x, o=o, s=s, rid=rid, pid=pid, m=m: x.remote_dma(
+            ap(A("win", 528 + 256 * s, 784 + 256 * s)), ap(o), T.sem.arrc, T.sem.sent, pid, rid, m),
+            [], [o], 0.4, "sent", len(topo.engines(core, cores[q])), lat=2.3, after=tuple(sent)))
+    arrive([A("win", 528, 1296)], "arrc", 1, tuple(sent))
+
+    aff(A("nw2", 1, 305), A("pd", 0, 304))
+    ts(A("lcr2", 32, 64), A("li2"), 15, Op.bitwise_and)
+    ts(A("lcr2", 0, 32), A("li2"), 4, Op.logical_shift_right)
+    copy(A("lcu2"), A("lcr2"))
+    for h in range(2):
+        c = (256 * h, 256 * h + 256)
+        aff(A("mk2", *c), ind(A("i16"), A("lcu2", 32 + 16 * h, 48 + 16 * h)))
+        tt(A("tm2", *c), ind(A("nw2"), A("lcu2", 16 * h, 16 * h + 16)), A("mk2", *c), Op.mult)
+    for d in range(3):
+        wrap8(A("pc", 64 * d, 64 * d + 64), "c3", A("tm2"), 512, 32 * d, 32 * d + 32)
+    scan(A("sw", 128, 320), A("sel"), A("pc", 0, 192), Op.add, Op.max)
+    ts(A("lfu"), A("sw", 129, 320, 2), sbcol, Op.subtract)
+    add("a", lambda q: q.activation(ap(A("sg")), ap(A("v")), Fn.Sign, bias=100.0625, scale=-1.0),
+        [A("sg")], [A("v")], 0.55)
+    mm(A("p2"), A("bc"), A("sg"))
+    tt(A("vs"), A("p2"), A("v"), Op.mult)
+    zb = ["pz", "pd"]
+    for h in range(2):
+        c = (256 * h, 256 * h + 256)
+        mm(A(zb[h], 0, 256), A("wz"), A("v", *c), True, False)
+        mm(A(zb[h], 0, 256), A("wm"), A("vs", *c), False, False)
+
+    for h in range(2):
+        for d in range(3):
+            c = 512 * d + 256 * h
+            aff(A("gd", c, c + 256), ind(A("win"), A("lfu", c // 16, c // 16 + 16)))
+            if d < 2:
+                mm(A(zb[h], 0, 256), A("pm", 128 * d, 128 * d + 128), A("gd", c, c + 256), False, d == 1)
+        for p in (0, 64):
+            tt(A("yo", 256 * h, 256 * h + 256, 1, p, p + 64), A(zb[h], 0, 256, 1, p, p + 64),
+               A("gd", c, c + 256, 1, 64 - p, 128 - p), Op.add)
+        store("sa"[h], T.y2[:, 256 * h:256 * h + 256], A("yo", 256 * h, 256 * h + 256), "oy2")
+
+    total = emit(g, T, arrange(ops))
+    g.sync.wait_ge(T.sem.oy1, total["oy1"])
+    g.sync.wait_ge(T.sem.oy2, total["oy2"])
+    g.wait_ge(T.sem.sent, total["sent"])

@@ -32,14 +32,14 @@ SCRATCH = {k: ("sbuf", [128, v[0]], v[1]) for k, v in SB.items()}
 PSUM = ["pa", "pb", "pc", "pd", "p0", "p1", "p2", "pz"]
 for _p in PSUM:
     SCRATCH[_p] = ("psum", [128, 512], F32)
-SEMAPHORES = ["cv", "ca", "ct", "cg", "lx0", "lbd", "lnb", "lxn", "lx", "oy1", "oy2", "arra", "arrb", "arrc", "sent"]
+SEMAPHORES = ["cv", "ca", "ct", "cg", "lx0", "lbd", "lnb", "lxn", "lx", "oy1", "oy2", "arr0", "arra", "arrb", "arrc",
+              "sent"]
 ENG_SEM = {"v": "cv", "a": "ca", "t": "ct", "g": "cg"}
-POOL = ("pool", 0, 1, 1, 0, 128, 1)
 GAP = 0.11
 VEC = 0.00104
 PE = 0.00052
-TRIES = 3000
-SLACK = 0.1
+TRIES = 7000
+SLACK = 0.3
 PLANS = {}
 
 
@@ -126,15 +126,34 @@ def arrange(ops):
             start, end, pick = sweep(key, pred, succ, False)
             score = max(end) + 0.001 * sum(end) / n
             if best is None or score <= best[0] + SLACK * rand() * (1 - trial / TRIES):
-                best = (score, start)
+                best = (score, start, end, pick)
                 if name not in PLANS or score < PLANS[name][0]:
                     PLANS[name] = (score, start, pick)
             if trial % 8 == 0:
                 key = [x + o["pri"] for x, o in zip(sweep(end, succ, pred, True)[1], ops)]
-            else:
-                key = [o["pri"] - x for x, o in zip(best[1], ops)]
-                for _ in range(1 + trial % 12):
-                    key[int(rand() * n)] += 3.0 * (rand() - 0.4)
+                continue
+            key = [o["pri"] - x for x, o in zip(best[1], ops)]
+            bs, be, bp = best[1:]
+            chain = []
+            i = max(range(n), key=lambda x: be[x])
+            while bs[i] > 0.3:
+                j = max(pred[i], key=lambda x: be[x]) if pred[i] else None
+                if j is None or be[j] + GAP + 0.02 < bs[i]:
+                    j = max((x for x in range(n) if bp[x] == bp[i] and bs[x] < bs[i]), key=lambda x: bs[x])
+                    chain.append((i, j))
+                i = j
+            for _ in range(1 + trial % 2):
+                i, j = chain[int(rand() * len(chain))]
+                if rand() < 0.4:
+                    key[j] -= 2.0 * rand()
+                    continue
+                up, todo, seen = 4.0 * rand(), [j if rand() < 0.6 else i], set()
+                while todo:
+                    x = todo.pop()
+                    if x not in seen:
+                        seen.add(x)
+                        key[x] += up
+                        todo += pred[x]
     score, start, pick = PLANS[name]
     for o, e in zip(ops, pick):
         o["e"], o["f"] = [x[:2] for x in o["alt"] if x[0] == e][0]
@@ -315,23 +334,23 @@ def rank_program(g, core, T, topo):
     def slot(at, q):
         return q if q < at else q - 1
 
-    def fused(src_of, dst_of, sem, turn, c):
+    def fused(src_of, dst_of, sem, c, pri=0.0):
         tr = []
         n = 0
         for q in peers:
             en = topo.engines(core, cores[q])
             w = len(en) // 4
-            j = slot(rank, q) + turn
+            j = slot(rank, q)
             rid, pid = topo.addr(cores[q])[:2]
             tr.append(RemoteDMATransfer(dst_ids=[DstId(rid=rid, pnc=pid)],
-                                        dma_engine_mask=sum(1 << e for e in en[j * w:(j + 1) * w]),
+                                        dma_engine_mask=sum(1 << e for e in en[(j + 1) * w if j else 0:(j + 2) * w]),
                                         remote_sem=T.sem[sem], src=ap(src_of(q)), dst=ap(dst_of(q))))
-            n += w
+            n += w if j else 2 * w
         return add("g", lambda x: x.remote_dma_fused(tr, local_sem=T.sem.sent), [], [src_of(q) for q in peers], c,
-                   "sent", n, lat=2.3)
+                   "sent", n, lat=2.3, pri=pri)
 
     def arrive(regions, sem, div, after):
-        n = sum(len(topo.engines(cores[q], core)) // div for q in peers)
+        n = sum(len(topo.engines(cores[q], core)) // (div if slot(q, rank) else (div + 1) // 2) for q in peers)
         add("-", None, regions, [], 0.0, sem, n, after=after)
 
     def wrap8(o, c, src, n, p0=0, p1=128):
@@ -395,7 +414,7 @@ def rank_program(g, core, T, topo):
     fill(A("n2w", 32, 40), 512.0)
     fill(A("t1", 0, 16), 0.0)
     fill(A("nw2", 0, 8), 512.0)
-    fill(A("nw2", 304, 344), 512.0)
+    fill(A("nw2", 304, 312), 512.0)
     fill(A("win", 512, 528), 0.0)
     ts(A("pk", 0, 1), A("pi", 0, 1), 15, Op.bitwise_and)
     ts(A("pk", 1, 2), A("pi", 0, 1), 4, Op.logical_shift_right)
@@ -406,12 +425,12 @@ def rank_program(g, core, T, topo):
     copy(pcol, A("pi", 0, 1))
     ts(A("b1", 15, 128, 16), A("iom", 0, 8), pcol, Op.is_equal)
     ts(A("bo"), A("iog"), kcol, Op.is_equal)
-    asel(A("prev"), A("onesb", 0, 128), [[16, 8], [0, 16]], Op.is_gt, 0, -1)
-    ts(A("tri0"), A("iog"), kcol, Op.is_equal, -1.0, Op.mult)
+    ts(A("prev"), A("iog"), kcol, Op.is_gt)
+    ts(A("tri0"), A("iom"), rcol, Op.is_gt, -1.0, Op.mult)
     ts(A("rf"), A("iom"), rcol, Op.is_equal)
     aff(r4col, rcol, 4.0, DUM - 64.0)
-    asel(A("tri"), A("tri0"), [[1, 128]], Op.is_gt, 0, -1)
-    asel(A("ident"), A("onesb", 0, 128), [[1, 128]], Op.is_equal, 0, -1)
+    tt(A("tri"), A("tri0"), A("bo"), Op.mult)
+    tt(A("ident"), A("rf"), A("bo"), Op.mult)
     scan(A("dc"), A("k64"), A("onesb", 0, 32), Op.add, Op.mult, r4col)
     aff(h0col, hcol, -1.0, 1.0)
     aff(A("ee", 0, 128), A("rf"), h0col)
@@ -436,6 +455,10 @@ def rank_program(g, core, T, topo):
             st[2 - d] = -st[2 - d] + (BIG if b else -BIG)
         iota(A("urow", q, 128, 16, 0, 1), [[st[0], 2], [st[1], 2], [st[2], 2]], base, 0)
     iota(A("ios"), [[1, 512]], 0, 0)
+    mine = A("nw2", 312 + 8 * rank, 320 + 8 * rank)
+    iota(mine, [[0, 8]], 512, 0, 30.0)
+    s0 = fused(lambda q: mine, lambda q: mine, "arr0", 2.5, 30.0)
+    arrive([A("nw2", 312 + 8 * q, 320 + 8 * q) for q in peers], "arr0", 4, (s0,))
     ts(b1col, rcol, 8.0, Op.is_lt, 98304.0, Op.mult)
     aff(sbcol, b1col, 1.0 / 3)
     aff(A("sel", 1, 192, 2), A("sel", 0, 192, 2), None, b1col)
@@ -446,9 +469,9 @@ def rank_program(g, core, T, topo):
     aff(A("b2", 15, 128, 16), A("m8", 0, 8), A("i16", 0, 1))
     for o in range(8):
         aff(A("wo", 128 * o, 128 * o + 128), A("rf"), A("m8", o, o + 1))
-    aff(A("nw", 256, 258 + 2 * rank), A("jb", 0, 2 + 2 * rank), None, 512.0)
-    if rank < 3:
-        aff(A("nw", 258 + 2 * rank, 264), A("jb", 2 + 2 * rank, 8), None, 480.0)
+    cut = min(2 + 2 * rank, 6)
+    aff(A("nw", 256, 256 + cut), A("jb", 0, cut), None, 512.0)
+    aff(A("nw", 256 + cut, 264), A("jb", cut, 8), None, 480.0)
     ts(A("rt"), A("iom"), kcol, Op.is_equal, -1.0, Op.mult)
     aff(A("c2", 7, 128, 8), A("bo", 0, 128, 8))
     asel(A("pm", 0, 128), A("onesf"), [[-32, 4], [16, 2], [-1, 16]], Op.is_equal, -16, 1)
@@ -493,7 +516,7 @@ def rank_program(g, core, T, topo):
     mm(A("pz", 128, 256), A("rx"), A("xa"))
     aff(A("gw", 512, 640), A("pz", 128, 256))
     sa = fused(lambda q: A("gw", 512 + 32 * q, 544 + 32 * q),
-               lambda q: A("xw", 4096 + 32 * rank, 4128 + 32 * rank), "arra", 0, 2.6)
+               lambda q: A("xw", 4096 + 32 * rank, 4128 + 32 * rank), "arra", 0.5, 3.0)
     arrive([A("xw", 4096 + 32 * q, 4128 + 32 * q) for q in peers], "arra", 4, (sa,))
     mm(A("pz", 16, 32), A("ee", 0, 128, 1, 0, 16), A("bdf", 16, 32, p1=16))
     copy(A("bdu", 16, 32), A("pz", 16, 32))
@@ -526,7 +549,7 @@ def rank_program(g, core, T, topo):
     aff(A("mkb"), ind(A("i16"), A("bcu", 8, 16)))
     aff(A("gb"), ind(A("gw"), A("lbu")))
     sb = fused(lambda q: A("gb", 32 * q, 32 * q + 32),
-               lambda q: A("gg", 32 * slot(q, rank), 32 * slot(q, rank) + 32), "arrb", 1, 0.5)
+               lambda q: A("gg", 32 * slot(q, rank), 32 * slot(q, rank) + 32), "arrb", 0.5)
     arrive([A("gg")], "arrb", 4, (sb,))
 
     for r in range(16):
@@ -583,7 +606,7 @@ def rank_program(g, core, T, topo):
         m = topo.mask(core, cores[q])
         sent.append(add("g", lambda x, o=o, s=s, rid=rid, pid=pid, m=m: x.remote_dma(
             ap(A("win", 528 + 256 * s, 784 + 256 * s)), ap(o), T.sem.arrc, T.sem.sent, pid, rid, m),
-            [], [o], 0.4, "sent", len(topo.engines(core, cores[q])), lat=2.3, after=tuple(sent)))
+            [], [o], 0.4, "sent", len(topo.engines(core, cores[q])), lat=2.3))
     arrive([A("win", 528, 1296)], "arrc", 1, tuple(sent))
 
     aff(A("nw2", 1, 305), A("pd", 0, 304))
@@ -617,7 +640,8 @@ def rank_program(g, core, T, topo):
         for p in (0, 64):
             tt(A("yo", 256 * h, 256 * h + 256, 1, p, p + 64), A(zb[h], 0, 256, 1, p, p + 64),
                A("gd", c, c + 256, 1, 64 - p, 128 - p), Op.add)
-        store("sa"[h], T.y2[:, 256 * h:256 * h + 256], A("yo", 256 * h, 256 * h + 256), "oy2")
+            store("sa"[p // 64], T.y2[p:p + 64, 256 * h:256 * h + 256],
+                  A("yo", 256 * h, 256 * h + 256, 1, p, p + 64), "oy2")
 
     total = emit(g, T, arrange(ops))
     g.sync.wait_ge(T.sem.oy1, total["oy1"])

@@ -5,41 +5,47 @@ F32, BF, F16, I32, U16 = "float32", "bfloat16", "float16", "int32", "uint16"
 ZC = 4224
 ST = 608
 ROOT = 16 + 8 * ST
-DUM = 5632
+TB = 1280
+DUM = 8256
 BIG = 16384
 
 SB = {
-    "xw": (4240, BF), "xn": (512, BF), "x0": (512, BF), "d1": (512, I32), "bdi": (8, I32), "bdk": (32, I32),
-    "bdf": (32, F16), "bdu": (32, U16), "mka": (128, BF), "xa": (128, BF), "rx": (128, BF),
-    "i8": (8, F32), "w1": (8192, F32), "w2": (8192, F32), "gw": (640, BF), "gb": (128, BF), "gg": (96, BF),
-    "onesb": (512, BF), "onesf": (128, F32), "b1": (144, BF), "b2": (144, BF), "pi": (4, I32), "pk": (8, I32),
-    "col": (24, F32), "iog": (128, BF), "iom": (128, BF), "bo": (128, BF), "prev": (128, BF), "rf": (128, BF),
-    "ident": (128, BF), "tri0": (128, BF), "tri": (128, BF), "k64": (32, BF), "dc": (32, F16), "i16": (16, F32),
-    "pa0": (128, BF), "pa1": (128, BF), "n2h": (32, F16), "offh": (32, F16), "io8": (8, I32),
-    "ee": (256, BF), "c1": (136, F32), "c4": (136, F32), "c2": (136, BF), "c3": (136, BF), "sel": (192, F32),
-    "obi": (8, I32), "obt": (8, F32), "m8": (32, F32), "lj": (8, U16), "wc": (128, F32), "wz": (128, F32),
-    "wm": (128, F32), "wo": (1024, BF), "bc": (128, BF), "rt": (128, BF), "pm": (256, F32), "urow": (128, F32),
-    "ios": (512, F32), "nr": (512, F32), "jb": (8, F32), "cc": (8, F32), "nw": (272, F32), "nw2": (344, F32),
-    "n2w": (40, F32), "nf": (64, BF), "sc": (80, BF), "nd": (64, F16), "off": (64, U16), "offf": (32, F32),
-    "sw": (320, F32), "sb": (32, F32), "l1u": (32, U16), "l2u": (32, U16), "li": (32, I32), "lcr": (64, I32),
-    "lcu": (64, U16), "li2": (32, I32), "lcr2": (64, I32), "lcu2": (64, U16), "bi": (8, I32), "bcr": (16, I32),
-    "bcu": (16, U16), "mk": (640, BF), "tm": (640, F16), "mk2": (512, BF), "tm2": (512, F16), "mkb": (128, BF),
-    "tmb": (128, F16), "nb1": (8, F32), "nb2": (8, F32), "lbu": (8, U16), "nbb": (8, F16), "l8u": (64, U16),
-    "lfu": (96, U16), "d2": (512, F32), "t1": (ROOT + 512, F32), "v": (512, F32), "sg": (512, BF),
-    "vs": (512, F32), "win": (1296, F32), "cb": (1024, F32), "gd": (1536, F32), "yo": (512, F32),
+    "xw": (4240, BF), "xn": (544, BF), "x0": (32, BF), "xt": (32, BF), "d1": (544, I32), "idb": (32, I32),
+    "bdi": (8, I32), "bdg": (8, F32), "lx": (8, U16), "xa": (128, BF), "xb": (128, BF),
+    "eef": (128, F32), "e0": (8, BF), "th8": (8, F32), "nfb": (8, BF), "jn": (8, F32),
+    "w1": (13888, F32), "w2": (13760, F32), "gw": (640, BF), "gg": (96, BF),
+    "onesb": (144, BF), "onesf": (128, F32), "b2": (144, BF), "pi": (4, I32), "pk": (8, I32),
+    "col": (32, F32), "iog": (128, BF), "iom": (128, BF), "iob": (128, BF), "bo": (128, BF), "prev": (128, BF),
+    "prev1": (128, BF), "rf": (128, BF), "rfb": (128, BF),
+    "ident": (128, BF), "tri": (128, BF), "dc": (32, F32), "i16": (16, F32),
+    "yt": (512, F32), "n2h": (40, F16), "offh": (32, F16), "io8": (12, I32), "io2": (16, I32),
+    "ee": (256, BF), "c1": (136, F32), "c4": (136, F32), "c2": (136, BF), "c5": (136, BF), "sel": (80, F32),
+    "obi": (12, I32), "obt": (12, F32), "m8": (40, F32), "lj": (16, U16), "wc": (128, F32), "wz": (128, F32),
+    "l2r": (32, F32), "l2t": (32, F32), "io128": (128, BF),
+    "r3": (128, F32), "wo": (1024, BF), "rt": (128, BF), "pm": (256, F32), "urow": (128, F32),
+    "ios": (512, F32), "nr": (512, F32), "jb": (8, F32), "cc": (6, F32), "nw": (272, F32), "nw2": (344, F32),
+    "nf": (64, BF), "sc": (80, BF), "nd": (64, F16), "off": (64, U16), "b8": (32, F32), "b64": (64, F32),
+    "nfg": (6, F32), "lq": (12, U16), "tb": (16, F32), "pv": (192, F32),
+    "lvb": (64, U16), "sw": (192, F32), "sb": (32, F32), "l1u": (40, U16), "l2u": (32, U16), "li": (40, I32),
+    "lcr": (80, I32), "lcu": (80, U16), "li2": (32, I32), "lcr2": (64, I32), "lcu2": (64, U16),
+    "mk": (640, BF), "tm": (640, F16), "mk2": (512, BF), "tm2": (512, F16),
+    "l2s": (32, F32), "lf": (96, F32), "lfu": (96, U16), "d2": (512, F32),
+    "t1": (TB + ROOT + 2048, F32), "v": (512, F32), "vb": (768, F32), "vg": (768, F32), "vc": (768, F32), "gd": (1536, F32),
+    "yo": (512, F32),
 }
 SCRATCH = {k: ("sbuf", [128, v[0]], v[1]) for k, v in SB.items()}
 PSUM = ["pa", "pb", "pc", "pd", "p0", "p1", "p2", "pz"]
 for _p in PSUM:
     SCRATCH[_p] = ("psum", [128, 512], F32)
-SEMAPHORES = ["cv", "ca", "ct", "cg", "lx0", "lbd", "lnb", "lxn", "lx", "oy1", "oy2", "arr0", "arra", "arrb", "arrc",
-              "sent"]
+SEMAPHORES = ["cv", "ca", "ct", "cg", "lx0", "lbd", "lnb", "lxn", "lx", "lrt", "lt1", "oy1", "oy2", "arra", "arrb", "arrc0",
+              "arrc1", "arrc2", "sent"]
 ENG_SEM = {"v": "cv", "a": "ca", "t": "ct", "g": "cg"}
 GAP = 0.11
 VEC = 0.00104
 PE = 0.00052
-TRIES = 7000
-SLACK = 0.3
+TRIES = 24000
+SLACK = 0.6
+SEED = 1
 PLANS = {}
 
 
@@ -70,94 +76,137 @@ def unfenced(o, p):
 
 
 def arrange(ops):
+    calls, ops, home = ops, [], []
+    for o in calls:
+        if o["glue"]:
+            p = ops[-1]
+            c = p["c"] + o["c"] + (GAP if o["e"] == "t" and o["tile"] != p["last"] else 0.0)
+            p.update(w=p["w"] + o["w"], r=p["r"] + o["r"], names=p["names"] | o["names"], c=c, last=o["tile"],
+                     banks=p["banks"] | o["banks"], alt=[(o["e"], None, c)],
+                     tile=p["tile"] if p["tile"] == o["tile"] else len(ops))
+        else:
+            ops.append(dict(o, last=o["tile"], after=[home[j] for j in o["after"]]))
+        home.append(len(ops) - 1)
     n = len(ops)
-    pred = [[j for j in range(i) if conflict(ops[i], ops[j]) or j in ops[i]["after"]] for i in range(n)]
-    level = [o["c"] + o["lat"] + o["pri"] for o in ops]
-    for i in range(n - 1, -1, -1):
-        for j in pred[i]:
-            level[j] = max(level[j], ops[j]["c"] + ops[j]["lat"] + ops[j]["pri"] + level[i] + GAP)
-    succ = [[] for _ in range(n)]
-    for i in range(n):
-        for j in pred[i]:
-            succ[j].append(i)
+    if n not in PLANS:
+        pred = [[j for j in range(i) if conflict(ops[i], ops[j]) or j in ops[i]["after"]] for i in range(n)]
+        above, before, behind = [0] * n, [], [[] for _ in range(n)]
+        for i in range(n):
+            keep = []
+            for j in reversed(pred[i]):
+                if not above[i] >> j & 1:
+                    keep.append((j, 0.0 if unfenced(ops[i], ops[j]) else GAP))
+                    behind[j].append((i, keep[-1][1]))
+                above[i] |= above[j] | 1 << j
+            before.append(keep)
+        up = [[j for j in range(i) if above[i] >> j & 1] + [i] for i in range(n)]
+        down = [[i] + [j for j in range(i + 1, n) if above[j] >> i & 1] for i in range(n)]
+        alt = [[(e, c) for e, f, c in o["alt"]] for o in ops]
+        lat = [o["lat"] for o in ops]
 
-    def sweep(key, before, behind, back):
-        busy = {}
-        start, end, pick = [0.0] * n, [0.0] * n, [None] * n
-        left = [len(p) for p in before]
-        ready = [i for i in range(n) if not left[i]]
-        while ready:
-            i = max(ready, key=lambda x: key[x])
-            ready.remove(i)
-            o = ops[i]
-            t0 = max([end[j] + (0.0 if unfenced(o, ops[j]) else GAP) for j in before[i]] + [0.0])
-            t0 += o["lat"] if back else 0.0
-            top = None
-            for e, f, c in o["alt"]:
-                t = t0
-                for a, b in busy.setdefault(e, []):
-                    if t + c <= a:
-                        break
-                    if b > t:
-                        t = b
-                if top is None or t + c < top[0]:
-                    top = (t + c, t, e)
-            start[i], end[i], pick[i] = top[1], top[0] + (0.0 if back else o["lat"]), top[2]
-            if top[2] != "-":
-                busy[top[2]].append((top[1], top[0]))
-                busy[top[2]].sort()
-            for k in behind[i]:
-                left[k] -= 1
-                if not left[k]:
-                    ready.append(k)
-        return start, end, pick
+        def sweep(key, first, then, back, bias):
+            lo, hi = {e: [] for e in "vatgs-"}, {e: [] for e in "vatgs-"}
+            start, end, pick = [0.0] * n, [0.0] * n, [None] * n
+            left = [len(p) for p in first]
+            ready = sorted((key[i], i) for i in range(n) if not left[i])
+            while ready:
+                i = ready.pop()[1]
+                t0 = 0.0
+                for j, gap in first[i]:
+                    if end[j] + gap > t0:
+                        t0 = end[j] + gap
+                if back:
+                    t0 += lat[i]
+                top = None
+                for e, c in alt[i]:
+                    t, a, b = t0, lo[e], hi[e]
+                    k = m = len(a)
+                    while k and b[k - 1] > t:
+                        k -= 1
+                    while k < m and t + c > a[k] + 1e-9:
+                        t = b[k]
+                        k += 1
+                    v = t + c + (bias[i] if e == "v" else 0.0)
+                    if top is None or v < top[0]:
+                        top = (v, t, t + c, e, k)
+                v, start[i], t, e, k = top
+                end[i], pick[i] = t + (0.0 if back else lat[i]), e
+                if e != "-":
+                    lo[e].insert(k, start[i])
+                    hi[e].insert(k, t)
+                more = False
+                for k, gap in then[i]:
+                    left[k] -= 1
+                    if not left[k]:
+                        ready.append((key[k], k))
+                        more = True
+                if more:
+                    ready.sort()
+            return start, end, pick
 
-    seed = [12345]
+        def plan(key, bias, again):
+            start, end, pick = sweep(key, before, behind, False, bias)
+            one = (max(end) + 0.02 * sum(end) / n, start, end, pick, bias)
+            if again:
+                two = plan(sweep(end, behind, before, True, bias)[1], bias, False)
+                one = two if two[0] < one[0] else one
+            return one
 
-    def rand():
-        seed[0] = (seed[0] * 1103515245 + 12345) % 2147483648
-        return seed[0] / 2147483648
+        seed = [SEED]
 
-    name = str(pred)
-    if name not in PLANS:
-        best = None
-        key = level
+        def rand(m=1.0):
+            seed[0] = (seed[0] * 1103515245 + 12345) % 2147483648
+            return m * seed[0] / 2147483648
+
+        level = [0.0] * n
+        for i in range(n - 1, -1, -1):
+            level[i] = min(c for e, c in alt[i]) + lat[i] + max([level[k] + gap for k, gap in behind[i]] + [0.0])
+        now = best = plan(level, [0.0] * n, True)
         for trial in range(TRIES):
-            start, end, pick = sweep(key, pred, succ, False)
-            score = max(end) + 0.001 * sum(end) / n
-            if best is None or score <= best[0] + SLACK * rand() * (1 - trial / TRIES):
-                best = (score, start, end, pick)
-                if name not in PLANS or score < PLANS[name][0]:
-                    PLANS[name] = (score, start, pick)
-            if trial % 8 == 0:
-                key = [x + o["pri"] for x, o in zip(sweep(end, succ, pred, True)[1], ops)]
-                continue
-            key = [o["pri"] - x for x, o in zip(best[1], ops)]
-            bs, be, bp = best[1:]
+            start, end, pick, bias = now[1:]
+            key = [-x for x in start]
+            prior, last = {}, {}
+            for i in sorted(range(n), key=lambda x: start[x]):
+                prior[i], last[pick[i]] = last.get(pick[i]), i
             chain = []
-            i = max(range(n), key=lambda x: be[x])
-            while bs[i] > 0.3:
-                j = max(pred[i], key=lambda x: be[x]) if pred[i] else None
-                if j is None or be[j] + GAP + 0.02 < bs[i]:
-                    j = max((x for x in range(n) if bp[x] == bp[i] and bs[x] < bs[i]), key=lambda x: bs[x])
-                    chain.append((i, j))
+            i = max(range(n), key=lambda x: end[x])
+            while i is not None and start[i] > 0.2:
+                t, j = max([(end[j] + gap, j) for j, gap in before[i]] + [(0.0, None)])
+                if t + 0.005 < start[i]:
+                    j = prior[i]
+                    if j is not None:
+                        chain.append((i, j))
                 i = j
-            for _ in range(1 + trial % 2):
-                i, j = chain[int(rand() * len(chain))]
-                if rand() < 0.4:
-                    key[j] -= 2.0 * rand()
+            for _ in range(1 + int(rand(2))):
+                u = rand()
+                if u < 0.25 or not chain:
+                    i, x = int(rand(n)), rand(4.0) - 2.0
+                    for j in up[i] if x > 0 else down[i]:
+                        key[j] += x
                     continue
-                up, todo, seen = 4.0 * rand(), [j if rand() < 0.6 else i], set()
-                while todo:
-                    x = todo.pop()
-                    if x not in seen:
-                        seen.add(x)
-                        key[x] += up
-                        todo += pred[x]
-    score, start, pick = PLANS[name]
-    for o, e in zip(ops, pick):
-        o["e"], o["f"] = [x[:2] for x in o["alt"] if x[0] == e][0]
-    return [ops[i] for i in sorted(range(n), key=lambda x: (start[x], x))]
+                i, j = chain[int(rand(len(chain)))]
+                x = rand(2.0)
+                if u < 0.45:
+                    bias = list(bias)
+                    bias[i if x < 1.0 else j] = (-1.5, -0.3, 0.0, 0.3, 1.5)[int(rand(5))]
+                elif u < 0.65:
+                    for k in down[j]:
+                        key[k] -= x
+                elif u < 0.8:
+                    key[j] -= x
+                else:
+                    for k in up[i if rand() < 0.5 else j]:
+                        key[k] += 1.5 * x
+            new = plan(key, bias, trial % 4 == 0)
+            if new[0] <= now[0] + SLACK * rand() ** 2 * (1 - trial / TRIES):
+                now = new
+            if new[0] < best[0]:
+                best = new
+        PLANS[n] = (max(best[2]), best[1], best[3], ops)
+    score, start, pick = PLANS[n][:3]
+    for o, i in zip(calls, home):
+        o["e"], o["f"] = [x[:2] for x in o["alt"] if x[0] == pick[i]][0]
+    return [calls[i] for i in sorted(range(len(calls)), key=lambda x: (start[home[x]], x))]
 
 
 def emit(g, T, ops):
@@ -245,8 +294,12 @@ def rank_program(g, core, T, topo):
         names = set(x[0] for x in ww + rr)
         ops.append({"e": e, "f": f, "w": ww, "r": rr, "sem": sem, "inc": inc, "dma": dma, "c": c, "lat": lat,
                     "pri": pri, "after": after, "names": names, "banks": names & set(PSUM), "tile": tile,
-                    "alt": alt or [(e, f, c)]})
+                    "alt": alt or [(e, f, c)], "glue": False})
         return len(ops) - 1
+
+    def glue(n):
+        for o in ops[len(ops) - n + 1:]:
+            o["glue"] = True
 
     def narrow(r):
         return r[0] in SB and SB[r[0]][1] in (BF, F16, U16)
@@ -267,8 +320,8 @@ def rank_program(g, core, T, topo):
     def ind(win, off):
         return ("ind", win, off)
 
-    def memset(o, c):
-        add("v", lambda q: q.memset(ap(o), c), [o], [], half(o, o))
+    def memset(o, c, pri=0.0):
+        add("v", lambda q: q.memset(ap(o), c), [o], [], half(o, o), pri=pri)
 
     def copy(o, i):
         add("v", lambda q: q.tensor_copy(ap(o), ap(i)), [o], [i], half(o, i))
@@ -325,8 +378,8 @@ def rank_program(g, core, T, topo):
         add("g", lambda q: q.affine_select(ap(o), ap(i), pat, cmp, 0.0, base, cm), [o], [i],
             0.21 + width(o) * 2 * VEC)
 
-    def load(e, o, src, sem, lat, pri, after=()):
-        return add(e, lambda q: q.dma_start(ap(o), src), [o], [], 0.06, sem, 16, True, lat, pri, after)
+    def load(e, o, src, sem, lat, pri, after=(), r=()):
+        return add(e, lambda q: q.dma_start(ap(o), src), [o], list(r), 0.06, sem, 16, True, lat, pri, after)
 
     def store(e, dst, i, sem):
         add(e, lambda q: q.dma_start(dst, ap(i)), [], [i], 0.06, sem, 16, True, 2.2)
@@ -349,301 +402,365 @@ def rank_program(g, core, T, topo):
         return add("g", lambda x: x.remote_dma_fused(tr, local_sem=T.sem.sent), [], [src_of(q) for q in peers], c,
                    "sent", n, lat=2.3, pri=pri)
 
-    def arrive(regions, sem, div, after):
-        n = sum(len(topo.engines(cores[q], core)) // (div if slot(q, rank) else (div + 1) // 2) for q in peers)
+    def arrive(regions, sem, after):
+        n = sum(len(topo.engines(cores[q], core)) // (4 if slot(q, rank) else 2) for q in peers)
         add("-", None, regions, [], 0.0, sem, n, after=after)
 
-    def wrap8(o, c, src, n, p0=0, p1=128):
+    def wrap8(o, c, src, n):
         for b in range(8):
-            mm(o, A(c, 7 - b, 135 - b, 1, p0, p1), A(src[0], src[1] + b, src[1] + n, 8, p0, p1), b == 0, b == 7)
+            mm(o, A(c, 7 - b, 135 - b), A(src[0], src[1] + b, src[1] + n, 8), b == 0, b == 7)
+        glue(8)
 
     def spread(o_of, src):
         for gr in range(8):
             a, h = gr // 2, gr % 2
             mm(o_of(gr), A("ee", 128 * h, 128 * h + 128, 1, 32 * a, 32 * a + 32),
                A(src[0], src[1], src[2], 1, 32 * a, 32 * a + 32))
+            glue(1 + h)
 
-    (rcol, kcol, hcol, c8col, g8col, pcol, r4col, h0col, ccol, b1col, sbcol, k6col, zc0, zc, nrc, tcol,
-     bias2) = [A("col", i, i + 1) for i in range(17)]
+    (rcol, kcol, hcol, g8col, r8col, r4col, h0col, ccol, b1col, sbcol, k6col, zc0, zc, nrc, tcol, bias2, h35, bcol,
+     dcol, lxcol, ecol, q0col, q1col, k6f, rtcol, rdcol, pcol, gcol) = [A("col", i, i + 1) for i in range(28)]
 
-    def number(lv, second):
+    def number(lv, src, prev, second):
         c = 32 * lv
         nf, nd = A("nf", c, c + 32), A("nd", c, c + 32)
         s0 = 40 * lv
-        ts(nf, A("pa", 32 + c, 64 + c), 100.0 * lv, Op.is_le)
+        ts(nf, src, 100.0 * lv, Op.is_le)
         scan(A("sc", s0 + 1, s0 + 33), A("onesb", 0, 32), nf, Op.add, Op.subtract)
         tt(nd, nf, A("dc"), Op.mult)
         p1, pc = A("pb", 64 * lv, 64 * lv + 32), A("pb", 64 * lv + 32, 64 * lv + 33)
         mm(p1, A("tri"), nf, True, False)
-        mm(p1, A("bo"), A("sc", s0, s0 + 32), False, False)
-        mm(p1, A("ident"), nd, False, True)
-        mm(pc, A("prev"), A("sc", s0 + 32, s0 + 33))
+        mm(p1, A("prev"), nf, False, False)
+        glue(2)
+        mm(p1, A("ident"), nd, False, False)
+        mm(p1, A("bo"), A("sc", s0, s0 + 32), False, True)
+        mm(pc, prev, A("sc", s0 + 32, s0 + 33))
+        glue(2)
         ts(A("off", c, c + 32), p1, pc, Op.add, rcol, Op.add)
         ts(second, p1, pc, Op.add, rcol, Op.add)
 
+    def digits(li, cr, cu, n):
+        ts(A(cr, n, 2 * n), A(li), 15, Op.bitwise_and)
+        ts(A(cr, 0, n), A(li), 4, Op.logical_shift_right)
+        copy(A(cu), A(cr))
+
+    def block(gr):
+        return 4 * (gr % 2) + gr // 2
+
+    memset(A("d1", 16, 528), 1, 300.0)
     iota(A("pi", 0, 1), [[0, 1]], 0, 1, 200.0)
-    first = len(ops)
-    iota(A("d1"), [[1, 512]], -192, 32, 50.0)
-    load("s", A("x0", p1=8), T.x[0, :], "lx0", 1.9, 90.0)
-    load("a", A("bdi", p1=16), T.bd[:, :], "lbd", 1.9, 90.0)
-    load("s", A("xn"), T.x[:, :], "lxn", 2.4, 80.0)
-    for k in range(6):
-        load("sa"[k % 2], A("d1", 0, 512, 1, k, 128, 16), T.nb[k, :], "lnb", 2.1, 40.0)
+    iota(A("idb"), [[1, 32]], 0, 32, 190.0)
+    for h in range(2):
+        load("sa"[h], A("x0", 16 * h, 16 * h + 16), T.x[0, 2048 * h:2048 * h + 2048], "lx0", 2.0, 90.0)
+    load("a", A("bdi", p1=16), T.bd[:, :], "lbd", 1.9, 95.0)
     for k in range(8):
-        load("s", A("xw", 0, 4096, 1, 16 * k, 16 * k + 16), T.x[:, :], "lx", 4.5, 70.0 if k < 2 else 0.0,
-             () if k < 2 else (first,))
+        c = 512 * block(k)
+        load("sa"[k % 2], A("xn", 16, 528, 1, 16 * k, 16 * k + 16), T.x[:, c:c + 512], "lxn", 2.2, 80.0)
+    for k in range(8):
+        c = 512 * block(k)
+        last = load("sa"[k % 2], A("d1", 16, 528, 1, 16 * k, 16 * k + 6), T.nb[:, c:c + 512], "lnb", 2.2, 70.0)
+    load("s", A("d1", 16, 528, 1, 6, 128, 16), ap(A("idb")), "lnb", 2.0, 70.0, r=[A("idb")])
+    for k in range(8):
+        load("s", A("xw", 0, 4096, 1, 16 * k, 16 * k + 16), T.x[:, :], "lx", 4.0, 0.0, (last,) if LATEX else ())
 
     memset(A("onesb"), 1.0)
-    fill(A("pa0"), 1.0)
-    fill(A("pa0", 0, 128, 16), 0.0)
-    fill(A("pa1"), 0.0)
-    fill(A("pa1", 0, 128, 16), 1.0)
-    scan(A("iom"), A("onesb", 0, 128), A("pa0"), Op.add, Op.mult)
-    scan(A("iog"), A("pa1"), A("onesb", 0, 128), Op.add, Op.mult, -1.0)
-    fill(A("k64"), 64.0)
-    fill(A("w1", 0, 512), 0.0)
-    iota(A("w2", 0, 512), [[0, 512]], 0, 0)
+    for c in (0, 528):
+        memset(A("d1", c, c + 16), 0)
+        fill(A("xn", c, c + 16), 0.0)
+    iota(A("iom"), [[0, 8], [1, 16]], 0, 0)
+    iota(A("iog"), [[1, 8], [0, 16]], 0, 0)
+    iota(A("iob"), [[1, 4], [4, 2], [0, 16]], 0, 0, 20.0)
+    iota(A("dc"), [[128, 32]], DUM, 8)
+    for c in range(128, 640, 128):
+        fill(A("w1", c, c + 128), 0.0)
+    aff(A("w2", 0, 512), A("xn", 16, 528), 0.0)
     fill(A("sc"), 0.0)
     fill(A("sel"), -65536.0)
     fill(A("xw", ZC, 4240), 0.0)
     fill(A("xw", 4096 + 32 * rank, 4128 + 32 * rank), 0.0)
     fill(A("onesf"), 1.0)
-    for c in ("c1", "c2", "c3", "c4", "b1", "b2"):
+    for c in ("c1", "c2", "c4", "c5", "b2"):
         fill(A(c), 0.0)
     fill(A("nw", 264, 272), 8000.0)
-    fill(A("n2w", 32, 40), 512.0)
-    fill(A("t1", 0, 16), 0.0)
-    fill(A("nw2", 0, 8), 512.0)
-    fill(A("nw2", 304, 312), 512.0)
-    fill(A("win", 512, 528), 0.0)
+    fill(A("t1", TB, TB + 16), 0.0)
+    fill(A("nw2", 0, 1), float(DUM))
+    fill(A("nw2", 305, 344), float(DUM))
     ts(A("pk", 0, 1), A("pi", 0, 1), 15, Op.bitwise_and)
     ts(A("pk", 1, 2), A("pi", 0, 1), 4, Op.logical_shift_right)
     ts(A("pk", 2, 3), A("pi", 0, 1), 4, Op.logical_shift_right, 1, Op.bitwise_and)
-    ts(A("pk", 3, 4), A("pi", 0, 1), 3, Op.logical_shift_right)
-    ts(A("pk", 4, 5), A("pi", 0, 1), 7, Op.bitwise_and)
+    ts(A("pk", 3, 4), A("pi", 0, 1), 7, Op.bitwise_and)
+    ts(A("pk", 4, 5), A("pi", 0, 1), 3, Op.logical_shift_right, 1, Op.bitwise_and)
     copy(A("col", 0, 5), A("pk", 0, 5))
-    copy(pcol, A("pi", 0, 1))
-    ts(A("b1", 15, 128, 16), A("iom", 0, 8), pcol, Op.is_equal)
     ts(A("bo"), A("iog"), kcol, Op.is_equal)
     ts(A("prev"), A("iog"), kcol, Op.is_gt)
-    ts(A("tri0"), A("iom"), rcol, Op.is_gt, -1.0, Op.mult)
+    aff(h35, hcol, 3.5)
+    aff(bcol, kcol, 0.5, h35)
+    ts(A("prev1"), A("iob"), bcol, Op.is_gt)
+    ts(dcol, bcol, kcol, Op.subtract, 512.0, Op.mult)
+    aff(lxcol, bcol, -512.0, 16.0)
     ts(A("rf"), A("iom"), rcol, Op.is_equal)
-    aff(r4col, rcol, 4.0, DUM - 64.0)
-    tt(A("tri"), A("tri0"), A("bo"), Op.mult)
-    tt(A("ident"), A("rf"), A("bo"), Op.mult)
-    scan(A("dc"), A("k64"), A("onesb", 0, 32), Op.add, Op.mult, r4col)
+    ts(A("rfb"), A("iom"), rcol, Op.is_equal, float(DUM), Op.mult)
+    ts(A("eef", p1=16), A("iom", p1=16), A("col", 0, 1, p1=16), Op.is_equal)
+    scan(A("io128"), A("onesb", 0, 128), A("onesb", 0, 128), Op.add, Op.mult, -1.0)
+    copy(pcol, A("pi", 0, 1))
+    ts(A("tri"), A("io128"), pcol, Op.is_gt, -1.0, Op.mult)
+    ts(A("ident"), A("io128"), pcol, Op.is_equal)
     aff(h0col, hcol, -1.0, 1.0)
     aff(A("ee", 0, 128), A("rf"), h0col)
     aff(A("ee", 128, 256), A("rf"), hcol)
     ts(A("i16"), A("iom", 0, 16), rcol, Op.is_equal)
-    ts(A("i8"), A("iom", 0, 8), g8col, Op.is_equal)
-    ts(A("rx"), A("iom"), c8col, Op.is_equal)
-    ts(ccol, A("i16", 6, 7), A("i16", 7, 8), Op.subtract, ZC / 32.0, Op.mult)
-    aff(A("c1", 7, 128, 16), A("i16", 0, 8), None, ccol)
-    aff(A("c1", 15, 128, 16), A("i16", 0, 8), None, ccol)
-    copy(A("io8"), A("iom", 0, 8))
-    memset(A("obi", p0=96), 2)
+    aff(ccol, A("i16", 7, 8), -float(ZC))
+    ts(A("c1", 7, 128, 8), A("iog", 0, 128, 8), rcol, Op.is_equal, ccol, Op.add)
+    aff(ecol, A("i16", 7, 8), dcol)
+    ts(A("c1", 103, 112, 8), A("c1", 103, 112, 8), ecol, Op.add)
+    copy(A("io8", 0, 8), A("iom", 0, 8))
+    copy(A("io8", 8, 9), A("pk", 3, 4))
+    memset(A("obi", 0, 9, p0=96), 2)
     for d in range(3):
-        ts(A("obi", p0=32 * d, p1=32 * d + 32), A("io8", p0=32 * d, p1=32 * d + 32), d, Op.logical_shift_right,
-           1, Op.bitwise_and)
+        ts(A("obi", 0, 9, 1, 32 * d, 32 * d + 32), A("io8", 0, 9, 1, 32 * d, 32 * d + 32), d,
+           Op.logical_shift_right, 1, Op.bitwise_and)
     fill(A("urow", p1=1), 16.0)
     for q in range(7):
         st, base = [4 * ST, 2 * ST, ST], 16
         if q < 6:
             d, b = q // 2, q % 2
-            base += st[2 - d] + (0 if b else BIG)
-            st[2 - d] = -st[2 - d] + (BIG if b else -BIG)
+            base += st[2 - d]
+            st[2 - d] = -st[2 - d]
+        if q % 2 == 0:
+            iota(A("b8", 4 * q, 4 * q + 8), [[st[0], 2], [st[1], 2], [st[2], 2]], base, 0)
+        if q < 6:
+            base += 0 if b else BIG
+            st[2 - d] += BIG if b else -BIG
         iota(A("urow", q, 128, 16, 0, 1), [[st[0], 2], [st[1], 2], [st[2], 2]], base, 0)
     iota(A("ios"), [[1, 512]], 0, 0)
-    mine = A("nw2", 312 + 8 * rank, 320 + 8 * rank)
-    iota(mine, [[0, 8]], 512, 0, 30.0)
-    s0 = fused(lambda q: mine, lambda q: mine, "arr0", 2.5, 30.0)
-    arrive([A("nw2", 312 + 8 * q, 320 + 8 * q) for q in peers], "arr0", 4, (s0,))
+    iota(A("io2", 0, 8), [[1, 8]], 0, 0)
+    iota(A("io2", 8, 16), [[4, 2], [-2, 2], [1, 2]], 2, 0)
+    iota(A("cc"), [[128, 6]], 512, 1)
+    ts(A("th8"), A("iom", 0, 8), kcol, Op.not_equal, -1000.0, Op.mult)
     ts(b1col, rcol, 8.0, Op.is_lt, 98304.0, Op.mult)
     aff(sbcol, b1col, 1.0 / 3)
-    aff(A("sel", 1, 192, 2), A("sel", 0, 192, 2), None, b1col)
-    ts(A("obt"), A("obi"), hcol, Op.is_equal)
-    ts(k6col, kcol, 6.0, Op.is_equal, 0.625, Op.mult)
-    aff(A("m8", 0, 8), A("obt"), 0.125, k6col)
+    aff(A("sel", 1, 80, 2), A("sel", 0, 80, 2), None, b1col)
+    ts(A("obt", 0, 9), A("obi", 0, 9), hcol, Op.is_equal)
+    ts(k6f, kcol, 6.0, Op.is_equal)
+    aff(k6col, k6f, 0.625)
+    aff(A("m8", 0, 8), A("obt", 0, 8), 0.125, k6col)
     aff(A("jb"), A("iom", 0, 8), 16.0, rcol)
     aff(A("b2", 15, 128, 16), A("m8", 0, 8), A("i16", 0, 1))
+    aff(A("e0"), A("onesb", 0, 8), A("i16", 0, 1))
     for o in range(8):
-        aff(A("wo", 128 * o, 128 * o + 128), A("rf"), A("m8", o, o + 1))
+        aff(A("wo", o, 1024, 8), A("rf"), A("m8", o, o + 1))
     cut = min(2 + 2 * rank, 6)
-    aff(A("nw", 256, 256 + cut), A("jb", 0, cut), None, 512.0)
-    aff(A("nw", 256 + cut, 264), A("jb", cut, 8), None, 480.0)
+    aff(A("jn", 0, cut), A("jb", 0, cut), None, 512.0)
+    aff(A("jn", cut, 8), A("jb", cut, 8), None, 480.0)
     ts(A("rt"), A("iom"), kcol, Op.is_equal, -1.0, Op.mult)
     aff(A("c2", 7, 128, 8), A("bo", 0, 128, 8))
-    asel(A("pm", 0, 128), A("onesf"), [[-32, 4], [16, 2], [-1, 16]], Op.is_equal, -16, 1)
-    asel(A("pm", 128, 256), A("onesf"), [[-64, 2], [32, 2], [-1, 32]], Op.is_equal, -32, 1)
-    aff(A("c4", 7, 128, 16), A("i16", 0, 8), -1.0)
-    aff(A("c4", 15, 128, 16), A("i16", 0, 8), -1.0)
-    aff(A("cc"), A("iom", 0, 8), 128.0, rcol)
-    for o in range(8):
-        aff(A("pd", 38 * o + 32, 38 * o + 38), A("cc", 0, 6), None, 528.0 + 16 * o, "a")
-    copy(A("lj"), A("iom", 0, 8))
-    aff(A("m8", 8, 16), A("m8", 0, 8), 0.125)
-    aff(A("bc"), A("bo"), A("i16", 0, 1))
+    aff(A("c5", 7, 128, 8), A("onesb", 0, 16), k6f)
+    asel(A("pm", 0, 128), A("onesf"), [[-64, 2], [16, 4], [-1, 16]], Op.is_equal, -48, 1)
+    asel(A("pm", 128, 256), A("onesf"), [[64, 2], [32, 2], [-1, 32]], Op.is_equal, -96, 1)
+    ts(A("c4", 7, 128, 8), A("iog", 0, 128, 8), rcol, Op.is_equal, -1.0, Op.mult)
+    copy(A("lj"), A("io2"))
     ts(zc0, kcol, 6.0, Op.is_lt, 1.0 / 64, Op.mult)
     aff(zc, k6col, 0.625, zc0)
-    aff(A("m8", 24, 32), A("obt"), 1.0 / 16)
-    aff(A("m8", 16, 24), A("obt"), 7.0 / 64, zc)
-    tt(A("wc"), ind(A("m8", 8, 16), A("lj")), A("rf"), Op.mult)
-    tt(A("wz"), ind(A("m8", 16, 24), A("lj")), A("rf"), Op.mult)
-    tt(A("wm"), ind(A("m8", 24, 32), A("lj")), A("rf"), Op.mult)
-    aff(A("c3", 7, 128, 16), A("obt"), -1.0, 1.0)
-    aff(A("c3", 15, 128, 16), A("obt"), -1.0, 1.0)
+    aff(A("m8", 16, 24), A("obt", 0, 8), 3.0 / 64, zc)
+    aff(A("m8", 24, 32), A("obt", 0, 8), -1.0, 1.0)
+    aff(A("m8", 24, 32, 1, 32, 64), A("obt", 0, 8, 1, 32, 64))
+    tt(A("wc"), ind(A("m8", 0, 8), A("lj", 8, 16)), A("rf"), Op.mult)
+    tt(A("wz"), ind(A("m8", 16, 24), A("lj", 0, 8)), A("rf"), Op.mult)
+    aff(rtcol, sbcol, None, float(ROOT))
+    fill(A("lf"), 0.0)
+    tt(A("r3"), ind(A("m8", 24, 32), A("lj", 0, 8)), A("rf"), Op.mult)
+    aff(q1col, r8col, None, 8.0)
+    aff(q0col, A("obt", 8, 9), -8.0, q1col)
+    ts(A("lq", 0, 4), A("iom", 0, 4), 2.0, Op.mult, q0col, Op.add)
+    ts(A("lq", 4, 8), A("iom", 0, 4), 2.0, Op.mult, q1col, Op.add)
+    ts(gcol, kcol, hcol, Op.subtract, 4.0, Op.mult)
+    ts(A("lq", 8, 12), A("onesb", 0, 4), g8col, Op.mult, gcol, Op.add)
+    aff(rdcol, gcol, 64.0, 512.0)
+    aff(A("b64"), ind(A("b8"), A("lq", 8, 12)))
 
-    for r in range(16):
-        mm(A("pa", 32, 64), A("b1", 15 - r, 143 - r, 1, 0, 8), A("x0", r, 512, 16, 0, 8), r == 0, r == 15)
-    number(0, A("offh"))
+    add("v", lambda q: q.transpose(ap(A("xt")), ap(A("x0"))), [A("xt")], [A("x0")], 64 * VEC)
+    number(0, A("xt"), A("prev1"), A("offh"))
+
+    copy(A("bdg", p1=16), A("bdi", p1=16))
+    mm(A("pz", 0, 8), A("eef", p1=16), A("bdg", p1=16))
+    ts(A("lx"), A("pz", 0, 8), lxcol, Op.add, 528.0, Op.min)
+    aff(A("xa"), ind(A("xn"), A("lx")))
+    mm(A("pz", 128, 256), A("rf"), A("xa"))
+    aff(A("xb"), A("pz", 128, 256))
+    sa = fused(lambda q: A("xb", 32 * q, 32 * q + 32),
+               lambda q: A("xw", 4096 + 32 * rank, 4128 + 32 * rank), "arra", 1.5, 3.0)
+    arrive([A("xw", 4096 + 32 * q, 4128 + 32 * q) for q in peers], "arra", (sa,))
+    banks = ["p0", "p1", "p2"]
+
+    mm(A("p0", 0, 8), A("xw", 4096, ZC, p1=16), A("e0", p1=16))
+    tt(A("nfb"), A("p0", 0, 8), A("th8"), Op.is_le)
+    mm(A("p0", 8, 16), A("rfb"), A("nfb"))
+    tt(A("nw", 256, 264), A("p0", 8, 16), A("jn"), Op.add)
+
+    aff(A("w1", 0, 128), ind(A("d1"), A("lx")))
+    copy(ind(A("w1", 128), A("off", 0, 32)), A("d1", 16, 528))
+    spread(lambda gr: A("pd", 32 * block(gr), 32 * block(gr) + 32), A("offh"))
+    aff(A("nw", 0, 256), A("pd", 0, 256))
+    wrap8(A("pc", 0, 80), "c1", A("w1"), 640)
+    scan(A("sw", 0, 80), A("sel"), A("pc", 0, 80), Op.add, Op.max)
+    ts(A("l1u"), A("sw", 1, 80, 2), sbcol, Op.subtract, float(ZC), Op.add)
+    ts(A("li"), A("sw", 1, 80, 2), sbcol, Op.subtract, float(ZC), Op.add)
+    parts = ((0, 128), (128, 384), (384, 640))
+    for a, b in parts:
+        aff(A("gw", a, b), ind(A("xw"), A("l1u", a // 16, b // 16)))
+    digits("li", "lcr", "lcu", 40)
+    gw = A("gw", 128, 640)
     mm(A("pb", 100, 101), A("urow", p1=1), A("onesf", 0, 1, 1, 0, 1))
     ts(nrc, A("pb", 100, 101), float(ROOT), Op.min, -1.0, Op.mult)
     ts(tcol, A("pb", 100, 101), float(ROOT), Op.is_gt, 2.0 * BIG, Op.mult)
     ts(bias2, tcol, A("pb", 100, 101), Op.subtract, float(BIG), Op.subtract)
     aff(A("nr"), A("ios"), -1.0, nrc)
 
-    bdi = A("bdi", p1=16)
-    for h, (o0, s0, o1, s1) in enumerate(((Op.bitwise_and, 511, Op.logical_shift_right, 9),
-                                          (Op.logical_shift_right, 4, Op.bitwise_and, 15))):
-        ts(A("bdk", 16 * h, 16 * h + 8, p1=16), bdi, s0, o0)
-        ts(A("bdk", 16 * h + 8, 16 * h + 16, p1=16), bdi, s1, o1)
-        copy(A("bdf", 16 * h, 16 * h + 16, p1=16), A("bdk", 16 * h, 16 * h + 16, p1=16))
-    mm(A("pz", 0, 16), A("ee", 0, 128, 1, 0, 16), A("bdf", 0, 16, p1=16))
-    copy(A("bdu", 0, 16), A("pz", 0, 16))
-    aff(A("mka"), ind(A("i8"), A("bdu", 8, 16)))
-    tt(A("xa"), ind(A("xn"), A("bdu", 0, 8)), A("mka"), Op.mult)
-    mm(A("pz", 128, 256), A("rx"), A("xa"))
-    aff(A("gw", 512, 640), A("pz", 128, 256))
-    sa = fused(lambda q: A("gw", 512 + 32 * q, 544 + 32 * q),
-               lambda q: A("xw", 4096 + 32 * rank, 4128 + 32 * rank), "arra", 0.5, 3.0)
-    arrive([A("xw", 4096 + 32 * q, 4128 + 32 * q) for q in peers], "arra", 4, (sa,))
-    mm(A("pz", 16, 32), A("ee", 0, 128, 1, 0, 16), A("bdf", 16, 32, p1=16))
-    copy(A("bdu", 16, 32), A("pz", 16, 32))
-    banks = ["p0", "p1", "p2"]
-
-    copy(ind(A("w1"), A("off", 0, 32)), A("d1"))
-    spread(lambda gr: A("pc", 64 + 32 * gr, 96 + 32 * gr), A("offh"))
-    aff(A("nw", 0, 256), A("pc", 64, 320))
-    wrap8(A("pc", 0, 64), "c1", A("w1"), 512)
-    scan(A("sw", 0, 64), A("sel", 0, 64), A("pc", 0, 64), Op.add, Op.max)
-    ts(A("l1u"), A("sw", 1, 64, 2), sbcol, Op.subtract, float(ZC), Op.add)
-    ts(A("li"), A("sw", 1, 64, 2), sbcol, Op.subtract, float(ZC), Op.add)
-    for h in range(2):
-        aff(A("gw", 256 * h, 256 * h + 256), ind(A("xw"), A("l1u", 16 * h, 16 * h + 16)))
-    ts(A("lcr", 32, 64), A("li"), 15, Op.bitwise_and)
-    ts(A("lcr", 0, 32), A("li"), 4, Op.logical_shift_right)
-    copy(A("lcu"), A("lcr"))
-
-    aff(A("mk", 512, 640), ind(A("i16"), A("bdu", 24, 32)))
-    tt(A("tm", 512, 640), ind(A("nw"), A("bdu", 16, 24)), A("mk", 512, 640), Op.mult)
-    wrap8(A("pz", 256, 272), "c2", A("tm", 512, 640), 128)
-    scan(A("sb", 0, 16), A("sel", 0, 16), A("pz", 256, 272), Op.add, Op.max)
-    ts(A("nb1"), A("sb", 1, 16, 2), sbcol, Op.subtract, 512.0, Op.subtract)
-    tt(A("nb2"), A("nb1"), A("jb"), Op.min)
-    ts(A("lbu"), A("nb2"), 512.0, Op.add)
-    ts(A("bi"), A("nb1"), 0.0, Op.min, 512.0, Op.add)
-    ts(A("bcr", 8, 16), A("bi"), 15, Op.bitwise_and)
-    ts(A("bcr", 0, 8), A("bi"), 4, Op.logical_shift_right)
-    copy(A("bcu"), A("bcr"))
-    aff(A("mkb"), ind(A("i16"), A("bcu", 8, 16)))
-    aff(A("gb"), ind(A("gw"), A("lbu")))
-    sb = fused(lambda q: A("gb", 32 * q, 32 * q + 32),
+    sb = fused(lambda q: A("gw", 32 * q, 32 * q + 32),
                lambda q: A("gg", 32 * slot(q, rank), 32 * slot(q, rank) + 32), "arrb", 0.5)
-    arrive([A("gg")], "arrb", 4, (sb,))
+    arrive([A("gg")], "arrb", (sb,))
 
     for r in range(16):
-        mm(A("pa", 64, 96), A("b2", 15 - r, 143 - r), A("gw", r, 512, 16), r == 0, r == 15)
-    number(1, A("offf"))
-    for h in range(2):
-        c = (256 * h, 256 * h + 256)
-        aff(A("mk", *c), ind(A("i16"), A("lcu", 32 + 16 * h, 48 + 16 * h)))
-        tt(A("tm", *c), ind(A("nw"), A("lcu", 16 * h, 16 * h + 16)), A("mk", *c), Op.mult)
-        bank = A(("pz", "pc")[h], 0, 256)
-        mm(bank, A("rt"), A("tm", *c))
-        aff(A("d2", *c), bank, None, bias2)
+        mm(A("pa", 64, 96), A("b2", 15 - r, 143 - r), A("gw", 128 + r, 640, 16), r == 0, r == 15)
+    glue(16)
+    number(1, A("pa", 64, 96), A("prev"), A("n2h", 0, 32))
+    for h, (a, b) in enumerate(parts):
+        aff(A("mk", a, b), ind(A("i16"), A("lcu", 40 + a // 16, 40 + b // 16)))
+        tt(A("tm", a, b), ind(A("nw"), A("lcu", a // 16, b // 16)), A("mk", a, b), Op.mult)
+        if h:
+            bank = A(("pz", "pc")[h - 1], 0, 256)
+            mm(bank, A("rt"), A("tm", a, b))
+            aff(A("d2", a - 128, b - 128), bank, None, bias2)
+
+    wrap8(A("pd", 400, 416), "c2", A("tm"), 128)
+    wrap8(A("pd", 416, 432), "c5", A("tm"), 128)
+    scan(A("sb"), A("sel", 0, 32), A("pd", 400, 432), Op.add, Op.max)
+    ts(A("tb"), A("sb", 1, 32, 2), sbcol, Op.subtract)
+    tt(A("pv", 0, 64), ind(A("tb"), A("lq", 0, 4)), A("b64"), Op.add)
+    aff(A("pv", 64, 128), ind(A("tb"), A("lq", 4, 8)), None, float(ROOT))
+    tt(A("pv", 128, 192), A("pv", 0, 64), A("pv", 64, 128), Op.min)
+    ts(A("lvb"), A("pv", 128, 192), ROOT + 511.0, Op.min)
     tt(ind(A("w2"), A("off", 32, 64)), A("d2"), A("nr"), Op.max)
-    ts(A("n2w", 0, 32), A("offf"), 512.0, Op.min)
-    ts(A("n2h"), A("offf"), 512.0, Op.min)
-    spread(lambda gr: A("pd", 38 * gr, 38 * gr + 32), A("n2h"))
+    if LVB:
+        ops[-1]["after"] = (len(ops) - 2,)
+
     wrap8(A("pc", 320, 384), "c4", A("w2"), 512)
     scan(A("sw", 64, 128), A("sel", 0, 64), A("pc", 320, 384), Op.add, Op.max)
     ts(A("l2u"), A("sw", 65, 128, 2), sbcol, Op.subtract)
     ts(A("li2"), A("sw", 65, 128, 2), sbcol, Op.subtract)
+    ts(A("l2r"), A("sw", 65, 128, 2), rtcol, Op.is_ge, rdcol, Op.mult)
+    aff(A("l2t"), A("sw", 65, 128, 2), None, float(TB))
+    tt(A("l2s"), A("l2r"), A("l2t"), Op.add)
 
-    asel(A("t1", ROOT, ROOT + 512), A("gw", 0, 512), [[0, 512]], Op.is_ge, 0, 0)
+    asel(A("t1", TB + ROOT, TB + ROOT + 512), gw, [[0, 512]], Op.is_ge, 0, 0)
+    for d in range(3):
+        for f in range(8):
+            q = 2 * d + 1 - ((f ^ 2) >> d & 1)
+            src = A("t1", TB + ROOT, TB + ROOT + 512, 1, 16 * q, 16 * q + 16)
+            c = TB + ROOT + 512 * (d + 1)
+            load("s", A("t1", c, c + 512, 1, 16 * f, 16 * f + 16), ap(src), "lrt", 3.0, 0.0, r=[src])
+        glue(8)
+    if NDMA:
+        mm(A("p2"), A("wo", 0, 128), gw)
+        aff(A("yt"), A("p2"))
     for o in range(8):
-        mm(A(banks[o % 3]), A("wo", 128 * o, 128 * o + 128), A("gw", 0, 512))
-        aff(A("t1", 16 + ST * o, 528 + ST * o), A(banks[o % 3]))
-        store("s", T.y1[16 * o:16 * o + 16, :], A("t1", 16 + ST * o, 528 + ST * o, 1, 16 * o, 16 * o + 16), "oy1")
+        c = TB + 16 + ST * o
+        if o < NDMA:
+            src = A("yt", 0, 512, 1, o, 128, 8)
+            for f in range(8):
+                add("s", lambda q, f=f, c=c, src=src: q.dma_start(ap(A("t1", c, c + 512, 1, 16 * f, 16 * f + 16)), ap(src)),
+                    [A("t1", c, c + 512, 1, 16 * f, 16 * f + 16)], [src], DMAC, "lt1", 16, True, 2.3)
+            glue(8)
+            store("s", T.y1[16 * o:16 * o + 16, :], src, "oy1")
+            continue
+        mm(A(banks[o % 3]), A("wo", o, 1024, 8), gw)
+        aff(A("t1", c, c + 512), A(banks[o % 3]))
+        store("s", T.y1[16 * o:16 * o + 16, :], A("t1", c, c + 512, 1, 16 * o, 16 * o + 16), "oy1")
     for o in range(8):
-        mm(A(("pz", "pb")[o // 4], 128 + 96 * (o % 4), 224 + 96 * (o % 4)), A("wo", 128 * o, 128 * o + 128), A("gg"))
+        mm(A(("pz", "pb")[o // 4], 128 + 96 * (o % 4), 224 + 96 * (o % 4)), A("wo", o, 1024, 8), A("gg"))
+        glue(1 + o % 4)
     for o in range(8):
-        aff(A("t1", 528 + ST * o, 624 + ST * o), A(("pz", "pb")[o // 4], 128 + 96 * (o % 4), 224 + 96 * (o % 4)))
+        c = TB + 528 + ST * o
+        aff(A("t1", c, c + 96), A(("pz", "pb")[o // 4], 128 + 96 * (o % 4), 224 + 96 * (o % 4)))
+    t1 = A("t1", TB, TB + ROOT + 512)
 
-    tt(A("tmb"), ind(A("n2w"), A("bcu", 0, 8)), A("mkb"), Op.mult)
-    wrap8(A("pa", 144, 160), "c2", A("tmb"), 128)
-    scan(A("sb", 16, 32), A("sel", 0, 16), A("pa", 144, 160), Op.add, Op.max)
-    ts(A("nbb"), A("sb", 17, 32, 2), sbcol, Op.subtract)
-    spread(lambda gr: A("pa", 192 + gr, 256, 8), A("nbb", 0, 8))
-    copy(A("l8u"), A("pa", 192, 256))
-
-    for h in range(2):
-        c = (256 * h, 256 * h + 256)
-        aff(A("v", *c), ind(A("t1"), A("l2u", 16 * h, 16 * h + 16)))
-        mm(A(banks[h], 0, 256), A("wc"), A("v", *c))
-        aff(A("win", *c), A(banks[h], 0, 256))
-
-    order = sorted(peers, key=lambda q: topo.die(cores[q]) == topo.die(core))
+    def turns(at):
+        return sorted((at ^ k for k in range(1, len(cores))), key=lambda q: topo.die(cores[q]) == topo.die(cores[at]))
+    order = turns(rank)
     sent = []
     for i, q in enumerate(order):
-        o = A("cb", 256 * q, 256 * q + 256)
-        for h in range(2):
-            aff(A("cb", 256 * q + 128 * h, 256 * q + 128 * h + 128),
-                ind(A("win", 0, 528), A("l8u", 16 * q + 8 * h, 16 * q + 8 * h + 8)))
+        o = A("vb", 256 * i, 256 * i + 256)
+        aff(o, ind(t1, A("lvb", 16 * q, 16 * q + 16)))
+        if i >= RAW:
+            mm(A(banks[i], 0, 256), A("wc"), o)
+            o = A("vc", 256 * i, 256 * i + 256)
+            aff(o, A(banks[i], 0, 256))
         rid, pid = topo.addr(cores[q])[:2]
         s = slot(q, rank)
         m = topo.mask(core, cores[q])
-        sent.append(add("g", lambda x, o=o, s=s, rid=rid, pid=pid, m=m: x.remote_dma(
-            ap(A("win", 528 + 256 * s, 784 + 256 * s)), ap(o), T.sem.arrc, T.sem.sent, pid, rid, m),
+        land = A("t1", 512 + 256 * s, 768 + 256 * s) if i >= RAW else A("vg", 256 * s, 256 * s + 256)
+        sent.append(add("g", lambda x, o=o, s=s, rid=rid, pid=pid, m=m, land=land: x.remote_dma(
+            ap(land), ap(o), T.sem["arrc%d" % s], T.sem.sent, pid, rid, m),
             [], [o], 0.4, "sent", len(topo.engines(core, cores[q])), lat=2.3))
-    arrive([A("win", 528, 1296)], "arrc", 1, tuple(sent))
 
+    for r in range(16):
+        mm(A("pa", 128, 134), A("b2", 15 - r, 143 - r), A("gg", r, 96, 16), r == 0, r == 15)
+    glue(16)
+    ts(A("nfg"), A("pa", 128, 134), 100.0, Op.is_le, float(DUM), Op.mult)
+    tt(A("n2h", 32, 38), A("nfg"), A("cc"), Op.add)
+    spread(lambda gr: A("pd", 38 * gr, 38 * gr + 38), A("n2h", 0, 38))
     aff(A("nw2", 1, 305), A("pd", 0, 304))
-    ts(A("lcr2", 32, 64), A("li2"), 15, Op.bitwise_and)
-    ts(A("lcr2", 0, 32), A("li2"), 4, Op.logical_shift_right)
-    copy(A("lcu2"), A("lcr2"))
+
+    for h in range(2):
+        c = (256 * h, 256 * h + 256)
+        aff(A("v", *c), ind(t1, A("l2u", 16 * h, 16 * h + 16)))
+        mm(A(("pa", "pb")[h], 0, 256), A("wc"), A("v", *c))
+        aff(A("t1", *c), A(("pa", "pb")[h], 0, 256))
+    for i in range(3):
+        q = [p for p in peers if turns(p)[i] == rank][0]
+        s = slot(rank, q)
+        land = A("t1", 512 + 256 * s, 768 + 256 * s) if i >= RAW else A("vg", 256 * s, 256 * s + 256)
+        add("-", None, [land], [], 0.0, "arrc%d" % s, len(topo.engines(cores[q], core)), after=(sent[i],))
+        if i >= RAW:
+            continue
+        mm(A(banks[i], 0, 256), A("wc"), A("vg", 256 * s, 256 * s + 256))
+        aff(A("t1", 512 + 256 * s, 768 + 256 * s), A(banks[i], 0, 256))
+
+    digits("li2", "lcr2", "lcu2", 32)
     for h in range(2):
         c = (256 * h, 256 * h + 256)
         aff(A("mk2", *c), ind(A("i16"), A("lcu2", 32 + 16 * h, 48 + 16 * h)))
         tt(A("tm2", *c), ind(A("nw2"), A("lcu2", 16 * h, 16 * h + 16)), A("mk2", *c), Op.mult)
+    wrap8(A("pc", 0, 64), "c2", A("tm2"), 512)
+    scan(A("sw", 128, 192), A("sel", 0, 64), A("pc", 0, 64), Op.add, Op.max)
     for d in range(3):
-        wrap8(A("pc", 64 * d, 64 * d + 64), "c3", A("tm2"), 512, 32 * d, 32 * d + 32)
-    scan(A("sw", 128, 320), A("sel"), A("pc", 0, 192), Op.add, Op.max)
-    ts(A("lfu"), A("sw", 129, 320, 2), sbcol, Op.subtract)
-    add("a", lambda q: q.activation(ap(A("sg")), ap(A("v")), Fn.Sign, bias=100.0625, scale=-1.0),
-        [A("sg")], [A("v")], 0.55)
-    mm(A("p2"), A("bc"), A("sg"))
-    tt(A("vs"), A("p2"), A("v"), Op.mult)
-    zb = ["pz", "pd"]
-    for h in range(2):
-        c = (256 * h, 256 * h + 256)
-        mm(A(zb[h], 0, 256), A("wz"), A("v", *c), True, False)
-        mm(A(zb[h], 0, 256), A("wm"), A("vs", *c), False, False)
+        p = (32 * d, 32 * d + 32)
+        tt(A("lf", p[0], p[1], 1, *p), A("sw", 129, 192, 2, *p), A("l2s", 0, 32, 1, *p), Op.min)
+    mm(A("pc", 128, 224), A("r3", p1=96), A("lf", p1=96))
+    ts(A("lfu"), A("pc", 128, 224), sbcol, Op.subtract)
+    zb = ["pz", "pd", "pa", "pb"]
+    cuts = list(zip(CUTS, CUTS[1:]))
+    for h, (a, b) in enumerate(cuts):
+        mm(A(zb[h], 0, b - a), A("wz"), A("v", a, b), True, False)
 
-    for h in range(2):
-        for d in range(3):
-            c = 512 * d + 256 * h
-            aff(A("gd", c, c + 256), ind(A("win"), A("lfu", c // 16, c // 16 + 16)))
-            if d < 2:
-                mm(A(zb[h], 0, 256), A("pm", 128 * d, 128 * d + 128), A("gd", c, c + 256), False, d == 1)
-        for p in (0, 64):
-            tt(A("yo", 256 * h, 256 * h + 256, 1, p, p + 64), A(zb[h], 0, 256, 1, p, p + 64),
-               A("gd", c, c + 256, 1, 64 - p, 128 - p), Op.add)
-            store("sa"[p // 64], T.y2[p:p + 64, 256 * h:256 * h + 256],
-                  A("yo", 256 * h, 256 * h + 256, 1, p, p + 64), "oy2")
+    for h, (a, b) in enumerate(cuts):
+        for j, d in enumerate((0, 2, 1)):
+            gd = A("gd", 512 * d + a, 512 * d + b)
+            aff(gd, ind(A("t1"), A("lfu", gd[1] // 16, gd[2] // 16)), 0.125)
+            if j < 2:
+                mm(A(zb[h], 0, b - a), A("pm", 128 * j, 128 * j + 128), gd, False, j == 1)
+        tt(A("yo", a, b), A(zb[h], 0, b - a), gd, Op.add)
+        store("sa"[h % 2], T.y2[:, a:b], A("yo", a, b), "oy2")
 
     total = emit(g, T, arrange(ops))
     g.sync.wait_ge(T.sem.oy1, total["oy1"])
     g.sync.wait_ge(T.sem.oy2, total["oy2"])
     g.wait_ge(T.sem.sent, total["sent"])
+
+
+LATEX = False
+NDMA = 2
+DMAC = 0.12
+LVB = False
+RAW = 1
+CUTS = (0, 128, 256, 384, 512)

@@ -10,20 +10,20 @@ DUM = 8256
 BIG = 16384
 
 SB = {
-    "xw": (4240, BF), "xn": (544, BF), "x0": (32, BF), "xt": (32, BF), "d1": (544, I32), "idb": (32, I32),
+    "xw": (4240, BF), "xn": (544, BF), "x0": (32, BF), "xt": (32, BF), "d1": (544, I32), "idb": (64, I32),
     "bdi": (8, I32), "bdg": (8, F32), "lx": (8, U16), "xa": (128, BF), "xb": (128, BF),
     "eef": (128, F32), "e0": (8, BF), "th8": (8, F32), "nfb": (8, BF), "jn": (8, F32),
     "w1": (13888, F32), "w2": (13760, F32), "gw": (640, BF), "gg": (96, BF),
     "onesb": (144, BF), "onesf": (128, F32), "b2": (144, BF), "pi": (4, I32), "pk": (8, I32),
-    "col": (32, F32), "iog": (128, BF), "iom": (128, BF), "iob": (128, BF), "bo": (128, BF), "prev": (128, BF),
+    "col": (40, F32), "iog": (128, BF), "iom": (128, BF), "iob": (128, BF), "bo": (128, BF), "prev": (128, BF),
     "prev1": (128, BF), "rf": (128, BF), "rfb": (128, BF),
     "ident": (128, BF), "tri": (128, BF), "dc": (32, F32), "i16": (16, F32),
-    "yt": (512, F32), "n2h": (40, F16), "offh": (32, F16), "io8": (12, I32), "io2": (16, I32),
+    "yt": (1024, F32), "n2h": (40, F16), "offh": (32, F16), "io8": (12, I32), "io2": (16, I32),
     "ee": (256, BF), "c1": (136, F32), "c4": (136, F32), "c2": (136, BF), "c5": (136, BF), "sel": (80, F32),
     "obi": (12, I32), "obt": (12, F32), "m8": (40, F32), "lj": (16, U16), "wc": (128, F32), "wz": (128, F32),
     "l2r": (32, F32), "l2t": (32, F32), "io128": (128, BF),
     "r3": (128, F32), "wo": (1024, BF), "rt": (128, BF), "pm": (256, F32), "urow": (128, F32),
-    "ios": (512, F32), "nr": (512, F32), "jb": (8, F32), "cc": (6, F32), "nw": (272, F32), "nw2": (344, F32),
+    "ios": (256, BF), "nr": (512, F32), "jb": (8, F32), "cc": (6, F32), "nw": (272, F32), "nw2": (344, F32),
     "nf": (64, BF), "sc": (80, BF), "nd": (64, F16), "off": (64, U16), "b8": (32, F32), "b64": (64, F32),
     "nfg": (6, F32), "lq": (12, U16), "tb": (16, F32), "pv": (192, F32),
     "lvb": (64, U16), "sw": (192, F32), "sb": (32, F32), "l1u": (40, U16), "l2u": (32, U16), "li": (40, I32),
@@ -43,9 +43,9 @@ ENG_SEM = {"v": "cv", "a": "ca", "t": "ct", "g": "cg"}
 GAP = 0.11
 VEC = 0.00104
 PE = 0.00052
-TRIES = 24000
-SLACK = 0.6
-SEED = 1
+TRIES = 1000
+SLACK = 0.2
+SEED = 5
 PLANS = {}
 
 
@@ -103,6 +103,7 @@ def arrange(ops):
         down = [[i] + [j for j in range(i + 1, n) if above[j] >> i & 1] for i in range(n)]
         alt = [[(e, c) for e, f, c in o["alt"]] for o in ops]
         lat = [o["lat"] for o in ops]
+        slow = [o["slow"] for o in ops]
 
         def sweep(key, first, then, back, bias):
             lo, hi = {e: [] for e in "vatgs-"}, {e: [] for e in "vatgs-"}
@@ -126,7 +127,7 @@ def arrange(ops):
                     while k < m and t + c > a[k] + 1e-9:
                         t = b[k]
                         k += 1
-                    v = t + c + (bias[i] if e == "v" else 0.0)
+                    v = t + c + (bias[i] if e == "v" else 0.0 if e == "a" else -abs(bias[i]))
                     if top is None or v < top[0]:
                         top = (v, t, t + c, e, k)
                 v, start[i], t, e, k = top
@@ -146,7 +147,18 @@ def arrange(ops):
 
         def plan(key, bias, again):
             start, end, pick = sweep(key, before, behind, False, bias)
-            one = (max(end) + 0.02 * sum(end) / n, start, end, pick, bias)
+            free, late = {}, [0.0] * n
+            for i in sorted(range(n), key=lambda x: (start[x], x)):
+                e = pick[i]
+                t = free.get(e, 0.0)
+                for j, gap in before[i]:
+                    if late[j] + gap > t:
+                        t = late[j] + gap
+                t += (end[i] - start[i] - lat[i]) * slow[i]
+                late[i] = t + lat[i]
+                if e != "-":
+                    free[e] = t
+            one = (max(end) + MIX * max(late) + 0.02 * sum(end) / n, start, end, pick, bias, max(late))
             if again:
                 two = plan(sweep(end, behind, before, True, bias)[1], bias, False)
                 one = two if two[0] < one[0] else one
@@ -163,7 +175,7 @@ def arrange(ops):
             level[i] = min(c for e, c in alt[i]) + lat[i] + max([level[k] + gap for k, gap in behind[i]] + [0.0])
         now = best = plan(level, [0.0] * n, True)
         for trial in range(TRIES):
-            start, end, pick, bias = now[1:]
+            start, end, pick, bias = now[1:5]
             key = [-x for x in start]
             prior, last = {}, {}
             for i in sorted(range(n), key=lambda x: start[x]):
@@ -202,7 +214,72 @@ def arrange(ops):
                 now = new
             if new[0] < best[0]:
                 best = new
-        PLANS[n] = (max(best[2]), best[1], best[3], ops)
+        cost = [dict(a) for a in alt]
+
+        def run(order, pick, factor):
+            free, last = {}, {}
+            start, end, why = [0.0] * n, [0.0] * n, [None] * n
+            for i in order:
+                e = pick[i]
+                t, w = free.get(e, 0.0), last.get(e)
+                for j, gap in before[i]:
+                    if end[j] + gap > t:
+                        t, w = end[j] + gap, j
+                start[i], why[i] = t, w
+                t += cost[i][e] * factor[i]
+                end[i] = t + lat[i]
+                if e != "-":
+                    free[e], last[e] = t, i
+            return start, end, why
+
+        def judge(order, pick):
+            a, b = run(order, pick, even), run(order, pick, slow)
+            return max(a[1]) + MIX * max(b[1]) + 0.02 * sum(a[1]) / n, order, pick, a, b
+
+        even = [1.0] * n
+        now = best = judge(sorted(range(n), key=lambda x: (best[1][x], x)), best[3])
+        for trial in range(MOVES):
+            order, pick = now[1:3]
+            start, end, why = now[3 + trial % 2]
+            i, chain = max(range(n), key=lambda x: end[x]), []
+            while why[i] is not None:
+                if not above[i] >> why[i] & 1:
+                    chain.append((i, why[i]))
+                i = why[i]
+            u = rand()
+            if u < 0.15 or not chain:
+                a = int(rand(n - 12))
+                j, i = order[a], order[a + 1 + int(rand(11))]
+                if above[i] >> j & 1:
+                    continue
+            else:
+                i, j = chain[int(rand(len(chain)))]
+            if u > 0.8:
+                x = i if rand() < 0.5 else j
+                if len(alt[x]) < 2:
+                    continue
+                pick = list(pick)
+                pick[x] = [e for e, c in alt[x] if e != pick[x]][int(rand(len(alt[x]) - 1))]
+            else:
+                a, b = order.index(j), order.index(i)
+                far = int(rand() ** 3 * 40)
+                if rand() < 0.5:
+                    a = max(0, a - far)
+                    part = order[a:b + 1]
+                    mask = above[i] | 1 << i
+                    order = order[:a] + [x for x in part if mask >> x & 1] + [x for x in part if not mask >> x & 1] + order[b + 1:]
+                else:
+                    b = min(n - 1, b + far)
+                    part = order[a:b + 1]
+                    order = (order[:a] + [x for x in part if x != j and not above[x] >> j & 1]
+                             + [x for x in part if x == j or above[x] >> j & 1] + order[b + 1:])
+            new = judge(order, pick)
+            if new[0] <= now[0] + HEAT * rand() ** 3 * (1 - trial / MOVES):
+                now = (new[0], sorted(order, key=lambda x: new[3][0][x])) + new[2:]
+                if new[0] < best[0]:
+                    best = new
+        place = {x: k for k, x in enumerate(best[1])}
+        PLANS[n] = ((max(best[3][1]), max(best[4][1])), [best[3][0][x] + 1e-6 * place[x] for x in range(n)], best[2], ops)
     score, start, pick = PLANS[n][:3]
     for o, i in zip(calls, home):
         o["e"], o["f"] = [x[:2] for x in o["alt"] if x[0] == pick[i]][0]
@@ -294,7 +371,9 @@ def rank_program(g, core, T, topo):
         names = set(x[0] for x in ww + rr)
         ops.append({"e": e, "f": f, "w": ww, "r": rr, "sem": sem, "inc": inc, "dma": dma, "c": c, "lat": lat,
                     "pri": pri, "after": after, "names": names, "banks": names & set(PSUM), "tile": tile,
-                    "alt": alt or [(e, f, c)], "glue": False})
+                    "alt": alt or [(e, f, c)], "glue": False,
+                    "slow": 1.0 if sem else 1.7 if len(rr) > len(r) and w[0][0] == "ind" else
+                    1.5 if any(isinstance(x, tuple) and x[0] == "ind" for x in r) else 1.2})
         return len(ops) - 1
 
     def glue(n):
@@ -360,10 +439,13 @@ def rank_program(g, core, T, topo):
         alt = [x for x in (("a", on_a, cost(o, i) + 0.015), ("v", on_v, half(o, i))) if e in ("*", x[0])]
         add(e, alt[0][1], [o], [i, scale, bias], alt[0][2], alt=alt)
 
-    def fill(o, c):
-        src = A("onesb", 0, width(o), 1, o[4], o[5])
-        alt = [("a", lambda q: q.activation(ap(o), ap(src), Fn.Identity, scale=float(c)), cost(o, o) + 0.015),
-               ("v", lambda q: q.memset(ap(o), c), half(o, o))]
+    def fill(o, c, src=None):
+        scale = 0.0 if src else float(c)
+        src = src or A("onesb", 0, width(o), 1, o[4], o[5])
+        alt = [("a", lambda q: q.activation(ap(o), ap(src), Fn.Identity, scale=scale), cost(o, o) + 0.015),
+               ("v", lambda q: q.memset(ap(o), c), half(o, o)),
+               ("g", lambda q: q.iota(ap(o), [[0, width(o)]], int(c), 0, allow_small_or_imprecise_dtypes=True),
+                0.16 + width(o) * 2 * VEC)]
         add("*", alt[0][1], [o], [src], alt[0][2], alt=alt)
 
     def mm(o, l, r, start=True, stop=True):
@@ -387,24 +469,23 @@ def rank_program(g, core, T, topo):
     def slot(at, q):
         return q if q < at else q - 1
 
-    def fused(src_of, dst_of, sem, c, pri=0.0):
+    def share(at, q, wide):
+        en = topo.engines(cores[at], cores[q])
+        w, j = len(en) // 4, slot(at, q)
+        return en[0 if wide and not j else (j + 1) * w:(j + 2) * w]
+
+    def fused(src_of, dst_of, sem, c, wide):
         tr = []
-        n = 0
         for q in peers:
-            en = topo.engines(core, cores[q])
-            w = len(en) // 4
-            j = slot(rank, q)
             rid, pid = topo.addr(cores[q])[:2]
             tr.append(RemoteDMATransfer(dst_ids=[DstId(rid=rid, pnc=pid)],
-                                        dma_engine_mask=sum(1 << e for e in en[(j + 1) * w if j else 0:(j + 2) * w]),
+                                        dma_engine_mask=sum(1 << e for e in share(rank, q, wide)),
                                         remote_sem=T.sem[sem], src=ap(src_of(q)), dst=ap(dst_of(q))))
-            n += w if j else 2 * w
         return add("g", lambda x: x.remote_dma_fused(tr, local_sem=T.sem.sent), [], [src_of(q) for q in peers], c,
-                   "sent", n, lat=2.3, pri=pri)
+                   "sent", sum(len(share(rank, q, wide)) for q in peers), lat=2.3)
 
-    def arrive(regions, sem, after):
-        n = sum(len(topo.engines(cores[q], core)) // (4 if slot(q, rank) else 2) for q in peers)
-        add("-", None, regions, [], 0.0, sem, n, after=after)
+    def arrive(regions, sem, after, wide):
+        add("-", None, regions, [], 0.0, sem, sum(len(share(q, rank, wide)) for q in peers), after=after)
 
     def wrap8(o, c, src, n):
         for b in range(8):
@@ -419,7 +500,8 @@ def rank_program(g, core, T, topo):
             glue(1 + h)
 
     (rcol, kcol, hcol, g8col, r8col, r4col, h0col, ccol, b1col, sbcol, k6col, zc0, zc, nrc, tcol, bias2, h35, bcol,
-     dcol, lxcol, ecol, q0col, q1col, k6f, rtcol, rdcol, pcol, gcol) = [A("col", i, i + 1) for i in range(28)]
+     dcol, lxcol, ecol, q0col, q1col, k6f, rtcol, rdcol, pcol, gcol, onec, rhalf, nrc2, rsb, nsb) = [
+        A("col", i, i + 1) for i in range(33)]
 
     def number(lv, src, prev, second):
         c = 32 * lv
@@ -444,12 +526,14 @@ def rank_program(g, core, T, topo):
         ts(A(cr, 0, n), A(li), 4, Op.logical_shift_right)
         copy(A(cu), A(cr))
 
+    def wo(o):
+        return A("wo", 512 * (o // 4) + o % 4, 512 * (o // 4) + 512, 4)
+
     def block(gr):
         return 4 * (gr % 2) + gr // 2
 
-    memset(A("d1", 16, 528), 1, 300.0)
     iota(A("pi", 0, 1), [[0, 1]], 0, 1, 200.0)
-    iota(A("idb"), [[1, 32]], 0, 32, 190.0)
+    iota(A("idb"), [[32, 2], [1, 32]], 0, 32, 190.0)
     for h in range(2):
         load("sa"[h], A("x0", 16 * h, 16 * h + 16), T.x[0, 2048 * h:2048 * h + 2048], "lx0", 2.0, 90.0)
     load("a", A("bdi", p1=16), T.bd[:, :], "lbd", 1.9, 95.0)
@@ -458,8 +542,11 @@ def rank_program(g, core, T, topo):
         load("sa"[k % 2], A("xn", 16, 528, 1, 16 * k, 16 * k + 16), T.x[:, c:c + 512], "lxn", 2.2, 80.0)
     for k in range(8):
         c = 512 * block(k)
-        last = load("sa"[k % 2], A("d1", 16, 528, 1, 16 * k, 16 * k + 6), T.nb[:, c:c + 512], "lnb", 2.2, 70.0)
-    load("s", A("d1", 16, 528, 1, 6, 128, 16), ap(A("idb")), "lnb", 2.0, 70.0, r=[A("idb")])
+        last = load("sa"[k % 2], A("d1", 16, 528, 1, 16 * k, 16 * k + 12, 2), T.nb[:, c:c + 512], "lnb", 2.2, 70.0)
+    for h in range(2):
+        load("s", A("d1", 16, 528, 1, 12 + 2 * h, 128, 16), ap(A("idb", 32 * h, 32 * h + 32)), "lnb", 2.0, 70.0,
+             r=[A("idb")])
+        load("sa"[h], A("d1", 16, 528, 1, 64 * h + 1, 64 * h + 64, 2), T.nb[0:4, :], "lnb", 2.2, 70.0)
     for k in range(8):
         load("s", A("xw", 0, 4096, 1, 16 * k, 16 * k + 16), T.x[:, :], "lx", 4.0, 0.0, (last,) if LATEX else ())
 
@@ -473,7 +560,7 @@ def rank_program(g, core, T, topo):
     iota(A("dc"), [[128, 32]], DUM, 8)
     for c in range(128, 640, 128):
         fill(A("w1", c, c + 128), 0.0)
-    aff(A("w2", 0, 512), A("xn", 16, 528), 0.0)
+    fill(A("w2", 0, 512), 0.0, A("xn", 16, 528))
     fill(A("sc"), 0.0)
     fill(A("sel"), -65536.0)
     fill(A("xw", ZC, 4240), 0.0)
@@ -509,9 +596,11 @@ def rank_program(g, core, T, topo):
     aff(A("ee", 0, 128), A("rf"), h0col)
     aff(A("ee", 128, 256), A("rf"), hcol)
     ts(A("i16"), A("iom", 0, 16), rcol, Op.is_equal)
-    aff(ccol, A("i16", 7, 8), -float(ZC))
-    ts(A("c1", 7, 128, 8), A("iog", 0, 128, 8), rcol, Op.is_equal, ccol, Op.add)
-    aff(ecol, A("i16", 7, 8), dcol)
+    ts(onec, A("i16", 14, 15), A("i16", 12, 13), Op.subtract, 1.0 / 32, Op.mult)
+    aff(ccol, onec, -float(ZC))
+    aff(rhalf, rcol, 0.5)
+    ts(A("c1", 7, 128, 8), A("iog", 0, 128, 8), rhalf, Op.is_equal, ccol, Op.add)
+    aff(ecol, onec, dcol)
     ts(A("c1", 103, 112, 8), A("c1", 103, 112, 8), ecol, Op.add)
     copy(A("io8", 0, 8), A("iom", 0, 8))
     copy(A("io8", 8, 9), A("pk", 3, 4))
@@ -532,10 +621,10 @@ def rank_program(g, core, T, topo):
             base += 0 if b else BIG
             st[2 - d] += BIG if b else -BIG
         iota(A("urow", q, 128, 16, 0, 1), [[st[0], 2], [st[1], 2], [st[2], 2]], base, 0)
-    iota(A("ios"), [[1, 512]], 0, 0)
+    iota(A("ios"), [[1, 256]], 0, 0)
     iota(A("io2", 0, 8), [[1, 8]], 0, 0)
     iota(A("io2", 8, 16), [[4, 2], [-2, 2], [1, 2]], 2, 0)
-    iota(A("cc"), [[128, 6]], 512, 1)
+    iota(A("cc"), [[128, 6]], 512 + DUM // 2, 1)
     ts(A("th8"), A("iom", 0, 8), kcol, Op.not_equal, -1000.0, Op.mult)
     ts(b1col, rcol, 8.0, Op.is_lt, 98304.0, Op.mult)
     aff(sbcol, b1col, 1.0 / 3)
@@ -548,7 +637,7 @@ def rank_program(g, core, T, topo):
     aff(A("b2", 15, 128, 16), A("m8", 0, 8), A("i16", 0, 1))
     aff(A("e0"), A("onesb", 0, 8), A("i16", 0, 1))
     for o in range(8):
-        aff(A("wo", o, 1024, 8), A("rf"), A("m8", o, o + 1))
+        aff(wo(o), A("rf"), A("m8", o, o + 1))
     cut = min(2 + 2 * rank, 6)
     aff(A("jn", 0, cut), A("jb", 0, cut), None, 512.0)
     aff(A("jn", cut, 8), A("jb", cut, 8), None, 480.0)
@@ -569,14 +658,16 @@ def rank_program(g, core, T, topo):
     aff(rtcol, sbcol, None, float(ROOT))
     fill(A("lf"), 0.0)
     tt(A("r3"), ind(A("m8", 24, 32), A("lj", 0, 8)), A("rf"), Op.mult)
-    aff(q1col, r8col, None, 8.0)
-    aff(q0col, A("obt", 8, 9), -8.0, q1col)
-    ts(A("lq", 0, 4), A("iom", 0, 4), 2.0, Op.mult, q0col, Op.add)
-    ts(A("lq", 4, 8), A("iom", 0, 4), 2.0, Op.mult, q1col, Op.add)
+    aff(q1col, r8col, 2.0, 17.0)
+    aff(q0col, A("obt", 8, 9), -16.0, q1col)
+    aff(rsb, sbcol, -1.0, float(ROOT))
+    aff(nsb, sbcol, -1.0)
+    ts(A("lq", 0, 4), A("iom", 0, 4), 4.0, Op.mult, q0col, Op.add)
+    ts(A("lq", 4, 8), A("iom", 0, 4), 4.0, Op.mult, q1col, Op.add)
     ts(gcol, kcol, hcol, Op.subtract, 4.0, Op.mult)
     ts(A("lq", 8, 12), A("onesb", 0, 4), g8col, Op.mult, gcol, Op.add)
     aff(rdcol, gcol, 64.0, 512.0)
-    aff(A("b64"), ind(A("b8"), A("lq", 8, 12)))
+    aff(A("b64"), ind(A("b8"), A("lq", 8, 12)), None, nsb)
 
     add("v", lambda q: q.transpose(ap(A("xt")), ap(A("x0"))), [A("xt")], [A("x0")], 64 * VEC)
     number(0, A("xt"), A("prev1"), A("offh"))
@@ -588,8 +679,8 @@ def rank_program(g, core, T, topo):
     mm(A("pz", 128, 256), A("rf"), A("xa"))
     aff(A("xb"), A("pz", 128, 256))
     sa = fused(lambda q: A("xb", 32 * q, 32 * q + 32),
-               lambda q: A("xw", 4096 + 32 * rank, 4128 + 32 * rank), "arra", 1.5, 3.0)
-    arrive([A("xw", 4096 + 32 * q, 4128 + 32 * q) for q in peers], "arra", (sa,))
+               lambda q: A("xw", 4096 + 32 * rank, 4128 + 32 * rank), "arra", FIRST, False)
+    arrive([A("xw", 4096 + 32 * q, 4128 + 32 * q) for q in peers], "arra", (sa,), False)
     banks = ["p0", "p1", "p2"]
 
     mm(A("p0", 0, 8), A("xw", 4096, ZC, p1=16), A("e0", p1=16))
@@ -601,7 +692,8 @@ def rank_program(g, core, T, topo):
     copy(ind(A("w1", 128), A("off", 0, 32)), A("d1", 16, 528))
     spread(lambda gr: A("pd", 32 * block(gr), 32 * block(gr) + 32), A("offh"))
     aff(A("nw", 0, 256), A("pd", 0, 256))
-    wrap8(A("pc", 0, 80), "c1", A("w1"), 640)
+    wrap8(A("pc", 0, 16), "c1", A("w1"), 128)
+    wrap8(A("pc", 16, 80), "c1", A("w1", 128), 512)
     scan(A("sw", 0, 80), A("sel"), A("pc", 0, 80), Op.add, Op.max)
     ts(A("l1u"), A("sw", 1, 80, 2), sbcol, Op.subtract, float(ZC), Op.add)
     ts(A("li"), A("sw", 1, 80, 2), sbcol, Op.subtract, float(ZC), Op.add)
@@ -614,11 +706,13 @@ def rank_program(g, core, T, topo):
     ts(nrc, A("pb", 100, 101), float(ROOT), Op.min, -1.0, Op.mult)
     ts(tcol, A("pb", 100, 101), float(ROOT), Op.is_gt, 2.0 * BIG, Op.mult)
     ts(bias2, tcol, A("pb", 100, 101), Op.subtract, float(BIG), Op.subtract)
-    aff(A("nr"), A("ios"), -1.0, nrc)
+    aff(nrc2, nrc, None, -256.0)
+    aff(A("nr", 0, 256), A("ios"), -1.0, nrc)
+    aff(A("nr", 256, 512), A("ios"), -1.0, nrc2)
 
     sb = fused(lambda q: A("gw", 32 * q, 32 * q + 32),
-               lambda q: A("gg", 32 * slot(q, rank), 32 * slot(q, rank) + 32), "arrb", 0.5)
-    arrive([A("gg")], "arrb", (sb,))
+               lambda q: A("gg", 32 * slot(q, rank), 32 * slot(q, rank) + 32), "arrb", 0.7, True)
+    arrive([A("gg")], "arrb", (sb,), True)
 
     for r in range(16):
         mm(A("pa", 64, 96), A("b2", 15 - r, 143 - r), A("gw", 128 + r, 640, 16), r == 0, r == 15)
@@ -635,9 +729,8 @@ def rank_program(g, core, T, topo):
     wrap8(A("pd", 400, 416), "c2", A("tm"), 128)
     wrap8(A("pd", 416, 432), "c5", A("tm"), 128)
     scan(A("sb"), A("sel", 0, 32), A("pd", 400, 432), Op.add, Op.max)
-    ts(A("tb"), A("sb", 1, 32, 2), sbcol, Op.subtract)
-    tt(A("pv", 0, 64), ind(A("tb"), A("lq", 0, 4)), A("b64"), Op.add)
-    aff(A("pv", 64, 128), ind(A("tb"), A("lq", 4, 8)), None, float(ROOT))
+    tt(A("pv", 0, 64), ind(A("sb"), A("lq", 0, 4)), A("b64"), Op.add)
+    aff(A("pv", 64, 128), ind(A("sb"), A("lq", 4, 8)), None, rsb)
     tt(A("pv", 128, 192), A("pv", 0, 64), A("pv", 64, 128), Op.min)
     ts(A("lvb"), A("pv", 128, 192), ROOT + 511.0, Op.min)
     tt(ind(A("w2"), A("off", 32, 64)), A("d2"), A("nr"), Op.max)
@@ -660,24 +753,24 @@ def rank_program(g, core, T, topo):
             c = TB + ROOT + 512 * (d + 1)
             load("s", A("t1", c, c + 512, 1, 16 * f, 16 * f + 16), ap(src), "lrt", 3.0, 0.0, r=[src])
         glue(8)
-    if NDMA:
-        mm(A("p2"), A("wo", 0, 128), gw)
-        aff(A("yt"), A("p2"))
+    for h in range((NDMA + 3) // 4):
+        mm(A(banks[2 - h]), A("wo", 512 * h, 512 * h + 128), gw)
+        aff(A("yt", 512 * h, 512 * h + 512), A(banks[2 - h]))
     for o in range(8):
         c = TB + 16 + ST * o
         if o < NDMA:
-            src = A("yt", 0, 512, 1, o, 128, 8)
-            for f in range(8):
-                add("s", lambda q, f=f, c=c, src=src: q.dma_start(ap(A("t1", c, c + 512, 1, 16 * f, 16 * f + 16)), ap(src)),
-                    [A("t1", c, c + 512, 1, 16 * f, 16 * f + 16)], [src], DMAC, "lt1", 16, True, 2.3)
-            glue(8)
-            store("s", T.y1[16 * o:16 * o + 16, :], src, "oy1")
+            src = A("yt", 512 * (o // 4), 512 * (o // 4) + 512, 1, o % 4, 128, 4)
+            for f in range(0, 128, 32):
+                add("s", lambda q, f=f, c=c, src=src: q.dma_start(ap(A("t1", c, c + 512, 1, f, f + 32)), ap(src)),
+                    [A("t1", c, c + 512, 1, f, f + 32)], [src], DMAC, "lt1", 16, True, 2.3)
+            glue(4)
+            store("s", T.y1[16 * o:16 * o + 16, :], src[:5] + (64, 4), "oy1")
             continue
-        mm(A(banks[o % 3]), A("wo", o, 1024, 8), gw)
+        mm(A(banks[o % 3]), wo(o), gw)
         aff(A("t1", c, c + 512), A(banks[o % 3]))
         store("s", T.y1[16 * o:16 * o + 16, :], A("t1", c, c + 512, 1, 16 * o, 16 * o + 16), "oy1")
     for o in range(8):
-        mm(A(("pz", "pb")[o // 4], 128 + 96 * (o % 4), 224 + 96 * (o % 4)), A("wo", o, 1024, 8), A("gg"))
+        mm(A(("pz", "pb")[o // 4], 128 + 96 * (o % 4), 224 + 96 * (o % 4)), wo(o), A("gg"))
         glue(1 + o % 4)
     for o in range(8):
         c = TB + 528 + ST * o
@@ -706,8 +799,10 @@ def rank_program(g, core, T, topo):
     for r in range(16):
         mm(A("pa", 128, 134), A("b2", 15 - r, 143 - r), A("gg", r, 96, 16), r == 0, r == 15)
     glue(16)
-    ts(A("nfg"), A("pa", 128, 134), 100.0, Op.is_le, float(DUM), Op.mult)
-    tt(A("n2h", 32, 38), A("nfg"), A("cc"), Op.add)
+    add("a", lambda q: q.activation(ap(A("nfg")), ap(A("pa", 128, 134)), Fn.Sign, bias=100.0625, scale=-1.0),
+        [A("nfg")], [A("pa", 128, 134)], 0.08)
+    for c in range(6):
+        aff(A("n2h", 32 + c, 33 + c), A("nfg", c, c + 1), DUM / 2.0, A("cc", c, c + 1))
     spread(lambda gr: A("pd", 38 * gr, 38 * gr + 38), A("n2h", 0, 38))
     aff(A("nw2", 1, 305), A("pd", 0, 304))
 
@@ -758,9 +853,13 @@ def rank_program(g, core, T, topo):
     g.wait_ge(T.sem.sent, total["sent"])
 
 
+MOVES = 130000
+HEAT = 0.6
 LATEX = False
-NDMA = 2
+MIX = 0.6
+NDMA = 4
 DMAC = 0.12
+FIRST = 1.3
 LVB = False
 RAW = 1
-CUTS = (0, 128, 256, 384, 512)
+CUTS = (0, 160, 320, 448, 512)

@@ -3,53 +3,65 @@ from concourse.mybir import AluOpType, ActivationFunctionType
 
 F32, BF, F16, I32, U16 = "float32", "bfloat16", "float16", "int32", "uint16"
 ZC = 4224
-ST = 608
-ROOT = 16 + 8 * ST
+ST = 640
+ROOT = 8 * ST
 TB = 1280
-DUM = 8256
+DUM = 8576
 BIG = 16384
+ZS = 176
+RS = 528
 
 SB = {
     "xw": (4240, BF), "xn": (544, BF), "x0": (32, BF), "xt": (32, BF), "d1": (544, I32), "idb": (64, I32),
-    "bdi": (8, I32), "bdg": (8, F32), "lx": (8, U16), "xa": (128, BF), "xb": (128, BF),
-    "eef": (128, F32), "e0": (8, BF), "th8": (8, F32), "nfb": (8, BF), "jn": (8, F32),
-    "w1": (13888, F32), "w2": (13760, F32), "gw": (640, BF), "gg": (96, BF),
-    "onesb": (144, BF), "onesf": (128, F32), "b2": (144, BF), "pi": (4, I32), "pk": (8, I32),
-    "col": (40, F32), "iog": (128, BF), "iom": (128, BF), "iob": (128, BF), "bo": (128, BF), "prev": (128, BF),
-    "prev1": (128, BF), "rf": (128, BF), "rfb": (128, BF),
-    "ident": (128, BF), "tri": (128, BF), "dc": (32, F32), "i16": (16, F32),
-    "yt": (1024, F32), "n2h": (40, F16), "offh": (32, F16), "io8": (12, I32), "io2": (16, I32),
-    "ee": (256, BF), "c1": (136, F32), "c4": (136, F32), "c2": (136, BF), "c5": (136, BF), "sel": (80, F32),
-    "obi": (12, I32), "obt": (12, F32), "m8": (40, F32), "lj": (16, U16), "wc": (128, F32), "wz": (128, F32),
-    "l2r": (32, F32), "l2t": (32, F32), "io128": (128, BF),
-    "r3": (128, F32), "wo": (1024, BF), "rt": (128, BF), "pm": (256, F32), "urow": (128, F32),
-    "ios": (256, BF), "nr": (512, F32), "jb": (8, F32), "cc": (6, F32), "nw": (272, F32), "nw2": (344, F32),
-    "nf": (64, BF), "sc": (80, BF), "nd": (64, F16), "off": (64, U16), "b8": (32, F32), "b64": (64, F32),
-    "nfg": (6, F32), "lq": (12, U16), "tb": (16, F32), "pv": (192, F32),
-    "lvb": (64, U16), "sw": (192, F32), "sb": (32, F32), "l1u": (40, U16), "l2u": (32, U16), "li": (40, I32),
+    "bdi": (8, I32), "bdg": (8, F32), "lx": (8, U16), "xa": (128, BF), "xb": (128, BF), "gs": (128, BF),
+    "eef": (128, F32), "e0": (8, BF), "th8": (8, F32), "nfb": (8, BF),
+    "w1": (14208, F32), "gw": (512, BF), "gg": (128, BF),
+    "onesb": (144, BF), "onesf": (128, F32), "b2": (136, BF), "pi": (4, I32), "pk": (8, I32),
+    "col": (48, F32), "iog": (144, BF), "iom": (128, BF), "iob": (128, BF), "bo": (136, BF), "trb": (128, BF),
+    "prev": (128, BF), "io128": (136, BF), "prev1": (128, BF), "rf": (128, BF), "rfb": (128, BF),
+    "idw": (136, BF), "tri": (128, BF), "dc": (32, F32), "i16": (16, F32),
+    "yt": (1024, F32), "n2": (128, F16), "nt": (80, F16), "offh": (32, F16), "io8": (12, I32), "io2": (16, I32),
+    "ee": (256, BF), "c1": (136, F32), "sel": (128, F32), "ioo": (128, BF),
+    "obi": (12, I32), "obt": (12, F32), "m8": (40, F32), "lj": (16, U16),
+    "fw": (432, F16), "c3": (144, BF), "rr": (32, F32), "wf": (256, F32), "pf": (220, F32), "pm": (256, F32), "l3": (8, U16), "kf": (496, F16),
+    "lf": (96, F32), "n2g": (80, F32), "uu": (256, F16), "dw": (128, BF),
+    "l2r": (32, F32), "l2t": (32, F32), "iou": (256, BF), "pl": (32, F32),
+    "st": (256, BF), "cm": (256, BF), "la": (256, BF),
+    "xr": (52, F16), "ls": (32, U16), "tg": (512, F16), "tmb": (128, F16), "wo": (1024, BF),
+    "jn": (8, F32), "ci": (16, F32), "nw": (272, F32), "nw2": (360, F32),
+    "nf": (32, BF), "sc": (104, BF), "nd": (32, F16), "fl": (64, BF), "nd2": (64, F16), "back": (128, BF),
+    "off": (32, U16), "b8": (32, F32), "nfg": (16, F32), "lq": (8, U16), "lp": (4, U16), "pv": (192, F32),
+    "lvb": (64, U16), "sw": (336, F32), "sb": (32, F32), "l1u": (40, U16), "l2u": (32, U16), "li": (40, I32),
     "lcr": (80, I32), "lcu": (80, U16), "li2": (32, I32), "lcr2": (64, I32), "lcu2": (64, U16),
-    "mk": (640, BF), "tm": (640, F16), "mk2": (512, BF), "tm2": (512, F16),
-    "l2s": (32, F32), "lf": (96, F32), "lfu": (96, U16), "d2": (512, F32),
-    "t1": (TB + ROOT + 2048, F32), "v": (512, F32), "vb": (768, F32), "vg": (768, F32), "vc": (768, F32), "gd": (1536, F32),
-    "yo": (512, F32),
+    "mk": (640, BF), "tm": (520, F32), "mk2": (512, BF), "tm2": (512, F16), "l2s": (32, F32), "lfu": (96, U16),
+    "t1": (TB + ROOT + 4 * RS, F32), "v": (512, F32), "vb": (768, F32), "vg": (768, F32), "vc": (768, F32),
+    "gd": (1536, F32), "yo": (512, F32),
 }
+PART = {"wc": ("wf", 0, 128), "wz": ("wf", 128, 128), "r3": ("pf", 0, 128),
+        "b64": ("pf", 128, 64), "lqf": ("pf", 192, 8), "late": ("pf", 200, 4),
+        "cc": ("pf", 204, 16), "ew": ("kf", 0, 144), "r80": ("kf", 144, 80), "c2": ("kf", 224, 136),
+        "c5": ("kf", 360, 136)}
+SHARED = ["fw", "wf", "pf", "kf"]
 SCRATCH = {k: ("sbuf", [128, v[0]], v[1]) for k, v in SB.items()}
 PSUM = ["pa", "pb", "pc", "pd", "p0", "p1", "p2", "pz"]
 for _p in PSUM:
     SCRATCH[_p] = ("psum", [128, 512], F32)
-SEMAPHORES = ["cv", "ca", "ct", "cg", "lx0", "lbd", "lnb", "lxn", "lx", "lrt", "lt1", "oy1", "oy2", "arra", "arrb", "arrc0",
-              "arrc1", "arrc2", "sent"]
+SEMAPHORES = ["cv", "ca", "ct", "cg", "lx0", "lbd", "lnb", "lxn", "lx", "lrt", "lt1", "oy1",
+              "oy2", "arra", "arrz", "arrk0",
+              "arrk1", "arrk2", "arrk3", "arrb", "arrc0", "arrc1", "arrc2", "sent"]
 ENG_SEM = {"v": "cv", "a": "ca", "t": "ct", "g": "cg"}
-GAP = 0.11
-VEC = 0.00104
-PE = 0.00052
-TRIES = 1000
+GAP = 0.24
+VEC = 0.0009
+PE = 0.00045
 SLACK = 0.2
 SEED = 5
 PLANS = {}
 
 
 def A(name, c0=0, c1=None, cs=1, p0=0, p1=128, ps=1):
+    if name in PART:
+        home, at, n = PART[name]
+        return (home, at + c0, at + (n if c1 is None else c1), cs, p0, p1, ps)
     if c1 is None:
         c1 = SB[name][0] if name in SB else 512
     return (name, c0, c1, cs, p0, p1, ps)
@@ -58,7 +70,11 @@ def A(name, c0=0, c1=None, cs=1, p0=0, p1=128, ps=1):
 def overlap(a, b):
     if a[0] != b[0] or a[1] >= b[2] or b[1] >= a[2] or a[4] >= b[5] or b[4] >= a[5]:
         return False
-    return not (a[3] == b[3] and (a[1] - b[1]) % a[3])
+    if a[3] == b[3]:
+        return not (a[1] - b[1]) % a[3]
+    if a[3] == 1:
+        a, b = b, a
+    return b[3] > 1 or any(b[1] <= c < b[2] for c in range(a[1], a[2], a[3]))
 
 
 def conflict(o, p):
@@ -75,27 +91,30 @@ def unfenced(o, p):
     return p["e"] == "t" and o["e"] == "t" and p["tile"] == o["tile"]
 
 
-def arrange(ops):
+def arrange(ops, rank):
     calls, ops, home = ops, [], []
     for o in calls:
         if o["glue"]:
             p = ops[-1]
-            c = p["c"] + o["c"] + (GAP if o["e"] == "t" and o["tile"] != p["last"] else 0.0)
-            p.update(w=p["w"] + o["w"], r=p["r"] + o["r"], names=p["names"] | o["names"], c=c, last=o["tile"],
-                     banks=p["banks"] | o["banks"], alt=[(o["e"], None, c)],
+            c = GAP if o["e"] == "t" and o["tile"] != p["last"] else 0.0
+            p.update(w=p["w"] + o["w"], r=p["r"] + o["r"], names=p["names"] | o["names"], last=o["tile"],
+                     banks=p["banks"] | o["banks"],
+                     alt=[(x[0], None, x[2] + y[2] + c) for x, y in zip(p["alt"], o["alt"])],
                      tile=p["tile"] if p["tile"] == o["tile"] else len(ops))
         else:
             ops.append(dict(o, last=o["tile"], after=[home[j] for j in o["after"]]))
         home.append(len(ops) - 1)
     n = len(ops)
-    if n not in PLANS:
+    rank = rank if SHARE else 0
+    if rank not in PLANS:
         pred = [[j for j in range(i) if conflict(ops[i], ops[j]) or j in ops[i]["after"]] for i in range(n)]
         above, before, behind = [0] * n, [], [[] for _ in range(n)]
         for i in range(n):
             keep = []
             for j in reversed(pred[i]):
                 if not above[i] >> j & 1:
-                    keep.append((j, 0.0 if unfenced(ops[i], ops[j]) else GAP))
+                    queued = ops[i]["e"] == ops[j]["e"] == "g" and j in ops[i]["after"]
+                    keep.append((j, -ops[j]["lat"] if queued else 0.0 if unfenced(ops[i], ops[j]) else GAP))
                     behind[j].append((i, keep[-1][1]))
                 above[i] |= above[j] | 1 << j
             before.append(keep)
@@ -104,6 +123,8 @@ def arrange(ops):
         alt = [[(e, c) for e, f, c in o["alt"]] for o in ops]
         lat = [o["lat"] for o in ops]
         slow = [o["slow"] for o in ops]
+        due = [(i, o["due"], 1.0) for i, o in enumerate(ops) if "due" in o]
+        due += [(i, AIM[o["w"][0][:2]], PULL) for i, o in enumerate(ops) if o["w"] and o["w"][0][:2] in AIM]
 
         def sweep(key, first, then, back, bias):
             lo, hi = {e: [] for e in "vatgs-"}, {e: [] for e in "vatgs-"}
@@ -158,7 +179,8 @@ def arrange(ops):
                 late[i] = t + lat[i]
                 if e != "-":
                     free[e] = t
-            one = (max(end) + MIX * max(late) + 0.02 * sum(end) / n, start, end, pick, bias, max(late))
+            one = (max(end) + MIX * max(late) + 0.02 * sum(end) / n + sum(w * max(0.0, start[i] - t) for i, t, w in due),
+                   start, end, pick, bias, max(late))
             if again:
                 two = plan(sweep(end, behind, before, True, bias)[1], bias, False)
                 one = two if two[0] < one[0] else one
@@ -172,9 +194,25 @@ def arrange(ops):
 
         level = [0.0] * n
         for i in range(n - 1, -1, -1):
-            level[i] = min(c for e, c in alt[i]) + lat[i] + max([level[k] + gap for k, gap in behind[i]] + [0.0])
+            level[i] = min(c for e, c in alt[i]) + lat[i] + max(
+                [level[k] + gap for k, gap in behind[i]] + [15.0 * ("due" in ops[i])])
         now = best = plan(level, [0.0] * n, True)
-        for trial in range(TRIES):
+        tries, moves, heat = TRIES, MOVES, HEAT
+        if PLANS:
+            done = next(iter(PLANS.values()))
+            same = [(done[1][i], done[2][i]) for i, o in enumerate(done[3]) if not o.get("own")]
+            key, bias = [0.0] * n, [0.0] * n
+            for i in range(n - 1, -1, -1):
+                if ops[i].get("own"):
+                    key[i] = max([key[k] + gap for k, gap in behind[i]] + [-KSEND[rank]]) + alt[i][0][1]
+                else:
+                    t, e = same.pop()
+                    key[i], bias[i] = -t, 1.5 if e == "a" else -1.5
+            for i in range(n - 1, -1, -1):
+                key[i] = max([key[i]] + [key[k] + 1e-3 for k, gap in behind[i]])
+            now = best = plan(key, bias, False)
+            tries, moves, heat = 0, MOVES2, HEAT2
+        for trial in range(tries):
             start, end, pick, bias = now[1:5]
             key = [-x for x in start]
             prior, last = {}, {}
@@ -183,8 +221,8 @@ def arrange(ops):
             chain = []
             i = max(range(n), key=lambda x: end[x])
             while i is not None and start[i] > 0.2:
-                t, j = max([(end[j] + gap, j) for j, gap in before[i]] + [(0.0, None)])
-                if t + 0.005 < start[i]:
+                t, j = max([(end[j] + gap, j) for j, gap in before[i]] + [(0.0, -1)])
+                if t + 0.005 < start[i] or j < 0:
                     j = prior[i]
                     if j is not None:
                         chain.append((i, j))
@@ -210,42 +248,74 @@ def arrange(ops):
                     for k in up[i if rand() < 0.5 else j]:
                         key[k] += 1.5 * x
             new = plan(key, bias, trial % 4 == 0)
-            if new[0] <= now[0] + SLACK * rand() ** 2 * (1 - trial / TRIES):
+            if new[0] <= now[0] + SLACK * rand() ** 2 * (1 - trial / tries):
                 now = new
             if new[0] < best[0]:
                 best = new
         cost = [dict(a) for a in alt]
 
-        def run(order, pick, factor):
-            free, last = {}, {}
-            start, end, why = [0.0] * n, [0.0] * n, [None] * n
-            for i in order:
+        slower = [{e: c * slow[i] for e, c in alt[i]} for i in range(n)]
+        rest = [0.0] * n
+        for i in range(n - 1, -1, -1):
+            rest[i] = min(cost[i].values()) + lat[i] + max([rest[k] + gap for k, gap in behind[i]] + [0.0])
+
+        def run(order, pick, cost, a, old, bar):
+            start, end, why = old[0][:], old[1][:], old[2][:]
+            free, last = dict.fromkeys("vatgs-", 0.0), dict.fromkeys("vatgs-")
+            k, left = a, set("vatgs")
+            while k and left:
+                k -= 1
+                i = order[k]
+                if pick[i] in left:
+                    left.discard(pick[i])
+                    free[pick[i]], last[pick[i]] = end[i] - lat[i], i
+            for i in order[a:]:
                 e = pick[i]
-                t, w = free.get(e, 0.0), last.get(e)
+                t, w = free[e], last[e]
                 for j, gap in before[i]:
                     if end[j] + gap > t:
                         t, w = end[j] + gap, j
+                if t + rest[i] > bar:
+                    return None
                 start[i], why[i] = t, w
-                t += cost[i][e] * factor[i]
+                t += cost[i][e]
                 end[i] = t + lat[i]
                 if e != "-":
                     free[e], last[e] = t, i
             return start, end, why
 
-        def judge(order, pick):
-            a, b = run(order, pick, even), run(order, pick, slow)
-            return max(a[1]) + MIX * max(b[1]) + 0.02 * sum(a[1]) / n, order, pick, a, b
+        def judge(order, pick, at, old, bar):
+            a = run(order, pick, cost, at, old[0], bar - 0.2 - MIX * (old[2] - 0.3))
+            if not a:
+                return None
+            u = max(a[1]) + 0.02 * sum(a[1]) / n + sum(w * max(0.0, a[0][i] - t) for i, t, w in due)
+            b = run(order, pick, slower, at, old[1], (bar - u) / MIX)
+            return b and (u + MIX * max(b[1]), order, pick, (a, b, max(b[1])))
 
-        even = [1.0] * n
-        now = best = judge(sorted(range(n), key=lambda x: (best[1][x], x)), best[3])
-        for trial in range(MOVES):
+        def waits(times, i):
+            chain = []
+            while times[2][i] is not None:
+                if not above[i] >> times[2][i] & 1:
+                    chain.append((i, times[2][i]))
+                i = times[2][i]
+            return chain
+
+        none = ([0.0] * n, [0.0] * n, [None] * n)
+        now = best = judge(sorted(range(n), key=lambda x: (best[1][x], x)), best[3], 0, (none, none, 0.0), 99.0)
+        chains = None
+        for trial in range(moves):
+            if trial % PACK == 0:
+                bias = [(1.5 if e == "a" else -1.5 if e == "v" else 0.0) * (rand() < 0.9) for e in now[2]]
+                one = plan([-x for x in now[3][0][0]], bias, trial % (2 * PACK) == 0)
+                new = judge(sorted(range(n), key=lambda x: (one[1][x], x)), one[3], 0, (none, none, 0.0), 99.0)
+                if new[0] <= now[0] + 0.1 * heat * (1 - trial / moves):
+                    now, chains = new, None
+                    best = new if new[0] < best[0] else best
             order, pick = now[1:3]
-            start, end, why = now[3 + trial % 2]
-            i, chain = max(range(n), key=lambda x: end[x]), []
-            while why[i] is not None:
-                if not above[i] >> why[i] & 1:
-                    chain.append((i, why[i]))
-                i = why[i]
+            if not chains:
+                chains = [waits(x, x[1].index(max(x[1]))) for x in now[3][:2]]
+                chains += [waits(now[3][0], i) for i, t, w in due if now[3][0][0][i] > t]
+            chain = chains[trial % len(chains)]
             u = rand()
             if u < 0.15 or not chain:
                 a = int(rand(n - 12))
@@ -260,6 +330,7 @@ def arrange(ops):
                     continue
                 pick = list(pick)
                 pick[x] = [e for e, c in alt[x] if e != pick[x]][int(rand(len(alt[x]) - 1))]
+                a = order.index(x)
             else:
                 a, b = order.index(j), order.index(i)
                 far = int(rand() ** 3 * 40)
@@ -267,20 +338,23 @@ def arrange(ops):
                     a = max(0, a - far)
                     part = order[a:b + 1]
                     mask = above[i] | 1 << i
-                    order = order[:a] + [x for x in part if mask >> x & 1] + [x for x in part if not mask >> x & 1] + order[b + 1:]
+                    order = (order[:a] + [x for x in part if mask >> x & 1]
+                             + [x for x in part if not mask >> x & 1] + order[b + 1:])
                 else:
                     b = min(n - 1, b + far)
                     part = order[a:b + 1]
                     order = (order[:a] + [x for x in part if x != j and not above[x] >> j & 1]
                              + [x for x in part if x == j or above[x] >> j & 1] + order[b + 1:])
-            new = judge(order, pick)
-            if new[0] <= now[0] + HEAT * rand() ** 3 * (1 - trial / MOVES):
-                now = (new[0], sorted(order, key=lambda x: new[3][0][x])) + new[2:]
+            bar = now[0] + heat * rand() ** 3 * (1 - trial / moves)
+            new = judge(order, pick, a, now[3], bar)
+            if new and new[0] <= bar:
+                now, chains = (new[0], sorted(order, key=lambda x: new[3][0][0][x])) + new[2:], None
                 if new[0] < best[0]:
                     best = new
         place = {x: k for k, x in enumerate(best[1])}
-        PLANS[n] = ((max(best[3][1]), max(best[4][1])), [best[3][0][x] + 1e-6 * place[x] for x in range(n)], best[2], ops)
-    score, start, pick = PLANS[n][:3]
+        PLANS[rank] = ((max(best[3][0][1]), best[3][2]), [best[3][0][0][x] + 1e-6 * place[x] for x in range(n)],
+                       best[2], ops)
+    score, start, pick = PLANS[rank][:3]
     for o, i in zip(calls, home):
         o["e"], o["f"] = [x[:2] for x in o["alt"] if x[0] == pick[i]][0]
     return [calls[i] for i in sorted(range(len(calls)), key=lambda x: (start[home[x]], x))]
@@ -357,7 +431,7 @@ def rank_program(g, core, T, topo):
     def width(r):
         return len(range(r[1], r[2], r[3]))
 
-    def add(e, f, w, r, c, sem=None, inc=0, dma=False, lat=0.0, pri=0.0, after=(), alt=None, tile=None):
+    def add(e, f, w, r, c, sem=None, inc=0, dma=False, lat=0.0, after=(), alt=None, tile=None):
         ww, rr = [], []
         for x in r:
             if isinstance(x, tuple):
@@ -370,10 +444,10 @@ def rank_program(g, core, T, topo):
                 ww.append(x)
         names = set(x[0] for x in ww + rr)
         ops.append({"e": e, "f": f, "w": ww, "r": rr, "sem": sem, "inc": inc, "dma": dma, "c": c, "lat": lat,
-                    "pri": pri, "after": after, "names": names, "banks": names & set(PSUM), "tile": tile,
+                    "after": after, "names": names, "banks": names & set(PSUM), "tile": tile,
                     "alt": alt or [(e, f, c)], "glue": False,
-                    "slow": 1.0 if sem else 1.7 if len(rr) > len(r) and w[0][0] == "ind" else
-                    1.5 if any(isinstance(x, tuple) and x[0] == "ind" for x in r) else 1.2})
+                    "slow": 1.0 if sem else 1.85 if len(rr) > len(r) and w[0][0] == "ind" else
+                    1.65 if any(isinstance(x, tuple) and x[0] == "ind" for x in r) else 1.3})
         return len(ops) - 1
 
     def glue(n):
@@ -399,8 +473,8 @@ def rank_program(g, core, T, topo):
     def ind(win, off):
         return ("ind", win, off)
 
-    def memset(o, c, pri=0.0):
-        add("v", lambda q: q.memset(ap(o), c), [o], [], half(o, o), pri=pri)
+    def memset(o, c):
+        add("v", lambda q: q.memset(ap(o), c), [o], [], half(o, o))
 
     def copy(o, i):
         add("v", lambda q: q.tensor_copy(ap(o), ap(i)), [o], [i], half(o, i))
@@ -418,7 +492,7 @@ def rank_program(g, core, T, topo):
     def scan(o, a, b, op0, op1, first=0.0):
         add("v", lambda q: q.tensor_tensor_scan(ap(o), ap(a), ap(b), sc(first), op0, op1), [o], [a, b, first], half(o, a))
 
-    def aff(o, i, scale=None, bias=None, e="*"):
+    def aff(o, i, scale=None, bias=None):
         kw = {}
         if bias is not None:
             kw["bias"] = bias
@@ -436,13 +510,14 @@ def rank_program(g, core, T, topo):
             if bias is None:
                 return q.tensor_scalar(ap(o), ap(i), sc(scale), None, Op.mult)
             return q.tensor_scalar(ap(o), ap(i), sc(scale), sc(bias), Op.mult, Op.add)
-        alt = [x for x in (("a", on_a, cost(o, i) + 0.015), ("v", on_v, half(o, i))) if e in ("*", x[0])]
-        add(e, alt[0][1], [o], [i, scale, bias], alt[0][2], alt=alt)
+        alt = [("a", on_a, cost(o, i) + 0.015), ("v", on_v, half(o, i))]
+        add("*", on_a, [o], [i, scale, bias], alt[0][2], alt=alt)
 
-    def fill(o, c, src=None):
-        scale = 0.0 if src else float(c)
-        src = src or A("onesb", 0, width(o), 1, o[4], o[5])
-        alt = [("a", lambda q: q.activation(ap(o), ap(src), Fn.Identity, scale=scale), cost(o, o) + 0.015),
+    def fill(o, c):
+        src = A("onesb", 0, width(o), 1, o[4], o[5])
+        if SB[o[0]][1] == F16:
+            return aff(o, src, float(c))
+        alt = [("a", lambda q: q.activation(ap(o), ap(src), Fn.Identity, scale=float(c)), cost(o, o) + 0.015),
                ("v", lambda q: q.memset(ap(o), c), half(o, o)),
                ("g", lambda q: q.iota(ap(o), [[0, width(o)]], int(c), 0, allow_small_or_imprecise_dtypes=True),
                 0.16 + width(o) * 2 * VEC)]
@@ -452,16 +527,18 @@ def rank_program(g, core, T, topo):
         add("t", lambda q: q.matmul(ap(o), ap(l), ap(r), start, stop), [o], [l, r],
             max(64, width(r)) * PE * (4 if SB[l[0]][1] == F32 else 1), tile=(l[4], l[5]))
 
-    def iota(o, pat, base, cm, pri=0.0):
+    def iota(o, pat, base, cm):
         kw = {} if SB[o[0]][1] == I32 else {"allow_small_or_imprecise_dtypes": True}
-        add("g", lambda q: q.iota(ap(o), pat, base, cm, **kw), [o], [], 0.16 + width(o) * 2 * VEC, pri=pri)
+        add("g", lambda q: q.iota(ap(o), pat, base, cm, **kw), [o], [], 0.16 + width(o) * 2 * VEC)
 
     def asel(o, i, pat, cmp, base, cm):
         add("g", lambda q: q.affine_select(ap(o), ap(i), pat, cmp, 0.0, base, cm), [o], [i],
             0.21 + width(o) * 2 * VEC)
 
-    def load(e, o, src, sem, lat, pri, after=(), r=()):
-        return add(e, lambda q: q.dma_start(ap(o), src), [o], list(r), 0.06, sem, 16, True, lat, pri, after)
+    def load(e, o, src, sem, lat, r=(), c=0.06):
+        def f(q):
+            return q.dma_start(ap(o), src)
+        return add(e[0], f, [o], list(r), c, sem, 16, True, lat, alt=[(x, f, c) for x in e])
 
     def store(e, dst, i, sem):
         add(e, lambda q: q.dma_start(dst, ap(i)), [], [i], 0.06, sem, 16, True, 2.2)
@@ -469,57 +546,34 @@ def rank_program(g, core, T, topo):
     def slot(at, q):
         return q if q < at else q - 1
 
-    def share(at, q, wide):
-        en = topo.engines(cores[at], cores[q])
-        w, j = len(en) // 4, slot(at, q)
-        return en[0 if wide and not j else (j + 1) * w:(j + 2) * w]
+    def share(at, q, w):
+        en = topo.engines(cores[at], cores[q])[::STEP]
+        return en[:w] if 3 * w > len(en) else en[slot(at, q):3 * w:3]
 
-    def fused(src_of, dst_of, sem, c, wide):
-        tr = []
-        for q in peers:
-            rid, pid = topo.addr(cores[q])[:2]
-            tr.append(RemoteDMATransfer(dst_ids=[DstId(rid=rid, pnc=pid)],
-                                        dma_engine_mask=sum(1 << e for e in share(rank, q, wide)),
-                                        remote_sem=T.sem[sem], src=ap(src_of(q)), dst=ap(dst_of(q))))
-        return add("g", lambda x: x.remote_dma_fused(tr, local_sem=T.sem.sent), [], [src_of(q) for q in peers], c,
-                   "sent", sum(len(share(rank, q, wide)) for q in peers), lat=2.3)
+    def transfer(src, to, sem, en):
+        ids = [DstId(rid=topo.addr(cores[q])[0], pnc=topo.addr(cores[q])[1]) for q, d in to]
+        return RemoteDMATransfer(dst_ids=ids, dma_engine_mask=sum(1 << e for e in en), remote_sem=T.sem[sem],
+                                 srcs=[ap(src)], dsts=[ap(d) for q, d in to])
 
-    def arrive(regions, sem, after, wide):
-        add("-", None, regions, [], 0.0, sem, sum(len(share(q, rank, wide)) for q in peers), after=after)
+    def fused(trs, c, sem="sent"):
+        tr = [transfer(*t) for t in trs]
+        return add("g", lambda x: x.remote_dma_fused(tr, local_sem=T.sem[sem]), [], [t[0] for t in trs], c,
+                   sem, sum(len(t[3]) for t in trs), lat=2.3)
 
-    def wrap8(o, c, src, n):
+    def wrap8(o, c, src, n, start=True):
         for b in range(8):
-            mm(o, A(c, 7 - b, 135 - b), A(src[0], src[1] + b, src[1] + n, 8), b == 0, b == 7)
+            mm(o, A(c, 7 - b, 135 - b), A(src[0], src[1] + b, src[1] + n, 8), start and b == 0, b == 7)
         glue(8)
 
-    def spread(o_of, src):
-        for gr in range(8):
-            a, h = gr // 2, gr % 2
-            mm(o_of(gr), A("ee", 128 * h, 128 * h + 128, 1, 32 * a, 32 * a + 32),
-               A(src[0], src[1], src[2], 1, 32 * a, 32 * a + 32))
-            glue(1 + h)
+    def wrap4(o, c, c0, src, start):
+        for b in range(8):
+            mm(o, A(c, c0 + 14 - 2 * b, c0 + 142 - 2 * b), A(src, b, 256, 8), start and b == 0, not start and b == 7)
+            glue(1 + b % 4)
 
-    (rcol, kcol, hcol, g8col, r8col, r4col, h0col, ccol, b1col, sbcol, k6col, zc0, zc, nrc, tcol, bias2, h35, bcol,
-     dcol, lxcol, ecol, q0col, q1col, k6f, rtcol, rdcol, pcol, gcol, onec, rhalf, nrc2, rsb, nsb) = [
-        A("col", i, i + 1) for i in range(33)]
-
-    def number(lv, src, prev, second):
-        c = 32 * lv
-        nf, nd = A("nf", c, c + 32), A("nd", c, c + 32)
-        s0 = 40 * lv
-        ts(nf, src, 100.0 * lv, Op.is_le)
-        scan(A("sc", s0 + 1, s0 + 33), A("onesb", 0, 32), nf, Op.add, Op.subtract)
-        tt(nd, nf, A("dc"), Op.mult)
-        p1, pc = A("pb", 64 * lv, 64 * lv + 32), A("pb", 64 * lv + 32, 64 * lv + 33)
-        mm(p1, A("tri"), nf, True, False)
-        mm(p1, A("prev"), nf, False, False)
-        glue(2)
-        mm(p1, A("ident"), nd, False, False)
-        mm(p1, A("bo"), A("sc", s0, s0 + 32), False, True)
-        mm(pc, prev, A("sc", s0 + 32, s0 + 33))
-        glue(2)
-        ts(A("off", c, c + 32), p1, pc, Op.add, rcol, Op.add)
-        ts(second, p1, pc, Op.add, rcol, Op.add)
+    def wrap16(o, src, start):
+        for b in range(16):
+            mm(o, A("c3", 15 - b, 143 - b), A(src, b, 512, 16), start and b == 0, b == 15)
+        glue(16)
 
     def digits(li, cr, cu, n):
         ts(A(cr, n, 2 * n), A(li), 15, Op.bitwise_and)
@@ -532,66 +586,73 @@ def rank_program(g, core, T, topo):
     def block(gr):
         return 4 * (gr % 2) + gr // 2
 
-    iota(A("pi", 0, 1), [[0, 1]], 0, 1, 200.0)
-    iota(A("idb"), [[32, 2], [1, 32]], 0, 32, 190.0)
+    (rcol, kcol, hcol, g8col, acol, jcol, h0col, ccol, b1col, sbcol, k6col, zc0, zc, r8col, h35, bcol,
+     dcol, lxcol, ecol, q0col, q1col, k6f, pcol, gcol, onec, rhalf, nsb, sbz, pw, k67, hp,
+     xt, x1, x2, x3, d32, d33, a0, wcol, r1col, w0, j0, j1) = [A("col", i, i + 1) for i in range(43)]
+    rtcol, rdcol, rsb, zsb = [A("late", i, i + 1) for i in range(4)]
+    m63, hneg = A("col", 44, 45), A("col", 43, 44)
+    ident, shift = A("idw", 1, 129), A("idw", 0, 128)
+
+    iota(A("pi", 0, 1), [[0, 1]], 0, 1)
+    iota(A("idb"), [[32, 2], [1, 32]], 0, 32)
     for h in range(2):
-        load("sa"[h], A("x0", 16 * h, 16 * h + 16), T.x[0, 2048 * h:2048 * h + 2048], "lx0", 2.0, 90.0)
-    load("a", A("bdi", p1=16), T.bd[:, :], "lbd", 1.9, 95.0)
+        load("sa", A("x0", 16 * h, 16 * h + 16), T.x[0, 2048 * h:2048 * h + 2048], "lx0", 2.0)
+    load("sa", A("bdi", p1=16), T.bd[:, :], "lbd", 1.9)
     for k in range(8):
         c = 512 * block(k)
-        load("sa"[k % 2], A("xn", 16, 528, 1, 16 * k, 16 * k + 16), T.x[:, c:c + 512], "lxn", 2.2, 80.0)
+        load("sa", A("xn", 16, 528, 1, 16 * k, 16 * k + 16), T.x[:, c:c + 512], "lxn", 2.2)
     for k in range(8):
         c = 512 * block(k)
-        last = load("sa"[k % 2], A("d1", 16, 528, 1, 16 * k, 16 * k + 12, 2), T.nb[:, c:c + 512], "lnb", 2.2, 70.0)
+        load("sa", A("d1", 16, 528, 1, 16 * k, 16 * k + 12, 2), T.nb[:, c:c + 512], "lnb", 2.2)
     for h in range(2):
-        load("s", A("d1", 16, 528, 1, 12 + 2 * h, 128, 16), ap(A("idb", 32 * h, 32 * h + 32)), "lnb", 2.0, 70.0,
-             r=[A("idb")])
-        load("sa"[h], A("d1", 16, 528, 1, 64 * h + 1, 64 * h + 64, 2), T.nb[0:4, :], "lnb", 2.2, 70.0)
-    for k in range(8):
-        load("s", A("xw", 0, 4096, 1, 16 * k, 16 * k + 16), T.x[:, :], "lx", 4.0, 0.0, (last,) if LATEX else ())
+        load("s", A("d1", 16, 528, 1, 12 + 2 * h, 128, 16), ap(A("idb", 32 * h, 32 * h + 32)), "lnb", 2.0, [A("idb")])
+        load("sa", A("d1", 16, 528, 1, 64 * h + 1, 64 * h + 64, 2), T.nb[0:4, :], "lnb", 2.2)
+    for k in range(7):
+        load("s", A("xw", 0, 4096, 1, 16 * k, 16 * k + 16), T.x[:, :], "lx", LX)
 
     memset(A("onesb"), 1.0)
     for c in (0, 528):
         memset(A("d1", c, c + 16), 0)
         fill(A("xn", c, c + 16), 0.0)
     iota(A("iom"), [[0, 8], [1, 16]], 0, 0)
-    iota(A("iog"), [[1, 8], [0, 16]], 0, 0)
-    iota(A("iob"), [[1, 4], [4, 2], [0, 16]], 0, 0, 20.0)
+    iota(A("iou"), [[2, 256]], -256, 0)
+    iota(A("iog"), [[1, 9], [0, 16]], 0, 0)
+    iota(A("iob"), [[1, 4], [4, 2], [0, 16]], 0, 0)
     iota(A("dc"), [[128, 32]], DUM, 8)
     for c in range(128, 640, 128):
         fill(A("w1", c, c + 128), 0.0)
-    fill(A("w2", 0, 512), 0.0, A("xn", 16, 528))
-    fill(A("sc"), 0.0)
+    fill(A("sc", 0, 1), 0.0)
     fill(A("sel"), -65536.0)
-    fill(A("xw", ZC, 4240), 0.0)
+    fill(A("xw", ZC, 4232), 0.0)
     fill(A("xw", 4096 + 32 * rank, 4128 + 32 * rank), 0.0)
-    fill(A("onesf"), 1.0)
-    for c in ("c1", "c2", "c4", "c5", "b2"):
+    for c in ("c1", "b2"):
         fill(A(c), 0.0)
+    fill(A("gg", 96, 128), 0.0)
+    fill(A("tm", 512, 520), DUM / 16.0)
     fill(A("nw", 264, 272), 8000.0)
-    fill(A("t1", TB, TB + 16), 0.0)
-    fill(A("nw2", 0, 1), float(DUM))
-    fill(A("nw2", 305, 344), float(DUM))
+    fill(A("t1", TB + ROOT + 512, TB + ROOT + 4 * RS, RS), 0.0)
+    fill(A("nw2", 320, 360), float(DUM))
     ts(A("pk", 0, 1), A("pi", 0, 1), 15, Op.bitwise_and)
     ts(A("pk", 1, 2), A("pi", 0, 1), 4, Op.logical_shift_right)
     ts(A("pk", 2, 3), A("pi", 0, 1), 4, Op.logical_shift_right, 1, Op.bitwise_and)
     ts(A("pk", 3, 4), A("pi", 0, 1), 7, Op.bitwise_and)
-    ts(A("pk", 4, 5), A("pi", 0, 1), 3, Op.logical_shift_right, 1, Op.bitwise_and)
-    copy(A("col", 0, 5), A("pk", 0, 5))
-    ts(A("bo"), A("iog"), kcol, Op.is_equal)
-    ts(A("prev"), A("iog"), kcol, Op.is_gt)
+    ts(A("pk", 4, 5), A("pi", 0, 1), 6, Op.logical_shift_right)
+    ts(A("pk", 5, 6), A("pi", 0, 1), 63, Op.bitwise_and)
+    copy(A("col", 0, 6), A("pk", 0, 6))
+    ts(A("bo"), A("iog", 0, 136), kcol, Op.is_equal)
+    ts(A("prev"), A("iog", 0, 128), kcol, Op.is_gt)
+    scan(A("io128"), A("onesb", 0, 136), A("onesb", 0, 136), Op.add, Op.mult, -2.0)
+    copy(pcol, A("pi", 0, 1))
+    ts(A("trb"), A("io128", 1, 129), pcol, Op.is_gt, -1.0, Op.mult)
+    ts(A("idw"), A("io128"), pcol, Op.is_equal)
     aff(h35, hcol, 3.5)
     aff(bcol, kcol, 0.5, h35)
     ts(A("prev1"), A("iob"), bcol, Op.is_gt)
     ts(dcol, bcol, kcol, Op.subtract, 512.0, Op.mult)
     aff(lxcol, bcol, -512.0, 16.0)
     ts(A("rf"), A("iom"), rcol, Op.is_equal)
-    ts(A("rfb"), A("iom"), rcol, Op.is_equal, float(DUM), Op.mult)
     ts(A("eef", p1=16), A("iom", p1=16), A("col", 0, 1, p1=16), Op.is_equal)
-    scan(A("io128"), A("onesb", 0, 128), A("onesb", 0, 128), Op.add, Op.mult, -1.0)
-    copy(pcol, A("pi", 0, 1))
-    ts(A("tri"), A("io128"), pcol, Op.is_gt, -1.0, Op.mult)
-    ts(A("ident"), A("io128"), pcol, Op.is_equal)
+    asel(A("tri"), A("onesb", 0, 128), [[0, 2], [1, 64]], Op.is_gt, 0, -1)
     aff(h0col, hcol, -1.0, 1.0)
     aff(A("ee", 0, 128), A("rf"), h0col)
     aff(A("ee", 128, 256), A("rf"), hcol)
@@ -599,78 +660,139 @@ def rank_program(g, core, T, topo):
     ts(onec, A("i16", 14, 15), A("i16", 12, 13), Op.subtract, 1.0 / 32, Op.mult)
     aff(ccol, onec, -float(ZC))
     aff(rhalf, rcol, 0.5)
-    ts(A("c1", 7, 128, 8), A("iog", 0, 128, 8), rhalf, Op.is_equal, ccol, Op.add)
+    ts(A("c1", 7, 112, 8), A("iog", 0, 112, 8), rhalf, Op.is_equal, ccol, Op.add)
     aff(ecol, onec, dcol)
     ts(A("c1", 103, 112, 8), A("c1", 103, 112, 8), ecol, Op.add)
     copy(A("io8", 0, 8), A("iom", 0, 8))
     copy(A("io8", 8, 9), A("pk", 3, 4))
-    memset(A("obi", 0, 9, p0=96), 2)
+    memset(A("obi", 0, 9, p0=96), 0)
     for d in range(3):
-        ts(A("obi", 0, 9, 1, 32 * d, 32 * d + 32), A("io8", 0, 9, 1, 32 * d, 32 * d + 32), d,
-           Op.logical_shift_right, 1, Op.bitwise_and)
-    fill(A("urow", p1=1), 16.0)
-    for q in range(7):
-        st, base = [4 * ST, 2 * ST, ST], 16
-        if q < 6:
-            d, b = q // 2, q % 2
-            base += st[2 - d]
-            st[2 - d] = -st[2 - d]
-        if q % 2 == 0:
-            iota(A("b8", 4 * q, 4 * q + 8), [[st[0], 2], [st[1], 2], [st[2], 2]], base, 0)
-        if q < 6:
-            base += 0 if b else BIG
-            st[2 - d] += BIG if b else -BIG
-        iota(A("urow", q, 128, 16, 0, 1), [[st[0], 2], [st[1], 2], [st[2], 2]], base, 0)
-    iota(A("ios"), [[1, 256]], 0, 0)
-    iota(A("io2", 0, 8), [[1, 8]], 0, 0)
-    iota(A("io2", 8, 16), [[4, 2], [-2, 2], [1, 2]], 2, 0)
-    iota(A("cc"), [[128, 6]], 512 + DUM // 2, 1)
-    ts(A("th8"), A("iom", 0, 8), kcol, Op.not_equal, -1000.0, Op.mult)
+        ts(A("obi", 0, 9, 1, 32 * d, 32 * d + 32), A("io8", 0, 9, 1, 32 * d, 32 * d + 32), 1 << d, Op.bitwise_and)
     ts(b1col, rcol, 8.0, Op.is_lt, 98304.0, Op.mult)
     aff(sbcol, b1col, 1.0 / 3)
-    aff(A("sel", 1, 80, 2), A("sel", 0, 80, 2), None, b1col)
-    ts(A("obt", 0, 9), A("obi", 0, 9), hcol, Op.is_equal)
+    aff(A("sel", 1, 128, 2), A("sel", 0, 128, 2), None, b1col)
+    aff(sbz, sbcol, None, -float(ZC))
+    aff(pw, A("obi", 7, 8), float(ST))
+    ts(k67, kcol, 6.0, Op.is_ge)
+    aff(hp, pw, hcol, k67)
+    ts(A("obt", 0, 9), A("obi", 0, 9), float(ST), Op.mult, hp, Op.is_equal)
     ts(k6f, kcol, 6.0, Op.is_equal)
     aff(k6col, k6f, 0.625)
     aff(A("m8", 0, 8), A("obt", 0, 8), 0.125, k6col)
-    aff(A("jb"), A("iom", 0, 8), 16.0, rcol)
-    aff(A("b2", 15, 128, 16), A("m8", 0, 8), A("i16", 0, 1))
+    ts(m63, jcol, 63.0, Op.not_equal, -1.0, Op.mult)
+    ts(A("back"), A("io128", 0, 128), pcol, Op.is_equal, m63, Op.mult)
+    aff(hneg, acol, -1.0, -256.0)
+    ts(A("uu"), A("iou"), hneg, Op.subtract)
+    for c in ("lf", "dw"):
+        fill(A(c), 0.0)
+    asel(A("pm", 0, 128), A("onesb", 0, 128), [[-64, 2], [16, 4], [-1, 16]], Op.is_equal, -48, 1)
+    asel(A("pm", 128, 256), A("onesb", 0, 128), [[64, 2], [32, 2], [-1, 32]], Op.is_equal, -96, 1)
+    ts(A("rfb"), A("iom"), rcol, Op.is_equal, float(DUM), Op.mult)
+    ts(A("th8"), A("iom", 0, 8), kcol, Op.not_equal, -1000.0, Op.mult)
+    aff(j0, rcol, None, 512.0)
+    aff(j1, rcol, None, 480.0)
     aff(A("e0"), A("onesb", 0, 8), A("i16", 0, 1))
+    for c in (7, 71):
+        aff(A("b2", c, c + 57, 8), A("m8", 0, 8), A("i16", 0, 1))
     for o in range(8):
         aff(wo(o), A("rf"), A("m8", o, o + 1))
     cut = min(2 + 2 * rank, 6)
-    aff(A("jn", 0, cut), A("jb", 0, cut), None, 512.0)
-    aff(A("jn", cut, 8), A("jb", cut, 8), None, 480.0)
-    ts(A("rt"), A("iom"), kcol, Op.is_equal, -1.0, Op.mult)
-    aff(A("c2", 7, 128, 8), A("bo", 0, 128, 8))
-    aff(A("c5", 7, 128, 8), A("onesb", 0, 16), k6f)
-    asel(A("pm", 0, 128), A("onesf"), [[-64, 2], [16, 4], [-1, 16]], Op.is_equal, -48, 1)
-    asel(A("pm", 128, 256), A("onesf"), [[64, 2], [32, 2], [-1, 32]], Op.is_equal, -96, 1)
-    ts(A("c4", 7, 128, 8), A("iog", 0, 128, 8), rcol, Op.is_equal, -1.0, Op.mult)
-    copy(A("lj"), A("io2"))
-    ts(zc0, kcol, 6.0, Op.is_lt, 1.0 / 64, Op.mult)
-    aff(zc, k6col, 0.625, zc0)
-    aff(A("m8", 16, 24), A("obt", 0, 8), 3.0 / 64, zc)
-    aff(A("m8", 24, 32), A("obt", 0, 8), -1.0, 1.0)
-    aff(A("m8", 24, 32, 1, 32, 64), A("obt", 0, 8, 1, 32, 64))
-    tt(A("wc"), ind(A("m8", 0, 8), A("lj", 8, 16)), A("rf"), Op.mult)
-    tt(A("wz"), ind(A("m8", 16, 24), A("lj", 0, 8)), A("rf"), Op.mult)
-    aff(rtcol, sbcol, None, float(ROOT))
-    fill(A("lf"), 0.0)
-    tt(A("r3"), ind(A("m8", 24, 32), A("lj", 0, 8)), A("rf"), Op.mult)
-    aff(q1col, r8col, 2.0, 17.0)
-    aff(q0col, A("obt", 8, 9), -16.0, q1col)
-    aff(rsb, sbcol, -1.0, float(ROOT))
-    aff(nsb, sbcol, -1.0)
-    ts(A("lq", 0, 4), A("iom", 0, 4), 4.0, Op.mult, q0col, Op.add)
-    ts(A("lq", 4, 8), A("iom", 0, 4), 4.0, Op.mult, q1col, Op.add)
-    ts(gcol, kcol, hcol, Op.subtract, 4.0, Op.mult)
-    ts(A("lq", 8, 12), A("onesb", 0, 4), g8col, Op.mult, gcol, Op.add)
-    aff(rdcol, gcol, 64.0, 512.0)
-    aff(A("b64"), ind(A("b8"), A("lq", 8, 12)), None, nsb)
+    aff(A("jn", 0, cut), A("iom", 0, cut), 16.0, j0)
+    aff(A("jn", cut, 8), A("iom", cut, 8), 16.0, j1)
+
+    first = len(ops)
+    builds = [rank] if SHARE else range(4)
+    if 0 in builds:
+        for c in range(0, 432, 144):
+            fill(A("fw", c, c + 144), 0.0)
+        iota(A("ioo"), [[0, 2], [1, 8], [32, 8]], 0, 0)
+        aff(xt, A("obi", 8, 9), -2.0 * ST, pw)
+        aff(x2, g8col, float(ST), xt)
+        ts(x3, A("obt", 8, 9), float(ROOT), Op.mult, x2, Op.max)
+        aff(x1, A("obt", 8, 9), -float(RS), float(RS))
+        for i, x in enumerate((x1, x3, x2)):
+            aff(A("xr", 9 * i, 9 * i + 9), A("bo", 0, 136, 16), x)
+        aff(r1col, rcol, None, 1.0)
+        ts(A("la", 0, 128), A("ioo"), rcol, Op.is_equal)
+        ts(A("la", 128, 256), A("ioo"), r1col, Op.is_equal, -1.0, Op.mult)
+        mm(A("p1", 0, 27), A("la", 0, 128), A("xr", 0, 27), True, False)
+        mm(A("p1", 0, 27), A("la", 128, 256), A("xr", 0, 27), False, True)
+        ts(a0, g8col, 0.0, Op.is_equal)
+        aff(d33, a0, -512.0, 64.0)
+        ts(wcol, jcol, 0.0, Op.is_equal)
+        aff(d32, wcol, 448.0, d33)
+        for h in range(2):
+            p = (64 * h, 64 * h + 64)
+            aff(A("fw", 14 + h, 288, 16, *p), A("p1", 0, 18, 1, *p), None, d32[:4] + p + (1,))
+            aff(A("fw", 302 + h, 432, 16, *p), A("p1", 18, 27, 1, *p))
+        glue(4)
+    if 1 in builds or 2 in builds:
+        copy(A("lj", 0, 8), A("iom", 0, 8))
+    if 1 in builds:
+        iota(A("io2", 8, 16), [[4, 2], [-2, 2], [1, 2]], 2, 0)
+        copy(A("lj", 8, 16), A("io2", 8, 16))
+        ts(zc0, kcol, 6.0, Op.is_lt, 1.0 / 64, Op.mult)
+        aff(zc, k6col, 0.625, zc0)
+        aff(A("m8", 16, 24), A("obt", 0, 8), 3.0 / 64, zc)
+        tt(A("wc"), ind(A("m8", 0, 8), A("lj", 8, 16)), A("rf"), Op.mult)
+        tt(A("wz"), ind(A("m8", 16, 24), A("lj", 0, 8)), A("rf"), Op.mult)
+    if 2 in builds:
+        aff(A("m8", 24, 32), A("obt", 0, 8), -1.0, 1.0)
+        aff(A("m8", 24, 32, 1, 32, 64), A("obt", 0, 8, 1, 32, 64))
+        tt(A("r3"), ind(A("m8", 24, 32), A("lj", 0, 8)), A("rf"), Op.mult)
+        for d in range(4):
+            st, base = [4 * ST, 2 * ST, ST], 0
+            if d < 3:
+                base += st[2 - d]
+                st[2 - d] = -st[2 - d]
+            iota(A("b8", 8 * d, 8 * d + 8), [[st[0], 2], [st[1], 2], [st[2], 2]], base, 0)
+        aff(rsb, sbcol, -1.0, float(ROOT))
+        ts(gcol, kcol, hcol, Op.subtract, 4.0, Op.mult)
+        aff(rdcol, gcol, RS / 8.0, float(RS))
+        iota(A("ci"), [[512, 2], [16, 8]], 512, 8)
+        aff(w0, rcol, -7.0)
+        aff(A("cc"), A("ci"), None, w0)
+        ts(r8col, rcol, 8.0, Op.is_ge)
+        aff(q1col, r8col, 2.0, 17.0)
+        aff(q0col, A("obt", 8, 9), -16.0, q1col)
+        aff(nsb, sbcol, -1.0)
+        ts(A("lq", 0, 4), A("iom", 0, 4), 4.0, Op.mult, q0col, Op.add)
+        ts(A("lq", 4, 8), A("iom", 0, 4), 4.0, Op.mult, q1col, Op.add)
+        ts(A("lp"), A("onesb", 0, 4), g8col, Op.mult, gcol, Op.add)
+        aff(A("b64"), ind(A("b8"), A("lp")), None, nsb)
+    if 3 in builds:
+        fill(A("ew"), 0.0)
+        ts(a0, jcol, 63.0, Op.is_equal, float(BIG), Op.mult)
+        ts(wcol, a0, 1.0, Op.max)
+        aff(d33, acol, -1.0, 1.0)
+        ts(A("ew", 14, 128, 16), A("onesb", 0, 8), wcol, Op.mult, d33, Op.mult)
+        ts(A("ew", 15, 128, 16), A("onesb", 0, 8), wcol, Op.mult, acol, Op.mult)
+        for c in ("c2", "c5"):
+            fill(A(c), 0.0)
+        aff(A("c2", 7, 128, 8), A("bo", 0, 128, 8))
+        fill(A("c3"), 0.0)
+        aff(A("c3", 15, 128, 16), A("bo", 0, 128, 16))
+        aff(A("c5", 7, 128, 8), A("onesb", 0, 16), k6f)
+        ts(A("pk", 6, 7), A("pi", 0, 1), 3, Op.logical_shift_right)
+        aff(d32, A("pk", 6, 7), 2.0, pcol)
+        ts(A("r80"), A("io128", 1, 81), d32, Op.is_equal)
+    for o in ops[first:]:
+        o["own"] = SHARE
 
     add("v", lambda q: q.transpose(ap(A("xt")), ap(A("x0"))), [A("xt")], [A("x0")], 64 * VEC)
-    number(0, A("xt"), A("prev1"), A("offh"))
+    ts(A("nf"), A("xt"), 0.0, Op.is_le)
+    scan(A("sc", 1, 33), A("onesb", 0, 32), A("nf"), Op.add, Op.subtract)
+    tt(A("nd"), A("nf"), A("dc"), Op.mult)
+    p1, pc = A("pb", 0, 32), A("pb", 32, 33)
+    mm(p1, A("trb"), A("nf"), True, False)
+    mm(p1, A("prev"), A("nf"), False, False)
+    glue(2)
+    mm(p1, ident, A("nd"), False, False)
+    mm(p1, A("bo", 0, 128), A("sc", 0, 32), False, True)
+    mm(pc, A("prev1"), A("sc", 32, 33))
+    glue(2)
+    ts(A("off"), p1, pc, Op.add, rcol, Op.add)
+    ts(A("offh"), p1, pc, Op.add, rcol, Op.add)
 
     copy(A("bdg", p1=16), A("bdi", p1=16))
     mm(A("pz", 0, 8), A("eef", p1=16), A("bdg", p1=16))
@@ -678,9 +800,17 @@ def rank_program(g, core, T, topo):
     aff(A("xa"), ind(A("xn"), A("lx")))
     mm(A("pz", 128, 256), A("rf"), A("xa"))
     aff(A("xb"), A("pz", 128, 256))
-    sa = fused(lambda q: A("xb", 32 * q, 32 * q + 32),
-               lambda q: A("xw", 4096 + 32 * rank, 4128 + 32 * rank), "arra", FIRST, False)
-    arrive([A("xw", 4096 + 32 * q, 4128 + 32 * q) for q in peers], "arra", (sa,), False)
+    sa = fused([(A("xb", 32 * q, 32 * q + 32), [(q, A("xw", 4096 + 32 * rank, 4128 + 32 * rank))], "arra",
+                 share(rank, q, AENG)) for q in peers], FIRST)
+    add("-", None, [A("xw", 4096 + 32 * q, 4128 + 32 * q) for q in peers], [], 0.0, "arra", 3 * AENG, after=(sa,))
+    if SHARE:
+        mine = A(SHARED[rank])
+        sk = fused([(mine, [(q, mine) for q in peers], "arrk%d" % rank, topo.engines(core, cores[peers[0]])[-KENG:])],
+                   KCALL)
+        ops[sk].update(after=(sa,), due=KSEND[rank])
+        for q in peers:
+            soon = add("-", None, [], [], 0.0, lat=KARR[q])
+            add("-", None, [A(SHARED[q])], [], 0.0, "arrk%d" % q, KENG, after=(sk, soon))
     banks = ["p0", "p1", "p2"]
 
     mm(A("p0", 0, 8), A("xw", 4096, ZC, p1=16), A("e0", p1=16))
@@ -689,80 +819,100 @@ def rank_program(g, core, T, topo):
     tt(A("nw", 256, 264), A("p0", 8, 16), A("jn"), Op.add)
 
     aff(A("w1", 0, 128), ind(A("d1"), A("lx")))
-    copy(ind(A("w1", 128), A("off", 0, 32)), A("d1", 16, 528))
-    spread(lambda gr: A("pd", 32 * block(gr), 32 * block(gr) + 32), A("offh"))
-    aff(A("nw", 0, 256), A("pd", 0, 256))
     wrap8(A("pc", 0, 16), "c1", A("w1"), 128)
+    for a, b in zip(SPLIT, SPLIT[1:]):
+        copy(ind(A("w1", 128), A("off", a, b)), A("d1", 16 + 16 * a, 16 + 16 * b))
+    for gr in range(8):
+        lo, c = (32 * (gr // 2), 32 * (gr // 2) + 32), 128 * (gr % 2)
+        mm(A("pd", 32 * block(gr), 32 * block(gr) + 32), A("ee", c, c + 128, 1, *lo), A("offh", 0, 32, 1, *lo))
+        glue(1 + gr % 2)
+    aff(A("nw", 0, 256), A("pd", 0, 256))
     wrap8(A("pc", 16, 80), "c1", A("w1", 128), 512)
-    scan(A("sw", 0, 80), A("sel"), A("pc", 0, 80), Op.add, Op.max)
-    ts(A("l1u"), A("sw", 1, 80, 2), sbcol, Op.subtract, float(ZC), Op.add)
-    ts(A("li"), A("sw", 1, 80, 2), sbcol, Op.subtract, float(ZC), Op.add)
-    parts = ((0, 128), (128, 384), (384, 640))
-    for a, b in parts:
-        aff(A("gw", a, b), ind(A("xw"), A("l1u", a // 16, b // 16)))
+    scan(A("sw", 0, 80), A("sel", 0, 80), A("pc", 0, 80), Op.add, Op.max)
+    ts(A("l1u"), A("sw", 1, 80, 2), sbz, Op.subtract)
+    aff(A("gs"), ind(A("xw"), A("l1u", 0, 8)))
+    ts(A("li"), A("sw", 1, 80, 2), sbz, Op.subtract)
     digits("li", "lcr", "lcu", 40)
-    gw = A("gw", 128, 640)
-    mm(A("pb", 100, 101), A("urow", p1=1), A("onesf", 0, 1, 1, 0, 1))
-    ts(nrc, A("pb", 100, 101), float(ROOT), Op.min, -1.0, Op.mult)
-    ts(tcol, A("pb", 100, 101), float(ROOT), Op.is_gt, 2.0 * BIG, Op.mult)
-    ts(bias2, tcol, A("pb", 100, 101), Op.subtract, float(BIG), Op.subtract)
-    aff(nrc2, nrc, None, -256.0)
-    aff(A("nr", 0, 256), A("ios"), -1.0, nrc)
-    aff(A("nr", 256, 512), A("ios"), -1.0, nrc2)
+    for h in range(2):
+        aff(A("gw", 256 * h, 256 * h + 256), ind(A("xw"), A("l1u", 8 + 16 * h, 24 + 16 * h)))
+    gw = A("gw")
 
-    sb = fused(lambda q: A("gw", 32 * q, 32 * q + 32),
-               lambda q: A("gg", 32 * slot(q, rank), 32 * slot(q, rank) + 32), "arrb", 0.7, True)
-    arrive([A("gg")], "arrb", (sb,), True)
+    sb = fused([(A("gs", 32 * q, 32 * q + 32), [(q, A("gg", 32 * slot(q, rank), 32 * slot(q, rank) + 32))], "arrb",
+                 share(rank, q, BENG)) for q in peers], BCALL)
+    add("-", None, [A("gg", 0, 96)], [], 0.0, "arrb", 3 * BENG, after=(sb,))
+    ops[sb]["due"] = BSEND
 
-    for r in range(16):
-        mm(A("pa", 64, 96), A("b2", 15 - r, 143 - r), A("gw", 128 + r, 640, 16), r == 0, r == 15)
-    glue(16)
-    number(1, A("pa", 64, 96), A("prev"), A("n2h", 0, 32))
-    for h, (a, b) in enumerate(parts):
-        aff(A("mk", a, b), ind(A("i16"), A("lcu", 40 + a // 16, 40 + b // 16)))
-        tt(A("tm", a, b), ind(A("nw"), A("lcu", a // 16, b // 16)), A("mk", a, b), Op.mult)
-        if h:
-            bank = A(("pz", "pc")[h - 1], 0, 256)
-            mm(bank, A("rt"), A("tm", a, b))
-            aff(A("d2", a - 128, b - 128), bank, None, bias2)
+    aff(A("mk", 0, 128), ind(A("i16"), A("lcu", 40, 48)))
+    tt(A("tmb"), ind(A("nw"), A("lcu", 0, 8)), A("mk", 0, 128), Op.mult)
+    for h in range(2):
+        a = 256 * h
+        aff(A("mk", a + 128, a + 384), ind(A("i16"), A("lcu", 48 + 16 * h, 64 + 16 * h)))
+        tt(A("tm", a, a + 256), ind(A("nw"), A("lcu", 8 + 16 * h, 24 + 16 * h)), A("mk", a + 128, a + 384), Op.mult)
 
-    wrap8(A("pd", 400, 416), "c2", A("tm"), 128)
-    wrap8(A("pd", 416, 432), "c5", A("tm"), 128)
-    scan(A("sb"), A("sel", 0, 32), A("pd", 400, 432), Op.add, Op.max)
+    for r in range(8):
+        mm(A("pa", 64, 128), A("b2", 7 - r, 135 - r), A("gw", 64 * r, 64 * r + 64), r == 0, r == 7)
+    glue(8)
+    cnt, before = A("sc", 40, 104), A("pb", 80, 81)
+    ts(A("fl"), A("pa", 64, 128), 100.0, Op.is_gt)
+    ts(A("nd2"), A("pa", 64, 128), 100.0, Op.is_le, float(DUM), Op.mult)
+    scan(cnt, A("onesb", 0, 64), A("fl"), Op.mult, Op.add)
+    mm(before, A("tri"), A("sc", 103, 104))
+    ts(A("st"), A("iou"), before, Op.subtract, hneg, Op.is_ge)
+    ts(A("n2", 0, 64), cnt, before, Op.add, -1.0, Op.add)
+    tt(A("n2", 64, 128), A("n2", 0, 64), A("nd2"), Op.max)
+    mm(A("pc", 320, 384), ident, cnt, True, False)
+    mm(A("pc", 320, 384), A("back"), cnt, False, True)
+    mm(A("pc", 384, 385), A("back"), A("sc", 103, 104))
+    glue(3)
+    for h in (0, 64):
+        ts(A("dw", h, h + 64, 1, h, h + 64), A("pc", 320, 384, 1, h, h + 64), A("pc", 384, 385, 1, h, h + 64), Op.subtract)
+    glue(2)
+    mm(A("pa", 128, 384), A("dw"), A("st"))
+    tt(A("cm"), A("pa", 128, 384), A("uu"), Op.is_le)
+    wrap4(A("pd", 320, 352), "fw", 0, "st", True)
+    wrap4(A("pd", 320, 352), "ew", 0, "cm", False)
+    ts(A("ls"), A("pd", 320, 352), 512.0, Op.min)
+    wrap4(A("pc", 128, 160), "fw", 144, "st", True)
+    wrap4(A("pc", 128, 160), "ew", 0, "cm", False)
+    ts(A("rr"), A("pc", 128, 160), ROOT + 512.0, Op.min)
+    wrap4(A("pc", 192, 224), "fw", 288, "st", True)
+    for h in range(2):
+        aff(A("tg", 256 * h, 256 * h + 256), ind(A("tm"), A("ls", 16 * h, 16 * h + 16)))
+    wrap16(A("pc", 192, 224), "tg", False)
+    tt(A("li2"), A("pc", 192, 224), A("rr"), Op.min)
+    copy(A("l2u"), A("li2"))
+    ts(A("l2r"), A("li2"), float(ROOT), Op.is_ge, rdcol, Op.mult)
+    aff(A("l2t"), A("li2"), None, float(TB))
+    tt(A("l2s"), A("l2r"), A("l2t"), Op.add)
+
+    mm(A("pb", 0, 80, p1=64), A("n2", 64, 128), A("r80"))
+    aff(A("nt", p1=64), A("pb", 0, 80, p1=64))
+
+    wrap8(A("pz", 0, 16), "c2", A("tmb"), 128)
+    wrap8(A("pz", 16, 32), "c5", A("tmb"), 128)
+    scan(A("sb"), A("sel", 0, 32), A("pz", 0, 32), Op.add, Op.max)
     tt(A("pv", 0, 64), ind(A("sb"), A("lq", 0, 4)), A("b64"), Op.add)
     aff(A("pv", 64, 128), ind(A("sb"), A("lq", 4, 8)), None, rsb)
     tt(A("pv", 128, 192), A("pv", 0, 64), A("pv", 64, 128), Op.min)
     ts(A("lvb"), A("pv", 128, 192), ROOT + 511.0, Op.min)
-    tt(ind(A("w2"), A("off", 32, 64)), A("d2"), A("nr"), Op.max)
-    if LVB:
-        ops[-1]["after"] = (len(ops) - 2,)
-
-    wrap8(A("pc", 320, 384), "c4", A("w2"), 512)
-    scan(A("sw", 64, 128), A("sel", 0, 64), A("pc", 320, 384), Op.add, Op.max)
-    ts(A("l2u"), A("sw", 65, 128, 2), sbcol, Op.subtract)
-    ts(A("li2"), A("sw", 65, 128, 2), sbcol, Op.subtract)
-    ts(A("l2r"), A("sw", 65, 128, 2), rtcol, Op.is_ge, rdcol, Op.mult)
-    aff(A("l2t"), A("sw", 65, 128, 2), None, float(TB))
-    tt(A("l2s"), A("l2r"), A("l2t"), Op.add)
 
     asel(A("t1", TB + ROOT, TB + ROOT + 512), gw, [[0, 512]], Op.is_ge, 0, 0)
     for d in range(3):
         for f in range(8):
             q = 2 * d + 1 - ((f ^ 2) >> d & 1)
             src = A("t1", TB + ROOT, TB + ROOT + 512, 1, 16 * q, 16 * q + 16)
-            c = TB + ROOT + 512 * (d + 1)
-            load("s", A("t1", c, c + 512, 1, 16 * f, 16 * f + 16), ap(src), "lrt", 3.0, 0.0, r=[src])
+            c = TB + ROOT + RS * (d + 1)
+            load("s", A("t1", c, c + 512, 1, 16 * f, 16 * f + 16), ap(src), "lrt", 3.0, [src])
         glue(8)
     for h in range((NDMA + 3) // 4):
         mm(A(banks[2 - h]), A("wo", 512 * h, 512 * h + 128), gw)
         aff(A("yt", 512 * h, 512 * h + 512), A(banks[2 - h]))
     for o in range(8):
-        c = TB + 16 + ST * o
+        c = TB + ST * o
         if o < NDMA:
             src = A("yt", 512 * (o // 4), 512 * (o // 4) + 512, 1, o % 4, 128, 4)
             for f in range(0, 128, 32):
-                add("s", lambda q, f=f, c=c, src=src: q.dma_start(ap(A("t1", c, c + 512, 1, f, f + 32)), ap(src)),
-                    [A("t1", c, c + 512, 1, f, f + 32)], [src], DMAC, "lt1", 16, True, 2.3)
+                load("s", A("t1", c, c + 512, 1, f, f + 32), ap(src), "lt1", 1.6, [src], DMAC)
             glue(4)
             store("s", T.y1[16 * o:16 * o + 16, :], src[:5] + (64, 4), "oy1")
             continue
@@ -770,18 +920,18 @@ def rank_program(g, core, T, topo):
         aff(A("t1", c, c + 512), A(banks[o % 3]))
         store("s", T.y1[16 * o:16 * o + 16, :], A("t1", c, c + 512, 1, 16 * o, 16 * o + 16), "oy1")
     for o in range(8):
-        mm(A(("pz", "pb")[o // 4], 128 + 96 * (o % 4), 224 + 96 * (o % 4)), wo(o), A("gg"))
+        mm(A(("pz", "pb")[o // 4], 128 + 96 * (o % 4), 224 + 96 * (o % 4)), wo(o), A("gg", 0, 96))
         glue(1 + o % 4)
     for o in range(8):
-        c = TB + 528 + ST * o
+        c = TB + 512 + ST * o
         aff(A("t1", c, c + 96), A(("pz", "pb")[o // 4], 128 + 96 * (o % 4), 224 + 96 * (o % 4)))
-    t1 = A("t1", TB, TB + ROOT + 512)
+        glue(1 + o % 4)
+    t1 = A("t1", TB, TB + ROOT + RS)
 
     def turns(at):
         return sorted((at ^ k for k in range(1, len(cores))), key=lambda q: topo.die(cores[q]) == topo.die(cores[at]))
-    order = turns(rank)
     sent = []
-    for i, q in enumerate(order):
+    for i, q in enumerate(turns(rank)):
         o = A("vb", 256 * i, 256 * i + 256)
         aff(o, ind(t1, A("lvb", 16 * q, 16 * q + 16)))
         if i >= RAW:
@@ -790,21 +940,24 @@ def rank_program(g, core, T, topo):
             aff(o, A(banks[i], 0, 256))
         rid, pid = topo.addr(cores[q])[:2]
         s = slot(q, rank)
-        m = topo.mask(core, cores[q])
+        m = sum(1 << e for e in share(rank, q, CENG))
         land = A("t1", 512 + 256 * s, 768 + 256 * s) if i >= RAW else A("vg", 256 * s, 256 * s + 256)
         sent.append(add("g", lambda x, o=o, s=s, rid=rid, pid=pid, m=m, land=land: x.remote_dma(
             ap(land), ap(o), T.sem["arrc%d" % s], T.sem.sent, pid, rid, m),
-            [], [o], 0.4, "sent", len(topo.engines(core, cores[q])), lat=2.3))
+            [], [o], 0.4, "sent", CENG, lat=2.3))
 
-    for r in range(16):
-        mm(A("pa", 128, 134), A("b2", 15 - r, 143 - r), A("gg", r, 96, 16), r == 0, r == 15)
-    glue(16)
-    add("a", lambda q: q.activation(ap(A("nfg")), ap(A("pa", 128, 134)), Fn.Sign, bias=100.0625, scale=-1.0),
-        [A("nfg")], [A("pa", 128, 134)], 0.08)
-    for c in range(6):
-        aff(A("n2h", 32 + c, 33 + c), A("nfg", c, c + 1), DUM / 2.0, A("cc", c, c + 1))
-    spread(lambda gr: A("pd", 38 * gr, 38 * gr + 38), A("n2h", 0, 38))
-    aff(A("nw2", 1, 305), A("pd", 0, 304))
+    for a in range(2):
+        mm(A("pd", 400 + 8 * a, 408 + 8 * a, p1=64), A("gg", 64 * a, 64 * a + 64), A("b2", 7, 64, 8))
+    glue(2)
+    ts(A("nfg", p1=64), A("pd", 400, 416, p1=64), 100.0, Op.is_le, float(DUM), Op.mult)
+    for a in range(2):
+        tt(A("nt", 8 + a, 80, 10, p1=64), A("nfg", 8 * a, 8 * a + 8, p1=64), A("cc", 8 * a, 8 * a + 8, p1=64), Op.add)
+    glue(2)
+    for j in range(4):
+        lo = (32 * (j // 2), 32 * (j // 2) + 32)
+        mm(A("pd", j, 320, 4), A("ee", 128 * (j % 2), 128 * (j % 2) + 128, 1, *lo), A("nt", 0, 80, 1, *lo))
+        glue(1 + j % 2)
+    aff(A("nw2", 0, 320), A("pd", 0, 320))
 
     for h in range(2):
         c = (256 * h, 256 * h + 256)
@@ -815,7 +968,7 @@ def rank_program(g, core, T, topo):
         q = [p for p in peers if turns(p)[i] == rank][0]
         s = slot(rank, q)
         land = A("t1", 512 + 256 * s, 768 + 256 * s) if i >= RAW else A("vg", 256 * s, 256 * s + 256)
-        add("-", None, [land], [], 0.0, "arrc%d" % s, len(topo.engines(cores[q], core)), after=(sent[i],))
+        add("-", None, [land], [], 0.0, "arrc%d" % s, CENG, after=(sent[i],))
         if i >= RAW:
             continue
         mm(A(banks[i], 0, 256), A("wc"), A("vg", 256 * s, 256 * s + 256))
@@ -826,13 +979,13 @@ def rank_program(g, core, T, topo):
         c = (256 * h, 256 * h + 256)
         aff(A("mk2", *c), ind(A("i16"), A("lcu2", 32 + 16 * h, 48 + 16 * h)))
         tt(A("tm2", *c), ind(A("nw2"), A("lcu2", 16 * h, 16 * h + 16)), A("mk2", *c), Op.mult)
-    wrap8(A("pc", 0, 64), "c2", A("tm2"), 512)
-    scan(A("sw", 128, 192), A("sel", 0, 64), A("pc", 0, 64), Op.add, Op.max)
+    wrap16(A("pc", 0, 32), "tm2", True)
     for d in range(3):
         p = (32 * d, 32 * d + 32)
-        tt(A("lf", p[0], p[1], 1, *p), A("sw", 129, 192, 2, *p), A("l2s", 0, 32, 1, *p), Op.min)
+        tt(A("lf", p[0], p[1], 1, *p), A("pc", 0, 32, 1, *p), A("l2s", 0, 32, 1, *p), Op.min)
+    glue(3)
     mm(A("pc", 128, 224), A("r3", p1=96), A("lf", p1=96))
-    ts(A("lfu"), A("pc", 128, 224), sbcol, Op.subtract)
+    copy(A("lfu"), A("pc", 128, 224))
     zb = ["pz", "pd", "pa", "pb"]
     cuts = list(zip(CUTS, CUTS[1:]))
     for h, (a, b) in enumerate(cuts):
@@ -847,19 +1000,29 @@ def rank_program(g, core, T, topo):
         tt(A("yo", a, b), A(zb[h], 0, b - a), gd, Op.add)
         store("sa"[h % 2], T.y2[:, a:b], A("yo", a, b), "oy2")
 
-    total = emit(g, T, arrange(ops))
+    total = emit(g, T, arrange(ops, rank))
     g.sync.wait_ge(T.sem.oy1, total["oy1"])
     g.sync.wait_ge(T.sem.oy2, total["oy2"])
     g.wait_ge(T.sem.sent, total["sent"])
 
 
-MOVES = 130000
-HEAT = 0.6
-LATEX = False
+TRIES = 100
+MOVES = 400000
+SHARE = False
+MOVES2 = 40000
+HEAT, HEAT2 = 0.5, 0.15
 MIX = 0.6
+PULL = 0.0
+AIM = {("yt", 0): 8.2, ("gs", 0): 7.3, ("st", 0): 9.2, ("ls", 0): 10.8, ("l2u", 0): 12.5, ("lfu", 0): 16.4}
 NDMA = 4
 DMAC = 0.12
-FIRST = 1.3
-LVB = False
+FIRST, BCALL = 1.3, 0.7
+KCALL, KENG = 1.5, 8
+KSEND, KARR = (5.0, 6.9, 6.9, 5.0), (10.0, 12.0, 11.4, 10.0)
+STEP, AENG, BENG, CENG = 1, 2, 2, 16
+BSEND = 8.9
+SPLIT = (0, 32)
+PACK = 2000
+LX, LQ = 3.7, 5.5
 RAW = 1
 CUTS = (0, 160, 320, 448, 512)

@@ -2,66 +2,47 @@ from concourse.bass import DstId, RemoteDMATransfer
 from concourse.mybir import AluOpType, ActivationFunctionType
 
 F32, BF, F16, I32, U16 = "float32", "bfloat16", "float16", "int32", "uint16"
-ZC = 4224
 ST = 640
 ROOT = 8 * ST
 TB = 1280
 DUM = 8576
 BIG = 16384
-ZS = 176
 RS = 528
 
 SB = {
-    "xw": (4240, BF), "xn": (544, BF), "x0": (32, BF), "xt": (32, BF), "d1": (544, I32), "idb": (64, I32),
-    "bdi": (8, I32), "bdg": (8, F32), "lx": (8, U16), "xa": (128, BF), "xb": (128, BF), "gs": (128, BF),
-    "eef": (128, F32), "e0": (8, BF), "th8": (8, F32), "nfb": (8, BF),
-    "w1": (14208, F32), "gw": (512, BF), "gg": (128, BF),
-    "onesb": (144, BF), "onesf": (128, F32), "b2": (136, BF), "pi": (4, I32), "pk": (8, I32),
-    "col": (48, F32), "iog": (144, BF), "iom": (128, BF), "iob": (128, BF), "bo": (136, BF), "trb": (128, BF),
-    "prev": (128, BF), "io128": (136, BF), "prev1": (128, BF), "rf": (128, BF), "rfb": (128, BF),
-    "idw": (136, BF), "tri": (128, BF), "dc": (32, F32), "i16": (16, F32),
-    "yt": (1024, F32), "n2": (128, F16), "nt": (80, F16), "offh": (32, F16), "io8": (12, I32), "io2": (16, I32),
-    "ee": (256, BF), "c1": (136, F32), "sel": (128, F32), "ioo": (128, BF),
-    "obi": (12, I32), "obt": (12, F32), "m8": (40, F32), "lj": (16, U16),
-    "fw": (432, F16), "c3": (144, BF), "rr": (32, F32), "wf": (256, F32), "pf": (220, F32), "pm": (256, F32), "l3": (8, U16), "kf": (496, F16),
-    "lf": (96, F32), "n2g": (80, F32), "uu": (256, F16), "dw": (128, BF),
-    "l2r": (32, F32), "l2t": (32, F32), "iou": (256, BF), "pl": (32, F32),
-    "st": (256, BF), "cm": (256, BF), "la": (256, BF),
-    "xr": (52, F16), "ls": (32, U16), "tg": (512, F16), "tmb": (128, F16), "wo": (1024, BF),
-    "jn": (8, F32), "ci": (16, F32), "nw": (272, F32), "nw2": (360, F32),
-    "nf": (32, BF), "sc": (104, BF), "nd": (32, F16), "fl": (64, BF), "nd2": (64, F16), "back": (128, BF),
-    "off": (32, U16), "b8": (32, F32), "nfg": (16, F32), "lq": (8, U16), "lp": (4, U16), "pv": (192, F32),
-    "lvb": (64, U16), "sw": (336, F32), "sb": (32, F32), "l1u": (40, U16), "l2u": (32, U16), "li": (40, I32),
-    "lcr": (80, I32), "lcu": (80, U16), "li2": (32, I32), "lcr2": (64, I32), "lcu2": (64, U16),
-    "mk": (640, BF), "tm": (520, F32), "mk2": (512, BF), "tm2": (512, F16), "l2s": (32, F32), "lfu": (96, U16),
-    "t1": (TB + ROOT + 4 * RS, F32), "v": (512, F32), "vb": (768, F32), "vg": (768, F32), "vc": (768, F32),
-    "gd": (1536, F32), "yo": (512, F32),
+    "xw": (4224, BF), "x0": (32, BF), "xt": (32, BF), "d1": (544, I32), "idb": (64, I32),
+    "bdi": (8, I32), "bdg": (8, F32), "eef": (128, F32), "lx": (16, U16), "xs": (4112, BF), "xa": (128, BF), "xb": (128, BF), "gs": (128, BF), "th8": (8, F32),
+    "nfb": (8, BF), "w1": (14208, F32), "gw": (512, BF), "gg": (96, BF), "onesb": (144, BF),
+    "pk": (24, I32), "col": (40, F32), "iog": (144, BF), "iom": (128, BF), "iob": (128, BF), "bo": (136, BF),
+    "trb": (128, BF), "prev": (128, BF), "io128": (136, BF), "prev1": (128, BF), "rf": (128, BF), "rfb": (128, BF),
+    "idw": (136, BF), "tri": (128, BF), "dc": (32, F32), "i16": (16, F32), "qw": (1128, F32), "tq": (512, F16),
+    "mq": (512, BF), "un": (512, F16), "ix": (112, BF), "e1": (96, BF), "dd": (96, BF), "th": (128, BF),
+    "i8": (8, F32), "xi": (96, F32), "xg": (96, F16), "tw": (1128, F32), "tg": (512, F16), "lm": (32, U16),
+    "nfs": (64, BF), "k2": (192, F32), "th64": (64, F32), "yt": (512, F32), "offh": (32, F16), "ee": (256, BF),
+    "c1": (136, F32), "sel": (80, F32), "ioo": (128, BF), "obi": (12, I32), "obt": (12, F32), "m8": (32, F32),
+    "lj": (16, U16), "fw": (288, BF), "ew": (144, BF), "wt": (800, BF), "c2": (136, BF), "c3": (144, BF),
+    "c5": (136, BF), "b2": (136, BF), "dw": (128, BF), "rr": (32, F32), "wc": (128, F32), "wz": (128, F32), "r3": (128, F32), "b64": (64, F32),
+    "sto": (64, F32), "pm": (256, F32), "lf": (96, F32), "uu": (256, F16), "l2r": (32, F32),
+    "st": (256, BF), "cm": (256, BF), "la": (256, BF), "xr": (24, F16), "ls": (32, U16), "tmb": (128, F16),
+    "wo": (1024, BF), "jn": (8, F32), "nw": (264, F32), "nf": (32, BF), "sc": (104, BF), "nd": (32, F16),
+    "fl": (64, BF), "n2": (64, F16), "back": (128, BF), "off": (32, U16), "lq": (8, U16), "lp": (4, U16),
+    "pv": (192, F32), "lvb": (64, U16), "sw": (80, F32), "sb": (32, F32), "l1u": (40, U16), "l2u": (32, U16),
+    "li": (40, I32), "lcr": (80, I32), "lcu": (80, U16), "li2": (32, I32), "mk": (640, BF), "tm": (512, F16),
+    "l2s": (32, F32), "lfu": (96, U16), "t1": (TB + ROOT + 4 * RS, F32), "v": (512, F32), "vb": (768, F32),
+    "vg": (768, F32), "vc": (768, F32), "gd": (1536, F32), "yo": (512, F32),
 }
-PART = {"wc": ("wf", 0, 128), "wz": ("wf", 128, 128), "r3": ("pf", 0, 128),
-        "b64": ("pf", 128, 64), "lqf": ("pf", 192, 8), "late": ("pf", 200, 4),
-        "cc": ("pf", 204, 16), "ew": ("kf", 0, 144), "r80": ("kf", 144, 80), "c2": ("kf", 224, 136),
-        "c5": ("kf", 360, 136)}
-SHARED = ["fw", "wf", "pf", "kf"]
 SCRATCH = {k: ("sbuf", [128, v[0]], v[1]) for k, v in SB.items()}
 PSUM = ["pa", "pb", "pc", "pd", "p0", "p1", "p2", "pz"]
 for _p in PSUM:
     SCRATCH[_p] = ("psum", [128, 512], F32)
-SEMAPHORES = ["cv", "ca", "ct", "cg", "lx0", "lbd", "lnb", "lxn", "lx", "lrt", "lt1", "oy1",
-              "oy2", "arra", "arrz", "arrk0",
-              "arrk1", "arrk2", "arrk3", "arrb", "arrc0", "arrc1", "arrc2", "sent"]
+SEMAPHORES = ["cv", "ca", "ct", "cg", "lx0", "lbd", "lnb", "lx", "lxs", "lrt", "lt1", "oy1", "oy2", "arra", "arrb",
+              "arrc0", "arrc1", "arrc2", "sent"]
 ENG_SEM = {"v": "cv", "a": "ca", "t": "ct", "g": "cg"}
-GAP = 0.24
-VEC = 0.0009
-PE = 0.00045
-SLACK = 0.2
-SEED = 5
-PLANS = {}
+QUEUES = "vatgs-"
+PLAN = []
 
 
 def A(name, c0=0, c1=None, cs=1, p0=0, p1=128, ps=1):
-    if name in PART:
-        home, at, n = PART[name]
-        return (home, at + c0, at + (n if c1 is None else c1), cs, p0, p1, ps)
     if c1 is None:
         c1 = SB[name][0] if name in SB else 512
     return (name, c0, c1, cs, p0, p1, ps)
@@ -91,8 +72,174 @@ def unfenced(o, p):
     return p["e"] == "t" and o["e"] == "t" and p["tile"] == o["tile"]
 
 
-def arrange(ops, rank):
-    calls, ops, home = ops, [], []
+def pack(key, alt, lat, before, behind):
+    n = len(alt)
+    lo, hi = [[] for e in QUEUES], [[] for e in QUEUES]
+    start, end, pick = [0.0] * n, [0.0] * n, [0] * n
+    left = [len(p) for p in before]
+    ready = [(key[i], i) for i in range(n) if not left[i]]
+    while ready:
+        ready.sort()
+        i = ready.pop()[1]
+        t0 = max([end[j] + gap for j, gap in before[i]] + [0.0])
+        top = None
+        for e, c in alt[i]:
+            t, a, b = t0, lo[e], hi[e]
+            k = len(a)
+            while k and b[k - 1] > t:
+                k -= 1
+            while k < len(a) and t + c > a[k] + 1e-9:
+                t = b[k]
+                k += 1
+            if top is None or t + c < top[0]:
+                top = (t + c, t, e, k)
+        t, start[i], e, k = top
+        end[i], pick[i] = t + lat[i], e
+        if e != 5:
+            lo[e].insert(k, start[i])
+            hi[e].insert(k, t)
+        for k, gap in behind[i]:
+            left[k] -= 1
+            if not left[k]:
+                ready.append((key[k], k))
+    return sorted(range(n), key=lambda x: (start[x], x)), pick
+
+
+def improve(ops):
+    n = len(ops)
+    pred = [[j for j in range(i) if conflict(ops[i], ops[j]) or j in ops[i]["after"]] for i in range(n)]
+    above, before, behind = [0] * n, [], [[] for _ in range(n)]
+    for i in range(n):
+        keep = []
+        for j in reversed(pred[i]):
+            if not above[i] >> j & 1:
+                queued = ops[i]["dma"] and j in ops[i]["after"]
+                keep.append((j, -ops[j]["lat"] if queued else 0.0 if unfenced(ops[i], ops[j]) else GAP))
+                behind[j].append((i, keep[-1][1]))
+            above[i] |= above[j] | 1 << j
+        before.append(keep)
+    alt = [[(QUEUES.index(e), c) for e, f, c in o["alt"]] for o in ops]
+    lat = [o["lat"] for o in ops]
+    c1 = [dict(a) for a in alt]
+    c2 = [{e: c * o["slow"] for e, c in a} for o, a in zip(ops, alt)]
+    wait = [tuple((j, gap + lat[j], gap + lat[j] + (GAP2 - GAP) * (gap > 0)) for j, gap in b) for b in before]
+    r1, r2 = lat[:], lat[:]
+    for i in range(n - 1, -1, -1):
+        r1[i] += max([r1[k] + gap + min(c1[k].values()) for k, gap in behind[i]] + [0.0])
+        r2[i] += max([r2[k] + gap + min(c2[k].values()) for k, gap in behind[i]] + [0.0])
+    seed = [SEED]
+
+    def rand(m=1.0):
+        seed[0] = (seed[0] * 1103515245 + 12345) % 2147483648
+        return m * seed[0] / 2147483648
+
+    def run(order, pick, a, old, bar):
+        e1, e2 = old[0][:], old[1][:]
+        f1, f2 = [0.0] * 6, [0.0] * 6
+        k, left = a, 31
+        while k and left:
+            k -= 1
+            i = order[k]
+            if left >> pick[i] & 1:
+                left ^= 1 << pick[i]
+                f1[pick[i]], f2[pick[i]] = e1[i], e2[i]
+        m1 = m2 = 0.0
+        for i in order[a:]:
+            e = pick[i]
+            t, u = f1[e], f2[e]
+            for j, gap, gap2 in wait[i]:
+                x = e1[j] + gap
+                if x > t:
+                    t = x
+                x = e2[j] + gap2
+                if x > u:
+                    u = x
+            t += c1[i][e]
+            u += c2[i][e]
+            e1[i], e2[i] = t, u
+            if e != 5:
+                f1[e], f2[e] = t, u
+            t += r1[i]
+            u += r2[i]
+            if t > m1 or u > m2:
+                m1, m2 = max(t, m1), max(u, m2)
+                if m1 + MIX * m2 > bar:
+                    return None
+        return m1 + MIX * m2 + MEAN * sum(e1) / n, order, pick, (e1, e2), m1, m2
+
+    def waits(now, w):
+        order, pick, end = now[1], now[2], now[3][w]
+        prior, last = [None] * n, [None] * 6
+        for i in order:
+            prior[i], last[pick[i]] = last[pick[i]], i
+        i, chain = max(range(n), key=lambda x: end[x] + lat[x]), []
+        while i is not None:
+            begin = end[i] - (c1, c2)[w][i][pick[i]] - 1e-7
+            up = [x[0] for x in wait[i] if end[x[0]] + x[1 + w] >= begin]
+            j = up[0] if up else prior[i] if pick[i] != 5 else None
+            if not up and j is not None and not above[i] >> j & 1:
+                chain.append((i, j))
+            i = j
+        return chain
+
+    none = ([0.0] * n, [0.0] * n)
+    start = best = run(*pack([r1[i] + min(c1[i].values()) for i in range(n)], alt, lat, before, behind), 0, none, 999.0)
+    for moves, heat, anew in ROUNDS:
+        now, chains = start if anew else best, None
+        for trial in range(moves):
+            order, pick = now[1:3]
+            if trial % PACK == 0:
+                key = [0.0] * n
+                for k, x in enumerate(order):
+                    key[x] = -k
+                some = [a if rand() < 0.1 else [(pick[i], c1[i][pick[i]])] for i, a in enumerate(alt)]
+                new = run(*pack(key, some, lat, before, behind), 0, none, 999.0)
+                if new[0] <= now[0] + 0.1 * heat * (1 - trial / moves):
+                    now, chains = new, None
+                    best = min(best, now)
+                continue
+            if not chains:
+                chains = [waits(now, 0), waits(now, 1)]
+                place = {x: k for k, x in enumerate(order)}
+            chain, u = chains[trial & 1], rand()
+            if u < 0.06 or not chain:
+                a = int(rand(n - 12))
+                j, i = order[a], order[a + 1 + int(rand(11))]
+                if above[i] >> j & 1:
+                    continue
+            else:
+                i, j = chain[int(rand(len(chain)))]
+            if u > 0.7:
+                x = i if rand() < 0.5 else j
+                if len(alt[x]) < 2:
+                    continue
+                pick = list(pick)
+                pick[x] = [e for e, c in alt[x] if e != pick[x]][int(rand(len(alt[x]) - 1))]
+                a = place[x]
+            else:
+                a, b, far = place[j], place[i], int(rand() ** 3 * 80)
+                if rand() < 0.5:
+                    a = max(0, a - far)
+                    part, mask = order[a:b + 1], above[i] | 1 << i
+                    order = (order[:a] + [x for x in part if mask >> x & 1]
+                             + [x for x in part if not mask >> x & 1] + order[b + 1:])
+                else:
+                    b = min(n - 1, b + far)
+                    part = order[a:b + 1]
+                    order = (order[:a] + [x for x in part if x != j and not above[x] >> j & 1]
+                             + [x for x in part if x == j or above[x] >> j & 1] + order[b + 1:])
+            bar = now[0] + heat * rand() ** 3 * (1 - trial / moves)
+            new = run(order, pick, a, now[3], bar - 7.0 * MEAN)
+            if new and new[0] <= bar:
+                end, pick = new[3][0], new[2]
+                now, chains = (new[0], sorted(order, key=lambda x: end[x] - c1[x][pick[x]])) + new[2:], None
+                if now[0] < best[0]:
+                    best = now
+    return best
+
+
+def arrange(calls):
+    ops, home = [], []
     for o in calls:
         if o["glue"]:
             p = ops[-1]
@@ -104,260 +251,13 @@ def arrange(ops, rank):
         else:
             ops.append(dict(o, last=o["tile"], after=[home[j] for j in o["after"]]))
         home.append(len(ops) - 1)
-    n = len(ops)
-    rank = rank if SHARE else 0
-    if rank not in PLANS:
-        pred = [[j for j in range(i) if conflict(ops[i], ops[j]) or j in ops[i]["after"]] for i in range(n)]
-        above, before, behind = [0] * n, [], [[] for _ in range(n)]
-        for i in range(n):
-            keep = []
-            for j in reversed(pred[i]):
-                if not above[i] >> j & 1:
-                    queued = ops[i]["e"] == ops[j]["e"] == "g" and j in ops[i]["after"]
-                    keep.append((j, -ops[j]["lat"] if queued else 0.0 if unfenced(ops[i], ops[j]) else GAP))
-                    behind[j].append((i, keep[-1][1]))
-                above[i] |= above[j] | 1 << j
-            before.append(keep)
-        up = [[j for j in range(i) if above[i] >> j & 1] + [i] for i in range(n)]
-        down = [[i] + [j for j in range(i + 1, n) if above[j] >> i & 1] for i in range(n)]
-        alt = [[(e, c) for e, f, c in o["alt"]] for o in ops]
-        lat = [o["lat"] for o in ops]
-        slow = [o["slow"] for o in ops]
-        due = [(i, o["due"], 1.0) for i, o in enumerate(ops) if "due" in o]
-        due += [(i, AIM[o["w"][0][:2]], PULL) for i, o in enumerate(ops) if o["w"] and o["w"][0][:2] in AIM]
-
-        def sweep(key, first, then, back, bias):
-            lo, hi = {e: [] for e in "vatgs-"}, {e: [] for e in "vatgs-"}
-            start, end, pick = [0.0] * n, [0.0] * n, [None] * n
-            left = [len(p) for p in first]
-            ready = sorted((key[i], i) for i in range(n) if not left[i])
-            while ready:
-                i = ready.pop()[1]
-                t0 = 0.0
-                for j, gap in first[i]:
-                    if end[j] + gap > t0:
-                        t0 = end[j] + gap
-                if back:
-                    t0 += lat[i]
-                top = None
-                for e, c in alt[i]:
-                    t, a, b = t0, lo[e], hi[e]
-                    k = m = len(a)
-                    while k and b[k - 1] > t:
-                        k -= 1
-                    while k < m and t + c > a[k] + 1e-9:
-                        t = b[k]
-                        k += 1
-                    v = t + c + (bias[i] if e == "v" else 0.0 if e == "a" else -abs(bias[i]))
-                    if top is None or v < top[0]:
-                        top = (v, t, t + c, e, k)
-                v, start[i], t, e, k = top
-                end[i], pick[i] = t + (0.0 if back else lat[i]), e
-                if e != "-":
-                    lo[e].insert(k, start[i])
-                    hi[e].insert(k, t)
-                more = False
-                for k, gap in then[i]:
-                    left[k] -= 1
-                    if not left[k]:
-                        ready.append((key[k], k))
-                        more = True
-                if more:
-                    ready.sort()
-            return start, end, pick
-
-        def plan(key, bias, again):
-            start, end, pick = sweep(key, before, behind, False, bias)
-            free, late = {}, [0.0] * n
-            for i in sorted(range(n), key=lambda x: (start[x], x)):
-                e = pick[i]
-                t = free.get(e, 0.0)
-                for j, gap in before[i]:
-                    if late[j] + gap > t:
-                        t = late[j] + gap
-                t += (end[i] - start[i] - lat[i]) * slow[i]
-                late[i] = t + lat[i]
-                if e != "-":
-                    free[e] = t
-            one = (max(end) + MIX * max(late) + 0.02 * sum(end) / n + sum(w * max(0.0, start[i] - t) for i, t, w in due),
-                   start, end, pick, bias, max(late))
-            if again:
-                two = plan(sweep(end, behind, before, True, bias)[1], bias, False)
-                one = two if two[0] < one[0] else one
-            return one
-
-        seed = [SEED]
-
-        def rand(m=1.0):
-            seed[0] = (seed[0] * 1103515245 + 12345) % 2147483648
-            return m * seed[0] / 2147483648
-
-        level = [0.0] * n
-        for i in range(n - 1, -1, -1):
-            level[i] = min(c for e, c in alt[i]) + lat[i] + max(
-                [level[k] + gap for k, gap in behind[i]] + [15.0 * ("due" in ops[i])])
-        now = best = plan(level, [0.0] * n, True)
-        tries, moves, heat = TRIES, MOVES, HEAT
-        if PLANS:
-            done = next(iter(PLANS.values()))
-            same = [(done[1][i], done[2][i]) for i, o in enumerate(done[3]) if not o.get("own")]
-            key, bias = [0.0] * n, [0.0] * n
-            for i in range(n - 1, -1, -1):
-                if ops[i].get("own"):
-                    key[i] = max([key[k] + gap for k, gap in behind[i]] + [-KSEND[rank]]) + alt[i][0][1]
-                else:
-                    t, e = same.pop()
-                    key[i], bias[i] = -t, 1.5 if e == "a" else -1.5
-            for i in range(n - 1, -1, -1):
-                key[i] = max([key[i]] + [key[k] + 1e-3 for k, gap in behind[i]])
-            now = best = plan(key, bias, False)
-            tries, moves, heat = 0, MOVES2, HEAT2
-        for trial in range(tries):
-            start, end, pick, bias = now[1:5]
-            key = [-x for x in start]
-            prior, last = {}, {}
-            for i in sorted(range(n), key=lambda x: start[x]):
-                prior[i], last[pick[i]] = last.get(pick[i]), i
-            chain = []
-            i = max(range(n), key=lambda x: end[x])
-            while i is not None and start[i] > 0.2:
-                t, j = max([(end[j] + gap, j) for j, gap in before[i]] + [(0.0, -1)])
-                if t + 0.005 < start[i] or j < 0:
-                    j = prior[i]
-                    if j is not None:
-                        chain.append((i, j))
-                i = j
-            for _ in range(1 + int(rand(2))):
-                u = rand()
-                if u < 0.25 or not chain:
-                    i, x = int(rand(n)), rand(4.0) - 2.0
-                    for j in up[i] if x > 0 else down[i]:
-                        key[j] += x
-                    continue
-                i, j = chain[int(rand(len(chain)))]
-                x = rand(2.0)
-                if u < 0.45:
-                    bias = list(bias)
-                    bias[i if x < 1.0 else j] = (-1.5, -0.3, 0.0, 0.3, 1.5)[int(rand(5))]
-                elif u < 0.65:
-                    for k in down[j]:
-                        key[k] -= x
-                elif u < 0.8:
-                    key[j] -= x
-                else:
-                    for k in up[i if rand() < 0.5 else j]:
-                        key[k] += 1.5 * x
-            new = plan(key, bias, trial % 4 == 0)
-            if new[0] <= now[0] + SLACK * rand() ** 2 * (1 - trial / tries):
-                now = new
-            if new[0] < best[0]:
-                best = new
-        cost = [dict(a) for a in alt]
-
-        slower = [{e: c * slow[i] for e, c in alt[i]} for i in range(n)]
-        rest = [0.0] * n
-        for i in range(n - 1, -1, -1):
-            rest[i] = min(cost[i].values()) + lat[i] + max([rest[k] + gap for k, gap in behind[i]] + [0.0])
-
-        def run(order, pick, cost, a, old, bar):
-            start, end, why = old[0][:], old[1][:], old[2][:]
-            free, last = dict.fromkeys("vatgs-", 0.0), dict.fromkeys("vatgs-")
-            k, left = a, set("vatgs")
-            while k and left:
-                k -= 1
-                i = order[k]
-                if pick[i] in left:
-                    left.discard(pick[i])
-                    free[pick[i]], last[pick[i]] = end[i] - lat[i], i
-            for i in order[a:]:
-                e = pick[i]
-                t, w = free[e], last[e]
-                for j, gap in before[i]:
-                    if end[j] + gap > t:
-                        t, w = end[j] + gap, j
-                if t + rest[i] > bar:
-                    return None
-                start[i], why[i] = t, w
-                t += cost[i][e]
-                end[i] = t + lat[i]
-                if e != "-":
-                    free[e], last[e] = t, i
-            return start, end, why
-
-        def judge(order, pick, at, old, bar):
-            a = run(order, pick, cost, at, old[0], bar - 0.2 - MIX * (old[2] - 0.3))
-            if not a:
-                return None
-            u = max(a[1]) + 0.02 * sum(a[1]) / n + sum(w * max(0.0, a[0][i] - t) for i, t, w in due)
-            b = run(order, pick, slower, at, old[1], (bar - u) / MIX)
-            return b and (u + MIX * max(b[1]), order, pick, (a, b, max(b[1])))
-
-        def waits(times, i):
-            chain = []
-            while times[2][i] is not None:
-                if not above[i] >> times[2][i] & 1:
-                    chain.append((i, times[2][i]))
-                i = times[2][i]
-            return chain
-
-        none = ([0.0] * n, [0.0] * n, [None] * n)
-        now = best = judge(sorted(range(n), key=lambda x: (best[1][x], x)), best[3], 0, (none, none, 0.0), 99.0)
-        chains = None
-        for trial in range(moves):
-            if trial % PACK == 0:
-                bias = [(1.5 if e == "a" else -1.5 if e == "v" else 0.0) * (rand() < 0.9) for e in now[2]]
-                one = plan([-x for x in now[3][0][0]], bias, trial % (2 * PACK) == 0)
-                new = judge(sorted(range(n), key=lambda x: (one[1][x], x)), one[3], 0, (none, none, 0.0), 99.0)
-                if new[0] <= now[0] + 0.1 * heat * (1 - trial / moves):
-                    now, chains = new, None
-                    best = new if new[0] < best[0] else best
-            order, pick = now[1:3]
-            if not chains:
-                chains = [waits(x, x[1].index(max(x[1]))) for x in now[3][:2]]
-                chains += [waits(now[3][0], i) for i, t, w in due if now[3][0][0][i] > t]
-            chain = chains[trial % len(chains)]
-            u = rand()
-            if u < 0.15 or not chain:
-                a = int(rand(n - 12))
-                j, i = order[a], order[a + 1 + int(rand(11))]
-                if above[i] >> j & 1:
-                    continue
-            else:
-                i, j = chain[int(rand(len(chain)))]
-            if u > 0.8:
-                x = i if rand() < 0.5 else j
-                if len(alt[x]) < 2:
-                    continue
-                pick = list(pick)
-                pick[x] = [e for e, c in alt[x] if e != pick[x]][int(rand(len(alt[x]) - 1))]
-                a = order.index(x)
-            else:
-                a, b = order.index(j), order.index(i)
-                far = int(rand() ** 3 * 40)
-                if rand() < 0.5:
-                    a = max(0, a - far)
-                    part = order[a:b + 1]
-                    mask = above[i] | 1 << i
-                    order = (order[:a] + [x for x in part if mask >> x & 1]
-                             + [x for x in part if not mask >> x & 1] + order[b + 1:])
-                else:
-                    b = min(n - 1, b + far)
-                    part = order[a:b + 1]
-                    order = (order[:a] + [x for x in part if x != j and not above[x] >> j & 1]
-                             + [x for x in part if x == j or above[x] >> j & 1] + order[b + 1:])
-            bar = now[0] + heat * rand() ** 3 * (1 - trial / moves)
-            new = judge(order, pick, a, now[3], bar)
-            if new and new[0] <= bar:
-                now, chains = (new[0], sorted(order, key=lambda x: new[3][0][0][x])) + new[2:], None
-                if new[0] < best[0]:
-                    best = new
-        place = {x: k for k, x in enumerate(best[1])}
-        PLANS[rank] = ((max(best[3][0][1]), best[3][2]), [best[3][0][0][x] + 1e-6 * place[x] for x in range(n)],
-                       best[2], ops)
-    score, start, pick = PLANS[rank][:3]
+    if not PLAN:
+        PLAN.extend([improve(ops), ops])
+    order, pick = PLAN[0][1:3]
+    place = {x: k for k, x in enumerate(order)}
     for o, i in zip(calls, home):
-        o["e"], o["f"] = [x[:2] for x in o["alt"] if x[0] == pick[i]][0]
-    return [calls[i] for i in sorted(range(len(calls)), key=lambda x: (start[home[x]], x))]
+        o["e"], o["f"] = [x[:2] for x in o["alt"] if x[0] == QUEUES[pick[i]]][0]
+    return [calls[i] for i in sorted(range(len(calls)), key=lambda x: (place[home[x]], x))]
 
 
 def emit(g, T, ops):
@@ -422,6 +322,7 @@ def rank_program(g, core, T, topo):
     peers = [q for q in range(len(cores)) if q != rank]
     Op, Fn = AluOpType, ActivationFunctionType
     ops = []
+    ZC = 4096 + 32 * rank
 
     def ap(r):
         if r[0] == "ind":
@@ -430,6 +331,9 @@ def rank_program(g, core, T, topo):
 
     def width(r):
         return len(range(r[1], r[2], r[3]))
+
+    def rows(r, p0, p1):
+        return r[:4] + (p0, p1, 1)
 
     def add(e, f, w, r, c, sem=None, inc=0, dma=False, lat=0.0, after=(), alt=None, tile=None):
         ww, rr = [], []
@@ -446,8 +350,8 @@ def rank_program(g, core, T, topo):
         ops.append({"e": e, "f": f, "w": ww, "r": rr, "sem": sem, "inc": inc, "dma": dma, "c": c, "lat": lat,
                     "after": after, "names": names, "banks": names & set(PSUM), "tile": tile,
                     "alt": alt or [(e, f, c)], "glue": False,
-                    "slow": 1.0 if sem else 1.85 if len(rr) > len(r) and w[0][0] == "ind" else
-                    1.65 if any(isinstance(x, tuple) and x[0] == "ind" for x in r) else 1.3})
+                    "slow": 1.0 if sem else SLOW[2] if len(rr) > len(r) and w[0][0] == "ind" else
+                    SLOW[1] if any(isinstance(x, tuple) and x[0] == "ind" for x in r) else SLOW[0]})
         return len(ops) - 1
 
     def glue(n):
@@ -513,14 +417,20 @@ def rank_program(g, core, T, topo):
         alt = [("a", on_a, cost(o, i) + 0.015), ("v", on_v, half(o, i))]
         add("*", on_a, [o], [i, scale, bias], alt[0][2], alt=alt)
 
+    def step(o, i, at, size=1.0):
+        s = size if at else -size
+        alt = [("a", lambda q: q.activation(ap(o), ap(i), Fn.Relu, scale=s, bias=size - s * at), cost(o, i) + 0.015),
+               ("v", lambda q: q.tensor_scalar(ap(o), ap(i), float(at), size, Op.is_equal, Op.mult), half(o, i))]
+        add("*", alt[0][1], [o], [i], alt[0][2], alt=alt)
+
     def fill(o, c):
         src = A("onesb", 0, width(o), 1, o[4], o[5])
-        if SB[o[0]][1] == F16:
-            return aff(o, src, float(c))
         alt = [("a", lambda q: q.activation(ap(o), ap(src), Fn.Identity, scale=float(c)), cost(o, o) + 0.015),
                ("v", lambda q: q.memset(ap(o), c), half(o, o)),
                ("g", lambda q: q.iota(ap(o), [[0, width(o)]], int(c), 0, allow_small_or_imprecise_dtypes=True),
                 0.16 + width(o) * 2 * VEC)]
+        if SB[o[0]][1] == I32:
+            return add("*", alt[1][1], [o], [], alt[1][2], alt=alt[1:])
         add("*", alt[0][1], [o], [src], alt[0][2], alt=alt)
 
     def mm(o, l, r, start=True, stop=True):
@@ -535,34 +445,37 @@ def rank_program(g, core, T, topo):
         add("g", lambda q: q.affine_select(ap(o), ap(i), pat, cmp, 0.0, base, cm), [o], [i],
             0.21 + width(o) * 2 * VEC)
 
-    def load(e, o, src, sem, lat, r=(), c=0.06):
+    def move(o, i):
+        asel(o, i, [[0, width(o)]], Op.is_ge, 0, 0)
+        on_g = ops.pop()["alt"]
+        aff(o, i)
+        ops[-1]["alt"] += on_g
+
+    def load(e, o, src, sem, lat, r=()):
         def f(q):
             return q.dma_start(ap(o), src)
-        return add(e[0], f, [o], list(r), c, sem, 16, True, lat, alt=[(x, f, c) for x in e])
+        return add(e[0], f, [o], list(r), DMAC, sem, 16, True, lat, alt=[(x, f, DMAC) for x in e])
 
-    def store(e, dst, i, sem):
-        add(e, lambda q: q.dma_start(dst, ap(i)), [], [i], 0.06, sem, 16, True, 2.2)
+    def store(e, dst, i, sem, behind=()):
+        add(e, lambda q: q.dma_start(dst, ap(i)), [], [i] + list(behind), DMAC, sem, 16, True, LOCAL)
 
     def slot(at, q):
         return q if q < at else q - 1
 
     def share(at, q, w):
-        en = topo.engines(cores[at], cores[q])[::STEP]
+        en = topo.engines(cores[at], cores[q])
         return en[:w] if 3 * w > len(en) else en[slot(at, q):3 * w:3]
 
-    def transfer(src, to, sem, en):
-        ids = [DstId(rid=topo.addr(cores[q])[0], pnc=topo.addr(cores[q])[1]) for q, d in to]
-        return RemoteDMATransfer(dst_ids=ids, dma_engine_mask=sum(1 << e for e in en), remote_sem=T.sem[sem],
-                                 srcs=[ap(src)], dsts=[ap(d) for q, d in to])
+    def fused(trs, c):
+        tr = [RemoteDMATransfer(dst_ids=[DstId(rid=topo.addr(cores[q])[0], pnc=topo.addr(cores[q])[1])],
+                                dma_engine_mask=sum(1 << e for e in en), remote_sem=T.sem[sem],
+                                srcs=[ap(src)], dsts=[ap(dst)]) for src, q, dst, sem, en in trs]
+        return add("g", lambda x: x.remote_dma_fused(tr, local_sem=T.sem.sent), [], [t[0] for t in trs], c,
+                   "sent", sum(len(t[4]) for t in trs), lat=REMOTE)
 
-    def fused(trs, c, sem="sent"):
-        tr = [transfer(*t) for t in trs]
-        return add("g", lambda x: x.remote_dma_fused(tr, local_sem=T.sem[sem]), [], [t[0] for t in trs], c,
-                   sem, sum(len(t[3]) for t in trs), lat=2.3)
-
-    def wrap8(o, c, src, n, start=True):
+    def wrap8(o, c, src, n):
         for b in range(8):
-            mm(o, A(c, 7 - b, 135 - b), A(src[0], src[1] + b, src[1] + n, 8), start and b == 0, b == 7)
+            mm(o, A(c, 7 - b, 135 - b), A(src[0], src[1] + b, src[1] + n, 8), b == 0, b == 7)
         glue(8)
 
     def wrap4(o, c, c0, src, start):
@@ -575,209 +488,180 @@ def rank_program(g, core, T, topo):
             mm(o, A("c3", 15 - b, 143 - b), A(src, b, 512, 16), start and b == 0, b == 15)
         glue(16)
 
-    def digits(li, cr, cu, n):
-        ts(A(cr, n, 2 * n), A(li), 15, Op.bitwise_and)
-        ts(A(cr, 0, n), A(li), 4, Op.logical_shift_right)
-        copy(A(cu), A(cr))
-
     def wo(o):
         return A("wo", 512 * (o // 4) + o % 4, 512 * (o // 4) + 512, 4)
 
     def block(gr):
         return 4 * (gr % 2) + gr // 2
 
-    (rcol, kcol, hcol, g8col, acol, jcol, h0col, ccol, b1col, sbcol, k6col, zc0, zc, r8col, h35, bcol,
-     dcol, lxcol, ecol, q0col, q1col, k6f, pcol, gcol, onec, rhalf, nsb, sbz, pw, k67, hp,
-     xt, x1, x2, x3, d32, d33, a0, wcol, r1col, w0, j0, j1) = [A("col", i, i + 1) for i in range(43)]
-    rtcol, rdcol, rsb, zsb = [A("late", i, i + 1) for i in range(4)]
-    m63, hneg = A("col", 44, 45), A("col", 43, 44)
-    ident, shift = A("idw", 1, 129), A("idw", 0, 128)
+    (g8col, rcol, kcol, hcol, acol, jcol, code, pcol, ccol, b1col, k6col, zc0, zc, h35, bcol, lxcol, ecol, q0col,
+     q1col, gcol, onec, rhalf, nsb, sbz, pw, k67, hp, xt, x1, x2, d32, d33, wcol, r1col, e63, m63, rdcol,
+     rsb) = [A("col", i, i + 1) for i in range(38)]
+    ident, pi = A("idw", 1, 129), A("pk", 23, 24)
 
-    iota(A("pi", 0, 1), [[0, 1]], 0, 1)
+    iota(pi, [[0, 1]], 0, 1)
     iota(A("idb"), [[32, 2], [1, 32]], 0, 32)
     for h in range(2):
-        load("sa", A("x0", 16 * h, 16 * h + 16), T.x[0, 2048 * h:2048 * h + 2048], "lx0", 2.0)
-    load("sa", A("bdi", p1=16), T.bd[:, :], "lbd", 1.9)
+        load("sa", A("x0", 16 * h, 16 * h + 16), T.x[0, 2048 * h:2048 * h + 2048], "lx0", LOCAL - 0.2)
+    load("sa", A("bdi", p1=16), T.bd[:, :], "lbd", LOCAL - 0.3)
     for k in range(8):
         c = 512 * block(k)
-        load("sa", A("xn", 16, 528, 1, 16 * k, 16 * k + 16), T.x[:, c:c + 512], "lxn", 2.2)
-    for k in range(8):
-        c = 512 * block(k)
-        load("sa", A("d1", 16, 528, 1, 16 * k, 16 * k + 12, 2), T.nb[:, c:c + 512], "lnb", 2.2)
+        load("sa", A("d1", 16, 528, 1, 16 * k, 16 * k + 12, 2), T.nb[:, c:c + 512], "lnb", LOCAL)
     for h in range(2):
-        load("s", A("d1", 16, 528, 1, 12 + 2 * h, 128, 16), ap(A("idb", 32 * h, 32 * h + 32)), "lnb", 2.0, [A("idb")])
-        load("sa", A("d1", 16, 528, 1, 64 * h + 1, 64 * h + 64, 2), T.nb[0:4, :], "lnb", 2.2)
+        load("s", A("d1", 16, 528, 1, 12 + 2 * h, 128, 16), ap(A("idb", 32 * h, 32 * h + 32)), "lnb", LOCAL - 0.2,
+             [A("idb")])
+        load("sa", A("d1", 16, 528, 1, 64 * h + 1, 64 * h + 64, 2), T.nb[0:4, :], "lnb", LOCAL)
+    load("sa", A("xs", 16, 4112, p1=16), T.x[:, :], "lxs", LOCAL + 0.2)
+    small = [i for i, o in enumerate(ops) if o["dma"]]
     for k in range(7):
-        load("s", A("xw", 0, 4096, 1, 16 * k, 16 * k + 16), T.x[:, :], "lx", LX)
+        ops[load("sa", A("xw", 0, 4096, 1, 16 * k, 16 * k + 16), T.x[:, :], "lx", LOCAL + 1.5)]["after"] = small
 
     memset(A("onesb"), 1.0)
     for c in (0, 528):
-        memset(A("d1", c, c + 16), 0)
-        fill(A("xn", c, c + 16), 0.0)
+        fill(A("d1", c, c + 16), 0)
     iota(A("iom"), [[0, 8], [1, 16]], 0, 0)
-    iota(A("iou"), [[2, 256]], -256, 0)
     iota(A("iog"), [[1, 9], [0, 16]], 0, 0)
     iota(A("iob"), [[1, 4], [4, 2], [0, 16]], 0, 0)
     iota(A("dc"), [[128, 32]], DUM, 8)
     for c in range(128, 640, 128):
         fill(A("w1", c, c + 128), 0.0)
-    fill(A("sc", 0, 1), 0.0)
-    fill(A("sel"), -65536.0)
-    fill(A("xw", ZC, 4232), 0.0)
-    fill(A("xw", 4096 + 32 * rank, 4128 + 32 * rank), 0.0)
-    for c in ("c1", "b2"):
+    fill(A("sc", 0, 40, 39), 0.0)
+    fill(A("sel"), -49152.0)
+    fill(A("xw", ZC, ZC + 32), 0.0)
+    for c in ("c1", "b2", "lf", "dw", "ew", "c2", "c3", "c5"):
         fill(A(c), 0.0)
-    fill(A("gg", 96, 128), 0.0)
-    fill(A("tm", 512, 520), DUM / 16.0)
-    fill(A("nw", 264, 272), 8000.0)
+    for c in (0, 144):
+        fill(A("fw", c, c + 144), 0.0)
     fill(A("t1", TB + ROOT + 512, TB + ROOT + 4 * RS, RS), 0.0)
-    fill(A("nw2", 320, 360), float(DUM))
-    ts(A("pk", 0, 1), A("pi", 0, 1), 15, Op.bitwise_and)
-    ts(A("pk", 1, 2), A("pi", 0, 1), 4, Op.logical_shift_right)
-    ts(A("pk", 2, 3), A("pi", 0, 1), 4, Op.logical_shift_right, 1, Op.bitwise_and)
-    ts(A("pk", 3, 4), A("pi", 0, 1), 7, Op.bitwise_and)
-    ts(A("pk", 4, 5), A("pi", 0, 1), 6, Op.logical_shift_right)
-    ts(A("pk", 5, 6), A("pi", 0, 1), 63, Op.bitwise_and)
-    copy(A("col", 0, 6), A("pk", 0, 6))
+    ts(A("pk", 16, 17), pi, 7, Op.bitwise_and)
+    ts(A("pk", 17, 18), pi, 15, Op.bitwise_and)
+    ts(A("pk", 18, 19), pi, 4, Op.logical_shift_right)
+    ts(A("pk", 19, 20), pi, 4, Op.logical_shift_right, 1, Op.bitwise_and)
+    ts(A("pk", 20, 21), pi, 6, Op.logical_shift_right)
+    ts(A("pk", 21, 22), pi, 63, Op.bitwise_and)
+    ts(A("pk", 22, 23), pi, 3, Op.logical_shift_right)
+    aff(A("col", 0, 8), A("pk", 16, 24))
+    iota(A("pk", 0, 8), [[4, 2], [-2, 2], [1, 2]], 2, 0)
+    iota(A("pk", 8, 16), [[1, 8]], 0, 0)
     ts(A("bo"), A("iog", 0, 136), kcol, Op.is_equal)
     ts(A("prev"), A("iog", 0, 128), kcol, Op.is_gt)
     scan(A("io128"), A("onesb", 0, 136), A("onesb", 0, 136), Op.add, Op.mult, -2.0)
-    copy(pcol, A("pi", 0, 1))
     ts(A("trb"), A("io128", 1, 129), pcol, Op.is_gt, -1.0, Op.mult)
     ts(A("idw"), A("io128"), pcol, Op.is_equal)
     aff(h35, hcol, 3.5)
     aff(bcol, kcol, 0.5, h35)
     ts(A("prev1"), A("iob"), bcol, Op.is_gt)
-    ts(dcol, bcol, kcol, Op.subtract, 512.0, Op.mult)
     aff(lxcol, bcol, -512.0, 16.0)
     ts(A("rf"), A("iom"), rcol, Op.is_equal)
-    ts(A("eef", p1=16), A("iom", p1=16), A("col", 0, 1, p1=16), Op.is_equal)
     asel(A("tri"), A("onesb", 0, 128), [[0, 2], [1, 64]], Op.is_gt, 0, -1)
-    aff(h0col, hcol, -1.0, 1.0)
-    aff(A("ee", 0, 128), A("rf"), h0col)
+    ts(A("ee", 0, 128), A("rf"), hcol, Op.subtract, 0.0, Op.max)
     aff(A("ee", 128, 256), A("rf"), hcol)
     ts(A("i16"), A("iom", 0, 16), rcol, Op.is_equal)
-    ts(onec, A("i16", 14, 15), A("i16", 12, 13), Op.subtract, 1.0 / 32, Op.mult)
-    aff(ccol, onec, -float(ZC))
+    ts(onec, A("i16", 14, 15), A("i16", 12, 13), Op.subtract, 16.0, Op.mult)
+    aff(ccol, onec, -ZC / 512.0)
     aff(rhalf, rcol, 0.5)
     ts(A("c1", 7, 112, 8), A("iog", 0, 112, 8), rhalf, Op.is_equal, ccol, Op.add)
-    aff(ecol, onec, dcol)
-    ts(A("c1", 103, 112, 8), A("c1", 103, 112, 8), ecol, Op.add)
-    copy(A("io8", 0, 8), A("iom", 0, 8))
-    copy(A("io8", 8, 9), A("pk", 3, 4))
+    ts(ecol, bcol, kcol, Op.subtract, onec, Op.mult)
+    aff(A("c1", 103, 112, 8), A("c1", 103, 112, 8), None, ecol)
     memset(A("obi", 0, 9, p0=96), 0)
     for d in range(3):
-        ts(A("obi", 0, 9, 1, 32 * d, 32 * d + 32), A("io8", 0, 9, 1, 32 * d, 32 * d + 32), 1 << d, Op.bitwise_and)
-    ts(b1col, rcol, 8.0, Op.is_lt, 98304.0, Op.mult)
-    aff(sbcol, b1col, 1.0 / 3)
-    aff(A("sel", 1, 128, 2), A("sel", 0, 128, 2), None, b1col)
-    aff(sbz, sbcol, None, -float(ZC))
+        ts(A("obi", 0, 9, 1, 32 * d, 32 * d + 32), A("pk", 8, 17, 1, 32 * d, 32 * d + 32), 1 << d, Op.bitwise_and)
+    ts(b1col, rcol, 8.0, Op.is_lt, 65536.0, Op.mult)
+    aff(A("sel", 1, 80, 2), A("sel", 0, 80, 2), None, b1col)
+    aff(sbz, b1col, 0.25, -float(ZC))
     aff(pw, A("obi", 7, 8), float(ST))
-    ts(k67, kcol, 6.0, Op.is_ge)
+    aff(k67, A("prev", 96, 97), -1.0, 1.0)
     aff(hp, pw, hcol, k67)
     ts(A("obt", 0, 9), A("obi", 0, 9), float(ST), Op.mult, hp, Op.is_equal)
-    ts(k6f, kcol, 6.0, Op.is_equal)
-    aff(k6col, k6f, 0.625)
+    aff(k6col, A("bo", 96, 97), 0.625)
+    fill(A("xs", 0, 16), 0.0)
+    memset(A("lx", 8, 16), 0)
+    aff(A("eef", p1=16), A("rf", p1=16))
     aff(A("m8", 0, 8), A("obt", 0, 8), 0.125, k6col)
-    ts(m63, jcol, 63.0, Op.not_equal, -1.0, Op.mult)
-    ts(A("back"), A("io128", 0, 128), pcol, Op.is_equal, m63, Op.mult)
-    aff(hneg, acol, -1.0, -256.0)
-    ts(A("uu"), A("iou"), hneg, Op.subtract)
-    for c in ("lf", "dw"):
-        fill(A(c), 0.0)
+    step(e63, jcol, 63, float(BIG))
+    aff(m63, e63, 1.0 / BIG, -1.0)
+    aff(A("back"), A("idw", 0, 128), m63)
+    for c in range(0, 512, 128):
+        aff(A("un", c, c + 128), A("io128", 1, 129), None, float(c))
+        aff(A("tw", 512 + c, 640 + c), A("un", c, c + 128), 1.0 / 16)
+    aff(A("uu"), A("un", 0, 512, 2), None, acol)
     asel(A("pm", 0, 128), A("onesb", 0, 128), [[-64, 2], [16, 4], [-1, 16]], Op.is_equal, -48, 1)
     asel(A("pm", 128, 256), A("onesb", 0, 128), [[64, 2], [32, 2], [-1, 32]], Op.is_equal, -96, 1)
-    ts(A("rfb"), A("iom"), rcol, Op.is_equal, float(DUM), Op.mult)
-    ts(A("th8"), A("iom", 0, 8), kcol, Op.not_equal, -1000.0, Op.mult)
-    aff(j0, rcol, None, 512.0)
-    aff(j1, rcol, None, 480.0)
-    aff(A("e0"), A("onesb", 0, 8), A("i16", 0, 1))
+    aff(A("rfb"), A("rf"), float(DUM))
+    aff(A("th8"), A("bo", 0, 128, 16), 1000.0, -1000.0)
+    aff(A("th64"), A("bo", 0, 128, 2), 1100.0, -1000.0)
+    ts(A("i8"), A("iom", 0, 8), g8col, Op.is_equal)
     for c in (7, 71):
         aff(A("b2", c, c + 57, 8), A("m8", 0, 8), A("i16", 0, 1))
     for o in range(8):
         aff(wo(o), A("rf"), A("m8", o, o + 1))
     cut = min(2 + 2 * rank, 6)
-    aff(A("jn", 0, cut), A("iom", 0, cut), 16.0, j0)
-    aff(A("jn", cut, 8), A("iom", cut, 8), 16.0, j1)
-
-    first = len(ops)
-    builds = [rank] if SHARE else range(4)
-    if 0 in builds:
-        for c in range(0, 432, 144):
-            fill(A("fw", c, c + 144), 0.0)
-        iota(A("ioo"), [[0, 2], [1, 8], [32, 8]], 0, 0)
-        aff(xt, A("obi", 8, 9), -2.0 * ST, pw)
-        aff(x2, g8col, float(ST), xt)
-        ts(x3, A("obt", 8, 9), float(ROOT), Op.mult, x2, Op.max)
-        aff(x1, A("obt", 8, 9), -float(RS), float(RS))
-        for i, x in enumerate((x1, x3, x2)):
-            aff(A("xr", 9 * i, 9 * i + 9), A("bo", 0, 136, 16), x)
-        aff(r1col, rcol, None, 1.0)
-        ts(A("la", 0, 128), A("ioo"), rcol, Op.is_equal)
-        ts(A("la", 128, 256), A("ioo"), r1col, Op.is_equal, -1.0, Op.mult)
-        mm(A("p1", 0, 27), A("la", 0, 128), A("xr", 0, 27), True, False)
-        mm(A("p1", 0, 27), A("la", 128, 256), A("xr", 0, 27), False, True)
-        ts(a0, g8col, 0.0, Op.is_equal)
-        aff(d33, a0, -512.0, 64.0)
-        ts(wcol, jcol, 0.0, Op.is_equal)
-        aff(d32, wcol, 448.0, d33)
-        for h in range(2):
-            p = (64 * h, 64 * h + 64)
-            aff(A("fw", 14 + h, 288, 16, *p), A("p1", 0, 18, 1, *p), None, d32[:4] + p + (1,))
-            aff(A("fw", 302 + h, 432, 16, *p), A("p1", 18, 27, 1, *p))
-        glue(4)
-    if 1 in builds or 2 in builds:
-        copy(A("lj", 0, 8), A("iom", 0, 8))
-    if 1 in builds:
-        iota(A("io2", 8, 16), [[4, 2], [-2, 2], [1, 2]], 2, 0)
-        copy(A("lj", 8, 16), A("io2", 8, 16))
-        ts(zc0, kcol, 6.0, Op.is_lt, 1.0 / 64, Op.mult)
-        aff(zc, k6col, 0.625, zc0)
-        aff(A("m8", 16, 24), A("obt", 0, 8), 3.0 / 64, zc)
-        tt(A("wc"), ind(A("m8", 0, 8), A("lj", 8, 16)), A("rf"), Op.mult)
-        tt(A("wz"), ind(A("m8", 16, 24), A("lj", 0, 8)), A("rf"), Op.mult)
-    if 2 in builds:
-        aff(A("m8", 24, 32), A("obt", 0, 8), -1.0, 1.0)
-        aff(A("m8", 24, 32, 1, 32, 64), A("obt", 0, 8, 1, 32, 64))
-        tt(A("r3"), ind(A("m8", 24, 32), A("lj", 0, 8)), A("rf"), Op.mult)
-        for d in range(4):
-            st, base = [4 * ST, 2 * ST, ST], 0
-            if d < 3:
-                base += st[2 - d]
-                st[2 - d] = -st[2 - d]
-            iota(A("b8", 8 * d, 8 * d + 8), [[st[0], 2], [st[1], 2], [st[2], 2]], base, 0)
-        aff(rsb, sbcol, -1.0, float(ROOT))
-        ts(gcol, kcol, hcol, Op.subtract, 4.0, Op.mult)
-        aff(rdcol, gcol, RS / 8.0, float(RS))
-        iota(A("ci"), [[512, 2], [16, 8]], 512, 8)
-        aff(w0, rcol, -7.0)
-        aff(A("cc"), A("ci"), None, w0)
-        ts(r8col, rcol, 8.0, Op.is_ge)
-        aff(q1col, r8col, 2.0, 17.0)
-        aff(q0col, A("obt", 8, 9), -16.0, q1col)
-        aff(nsb, sbcol, -1.0)
-        ts(A("lq", 0, 4), A("iom", 0, 4), 4.0, Op.mult, q0col, Op.add)
-        ts(A("lq", 4, 8), A("iom", 0, 4), 4.0, Op.mult, q1col, Op.add)
-        ts(A("lp"), A("onesb", 0, 4), g8col, Op.mult, gcol, Op.add)
-        aff(A("b64"), ind(A("b8"), A("lp")), None, nsb)
-    if 3 in builds:
-        fill(A("ew"), 0.0)
-        ts(a0, jcol, 63.0, Op.is_equal, float(BIG), Op.mult)
-        ts(wcol, a0, 1.0, Op.max)
-        aff(d33, acol, -1.0, 1.0)
-        ts(A("ew", 14, 128, 16), A("onesb", 0, 8), wcol, Op.mult, d33, Op.mult)
-        ts(A("ew", 15, 128, 16), A("onesb", 0, 8), wcol, Op.mult, acol, Op.mult)
-        for c in ("c2", "c5"):
-            fill(A(c), 0.0)
-        aff(A("c2", 7, 128, 8), A("bo", 0, 128, 8))
-        fill(A("c3"), 0.0)
-        aff(A("c3", 15, 128, 16), A("bo", 0, 128, 16))
-        aff(A("c5", 7, 128, 8), A("onesb", 0, 16), k6f)
-        ts(A("pk", 6, 7), A("pi", 0, 1), 3, Op.logical_shift_right)
-        aff(d32, A("pk", 6, 7), 2.0, pcol)
-        ts(A("r80"), A("io128", 1, 81), d32, Op.is_equal)
-    for o in ops[first:]:
-        o["own"] = SHARE
+    aff(A("jn", 0, cut), A("io128", 33, 33 + cut), 16.0, rcol)
+    aff(A("jn", cut, 8), A("io128", 31 + cut, 39), 16.0, rcol)
+    iota(A("ioo"), [[0, 2], [1, 8], [32, 8]], 0, 0)
+    aff(xt, A("obi", 8, 9), -2.0 * ST, pw)
+    aff(x2, g8col, float(ST), xt)
+    aff(x1, A("obt", 8, 9), -512.0, 512.0)
+    for i, x in enumerate((x1, x2)):
+        aff(A("xr", 9 * i, 9 * i + 9), A("bo", 0, 136, 16), x)
+    aff(r1col, rcol, None, 1.0)
+    ts(A("la", 0, 128), A("ioo"), rcol, Op.is_equal)
+    ts(A("la", 128, 256), A("ioo"), r1col, Op.is_equal, -1.0, Op.mult)
+    mm(A("p1", 0, 18), A("la", 0, 128), A("xr", 0, 18), True, False)
+    mm(A("p1", 0, 18), A("la", 128, 256), A("xr", 0, 18), False, True)
+    aff(d33, A("i8", 0, 1), -512.0, 64.0)
+    step(wcol, jcol, 0)
+    aff(d32, wcol, 448.0, d33)
+    for h in range(2):
+        p = (64 * h, 64 * h + 64)
+        aff(A("fw", 14 + h, 144, 16, *p), A("p1", 0, 9, 1, *p), None, rows(d32, *p))
+        aff(A("fw", 158 + h, 288, 16, *p), A("p1", 9, 18, 1, *p))
+    glue(4)
+    for h in range(2):
+        p = (64 * h, 64 * h + 64)
+        aff(A("ew", 14 + h, 128, 16, *p), A("onesb", 0, 8, 1, *p), rows(e63, *p), 1.0)
+    aff(A("c2", 7, 128, 8), A("bo", 0, 128, 8))
+    aff(A("c3", 15, 128, 16), A("bo", 0, 128, 16))
+    aff(A("c5", 7, 128, 8), A("bo", 96, 112))
+    iota(A("ix", 0, 32), [[0, 2], [2, 8], [-1, 2]], 1, 0)
+    for k in range(2, 6):
+        iota(A("ix", 16 * k, 16 * k + 16), [[[4, 4], [-2, 2], [1, 2]], [[8, 2], [-4, 2], [1, 4]]][k // 4], 1 << k // 2, 0)
+    aff(A("ix", 96, 104), A("iom", 0, 8))
+    ts(A("e1"), A("ix", 0, 96), code, Op.is_equal)
+    tt(A("dd", 1, 96), A("e1", 1, 96), A("e1", 0, 95), Op.subtract)
+    aff(A("dd", 0, 96, 8), A("e1", 0, 96, 8))
+    fill(A("wt", 768, 800), 0.0)
+    for r in range(8):
+        aff(A("wt", 96 * r, 96 * r + 96), A("dd"), A("i8", r, r + 1))
+    asel(A("th"), A("onesb", 0, 128), [[0, 16], [8, 8]], Op.is_gt, 0, -1)
+    for c in ("qw", "tw"):
+        aff(A(c, 1120, 1121), A("i8", 0, 1), float(DUM))
+    iota(A("xi", p1=64), [[128, 6], [1, 16]], 512 - TB, 2)
+    aff(A("xg", p1=64), A("xi", p1=64))
+    copy(A("lj"), A("pk", 0, 16))
+    aff(zc0, A("prev", 96, 97), 1.0 / 64)
+    aff(zc, k6col, 0.625, zc0)
+    aff(A("m8", 16, 24), A("obt", 0, 8), 3.0 / 64, zc)
+    tt(A("wc"), ind(A("m8", 0, 8), A("lj", 0, 8)), A("rf"), Op.mult)
+    tt(A("wz"), ind(A("m8", 16, 24), A("lj", 8, 16)), A("rf"), Op.mult)
+    aff(A("m8", 24, 32), A("obt", 0, 8), -1.0, 1.0)
+    aff(A("m8", 24, 32, 1, 32, 64), A("obt", 0, 8, 1, 32, 64))
+    tt(A("r3"), ind(A("m8", 24, 32), A("lj", 8, 16)), A("rf"), Op.mult)
+    ts(gcol, kcol, hcol, Op.subtract, 16.0, Op.mult)
+    aff(rsb, b1col, -0.25, float(ROOT))
+    aff(rdcol, gcol, RS / 32.0, float(RS))
+    aff(q1col, b1col, -2.0 / 65536, 19.0)
+    aff(q0col, A("obt", 8, 9), -16.0, q1col)
+    aff(nsb, b1col, -0.25)
+    ts(A("lq", 0, 4), A("iom", 0, 4), 4.0, Op.mult, q0col, Op.add)
+    ts(A("lq", 4, 8), A("iom", 0, 4), 4.0, Op.mult, q1col, Op.add)
+    ts(A("lp"), A("onesb", 0, 4), g8col, Op.mult, gcol, Op.add)
+    aff(A("b64"), ind(A("ix"), A("lp")), float(ST), nsb)
+    aff(A("sto"), A("iom", 0, 128, 2), ST / 2.0, nsb)
+    for o in ops:
+        if not o["dma"]:
+            o["alt"] = [(e, f, c * (EARLY if e in "va" else 1.0)) for e, f, c in o["alt"]]
+            o["slow"] /= EARLY
 
     add("v", lambda q: q.transpose(ap(A("xt")), ap(A("x0"))), [A("xt")], [A("x0")], 64 * VEC)
     ts(A("nf"), A("xt"), 0.0, Op.is_le)
@@ -794,53 +678,76 @@ def rank_program(g, core, T, topo):
     ts(A("off"), p1, pc, Op.add, rcol, Op.add)
     ts(A("offh"), p1, pc, Op.add, rcol, Op.add)
 
-    copy(A("bdg", p1=16), A("bdi", p1=16))
+    aff(A("bdg", p1=16), A("bdi", p1=16))
     mm(A("pz", 0, 8), A("eef", p1=16), A("bdg", p1=16))
-    ts(A("lx"), A("pz", 0, 8), lxcol, Op.add, 528.0, Op.min)
-    aff(A("xa"), ind(A("xn"), A("lx")))
-    mm(A("pz", 128, 256), A("rf"), A("xa"))
-    aff(A("xb"), A("pz", 128, 256))
-    sa = fused([(A("xb", 32 * q, 32 * q + 32), [(q, A("xw", 4096 + 32 * rank, 4128 + 32 * rank))], "arra",
-                 share(rank, q, AENG)) for q in peers], FIRST)
+    ts(A("lx", 0, 8), A("pz", 0, 8), lxcol, Op.add, 528.0, Op.min)
+    ts(A("lx", 8, 16, p1=16), A("bdi", p1=16), 16.0, Op.add)
+    aff(A("xa"), ind(A("xs"), A("lx", 8, 16)))
+    mm(A("p0", 0, 128), A("rf", p1=16), A("xa", p1=16))
+    aff(A("xb"), A("p0", 0, 128))
+    sa = fused([(A("xb", 32 * q, 32 * q + 32), q, A("xw", ZC, ZC + 32), "arra", share(rank, q, AENG)) for q in peers],
+               FIRST)
     add("-", None, [A("xw", 4096 + 32 * q, 4128 + 32 * q) for q in peers], [], 0.0, "arra", 3 * AENG, after=(sa,))
-    if SHARE:
-        mine = A(SHARED[rank])
-        sk = fused([(mine, [(q, mine) for q in peers], "arrk%d" % rank, topo.engines(core, cores[peers[0]])[-KENG:])],
-                   KCALL)
-        ops[sk].update(after=(sa,), due=KSEND[rank])
-        for q in peers:
-            soon = add("-", None, [], [], 0.0, lat=KARR[q])
-            add("-", None, [A(SHARED[q])], [], 0.0, "arrk%d" % q, KENG, after=(sk, soon))
     banks = ["p0", "p1", "p2"]
 
-    mm(A("p0", 0, 8), A("xw", 4096, ZC, p1=16), A("e0", p1=16))
-    tt(A("nfb"), A("p0", 0, 8), A("th8"), Op.is_le)
-    mm(A("p0", 8, 16), A("rfb"), A("nfb"))
-    tt(A("nw", 256, 264), A("p0", 8, 16), A("jn"), Op.add)
+    mm(A("pz", 0, 8), A("xw", 4096, 4224, p1=16), A("rf", 0, 128, 16, p1=16))
+    tt(A("nfb"), A("pz", 0, 8), A("th8"), Op.is_le)
+    mm(A("pz", 8, 16), A("rfb"), A("nfb"))
+    tt(A("nw", 256, 264), A("pz", 8, 16), A("jn"), Op.add)
 
-    aff(A("w1", 0, 128), ind(A("d1"), A("lx")))
+    aff(A("w1", 0, 128), ind(A("d1"), A("lx", 0, 8)))
     wrap8(A("pc", 0, 16), "c1", A("w1"), 128)
-    for a, b in zip(SPLIT, SPLIT[1:]):
-        copy(ind(A("w1", 128), A("off", a, b)), A("d1", 16 + 16 * a, 16 + 16 * b))
+    copy(ind(A("w1", 128), A("off")), A("d1", 16, 528))
     for gr in range(8):
         lo, c = (32 * (gr // 2), 32 * (gr // 2) + 32), 128 * (gr % 2)
         mm(A("pd", 32 * block(gr), 32 * block(gr) + 32), A("ee", c, c + 128, 1, *lo), A("offh", 0, 32, 1, *lo))
         glue(1 + gr % 2)
     aff(A("nw", 0, 256), A("pd", 0, 256))
     wrap8(A("pc", 16, 80), "c1", A("w1", 128), 512)
-    scan(A("sw", 0, 80), A("sel", 0, 80), A("pc", 0, 80), Op.add, Op.max)
+    scan(A("sw"), A("sel"), A("pc", 0, 80), Op.add, Op.max)
     ts(A("l1u"), A("sw", 1, 80, 2), sbz, Op.subtract)
     aff(A("gs"), ind(A("xw"), A("l1u", 0, 8)))
     ts(A("li"), A("sw", 1, 80, 2), sbz, Op.subtract)
-    digits("li", "lcr", "lcu", 40)
+    ts(A("lcr", 40, 80), A("li"), 15, Op.bitwise_and)
+    ts(A("lcr", 0, 40), A("li"), 4, Op.logical_shift_right)
+    copy(A("lcu"), A("lcr"))
     for h in range(2):
         aff(A("gw", 256 * h, 256 * h + 256), ind(A("xw"), A("l1u", 8 + 16 * h, 24 + 16 * h)))
     gw = A("gw")
 
-    sb = fused([(A("gs", 32 * q, 32 * q + 32), [(q, A("gg", 32 * slot(q, rank), 32 * slot(q, rank) + 32))], "arrb",
+    sb = fused([(A("gs", 32 * q, 32 * q + 32), q, A("gg", 32 * slot(q, rank), 32 * slot(q, rank) + 32), "arrb",
                  share(rank, q, BENG)) for q in peers], BCALL)
-    add("-", None, [A("gg", 0, 96)], [], 0.0, "arrb", 3 * BENG, after=(sb,))
-    ops[sb]["due"] = BSEND
+    add("-", None, [A("gg")], [], 0.0, "arrb", 3 * BENG, after=(sb,))
+
+    asel(A("t1", TB + ROOT, TB + ROOT + 512), gw, [[0, 512]], Op.is_ge, 0, 0)
+    for d in range(3):
+        for f in range(8):
+            q = 2 * d + 1 - ((f ^ 2) >> d & 1)
+            src = A("t1", TB + ROOT, TB + ROOT + 512, 1, 16 * q, 16 * q + 16)
+            c = TB + ROOT + RS * (d + 1)
+            load("sa", A("t1", c, c + 512, 1, 16 * f, 16 * f + 16), ap(src), "lrt", LOCAL + 1.0, [src])
+            glue(1 + f % 2)
+    mm(A(banks[2]), A("wo", 0, 128), gw)
+    aff(A("yt"), A(banks[2]))
+    for o in range(8):
+        c = TB + ST * o
+        if o < NDMA:
+            src = A("yt", 0, 512, 1, o, 128, 4)
+            for f in range(0, 128, 32):
+                load("s", A("t1", c, c + 512, 1, f, f + 32), ap(src), "lt1", LOCAL - 0.2, [src])
+            glue(4)
+            continue
+        mm(A(banks[o % 2]), wo(o), gw)
+        aff(A("t1", c, c + 512), A(banks[o % 2]))
+
+    for i in range(4):
+        mm(A(BK["nf"], 16 * i, 16 * i + 16), A("gs"), A("b2", 7, 135, 8))
+    glue(4)
+    tt(A("nfs"), A(BK["nf"], 0, 64), A("th64"), Op.is_le)
+    mm(A(BK["nf"], 64, 128), A("rfb"), A("nfs"))
+    tt(A("k2", 0, 64), A(BK["nf"], 64, 128), A("b64"), Op.add)
+    aff(A("k2", 64, 128), A(BK["nf"], 64, 128), -1.0, rsb)
+    tt(A("k2", 128, 192), A("k2", 64, 128), A("sto"), Op.max)
 
     aff(A("mk", 0, 128), ind(A("i16"), A("lcu", 40, 48)))
     tt(A("tmb"), ind(A("nw"), A("lcu", 0, 8)), A("mk", 0, 128), Op.mult)
@@ -848,18 +755,23 @@ def rank_program(g, core, T, topo):
         a = 256 * h
         aff(A("mk", a + 128, a + 384), ind(A("i16"), A("lcu", 48 + 16 * h, 64 + 16 * h)))
         tt(A("tm", a, a + 256), ind(A("nw"), A("lcu", 8 + 16 * h, 24 + 16 * h)), A("mk", a + 128, a + 384), Op.mult)
+        move(A("tw", a, a + 256), A("tm", a, a + 256))
 
     for r in range(8):
         mm(A("pa", 64, 128), A("b2", 7 - r, 135 - r), A("gw", 64 * r, 64 * r + 64), r == 0, r == 7)
     glue(8)
-    cnt, before = A("sc", 40, 104), A("pb", 80, 81)
+    wrap16(A(BK["lm"], 224, 256), "tm", True)
+    ts(A("lm"), A(BK["lm"], 224, 256), 608.0, Op.min)
+    cnt, before, bound = A("sc", 40, 104), A("pb", 80, 81), A("pb", 81, 82)
     ts(A("fl"), A("pa", 64, 128), 100.0, Op.is_gt)
-    ts(A("nd2"), A("pa", 64, 128), 100.0, Op.is_le, float(DUM), Op.mult)
+    ts(A("n2", p0=64), A("pa", 64, 128, p0=64), 100.0, Op.is_le, float(DUM), Op.mult)
     scan(cnt, A("onesb", 0, 64), A("fl"), Op.mult, Op.add)
     mm(before, A("tri"), A("sc", 103, 104))
-    ts(A("st"), A("iou"), before, Op.subtract, hneg, Op.is_ge)
-    ts(A("n2", 0, 64), cnt, before, Op.add, -1.0, Op.add)
-    tt(A("n2", 64, 128), A("n2", 0, 64), A("nd2"), Op.max)
+    mm(bound, A("th"), A("sc", 103, 104))
+    glue(2)
+    ts(A("st"), A("uu"), before, Op.is_ge)
+    ts(A("n2", p1=64), A("sc", 39, 103, p1=64), rows(before, 0, 64), Op.add, -float(TB), Op.add)
+    ts(A("mq"), A("un"), bound, Op.is_ge)
     mm(A("pc", 320, 384), ident, cnt, True, False)
     mm(A("pc", 320, 384), A("back"), cnt, False, True)
     mm(A("pc", 384, 385), A("back"), A("sc", 103, 104))
@@ -868,59 +780,52 @@ def rank_program(g, core, T, topo):
         ts(A("dw", h, h + 64, 1, h, h + 64), A("pc", 320, 384, 1, h, h + 64), A("pc", 384, 385, 1, h, h + 64), Op.subtract)
     glue(2)
     mm(A("pa", 128, 384), A("dw"), A("st"))
-    tt(A("cm"), A("pa", 128, 384), A("uu"), Op.is_le)
-    wrap4(A("pd", 320, 352), "fw", 0, "st", True)
-    wrap4(A("pd", 320, 352), "ew", 0, "cm", False)
-    ts(A("ls"), A("pd", 320, 352), 512.0, Op.min)
-    wrap4(A("pc", 128, 160), "fw", 144, "st", True)
-    wrap4(A("pc", 128, 160), "ew", 0, "cm", False)
-    ts(A("rr"), A("pc", 128, 160), ROOT + 512.0, Op.min)
-    wrap4(A("pc", 192, 224), "fw", 288, "st", True)
     for h in range(2):
-        aff(A("tg", 256 * h, 256 * h + 256), ind(A("tm"), A("ls", 16 * h, 16 * h + 16)))
-    wrap16(A("pc", 192, 224), "tg", False)
-    tt(A("li2"), A("pc", 192, 224), A("rr"), Op.min)
+        bank = BK["tb"][h]
+        if h:
+            mm(A(bank, 256, 352), A("wt", 0, 128, p1=64), A("xg", p1=64))
+        for r in range(4 * h, 4 * h + 4):
+            mm(A(bank, 64 * (r % 4), 64 * (r % 4) + 64), A("wt", 96 * r, 96 * r + 128), A("n2"))
+        glue(4)
+        aff(A("qw", 512 + 256 * h, 768 + 352 * h), A(bank, 0, 256 + 96 * h))
+    for h in range(2):
+        aff(A("qw", 256 * h, 256 * h + 256), ind(A("qw", 512), A("lm", 16 * h, 16 * h + 16)))
+    tt(A("cm"), A("pa", 128, 384), A("uu"), Op.is_le)
+    pls, pli, plf = A(BK["ls"], 320, 352), A(BK["li"], 192, 224), A(BK["lf"], 0, 32)
+    wrap4(pls, "fw", 0, "st", True)
+    wrap4(pls, "ew", 0, "cm", False)
+    ts(A("ls"), pls, 1120.0, Op.min)
+    ts(A("rr"), pls, 512.0, Op.min, float(ROOT), Op.add)
+    wrap4(pli, "fw", 144, "st", True)
+    for h in range(2):
+        aff(A("tg", 256 * h, 256 * h + 256), ind(A("tw"), A("ls", 16 * h, 16 * h + 16)))
+    wrap16(pli, "tg", False)
+    for h in range(2):
+        c = (256 * h, 256 * h + 256)
+        tt(A("tq", *c), ind(A("qw"), A("ls", 16 * h, 16 * h + 16)), A("mq", *c), Op.mult)
+    wrap16(plf, "tq", True)
+    tt(A("li2"), pli, A("rr"), Op.min)
     copy(A("l2u"), A("li2"))
     ts(A("l2r"), A("li2"), float(ROOT), Op.is_ge, rdcol, Op.mult)
-    aff(A("l2t"), A("li2"), None, float(TB))
-    tt(A("l2s"), A("l2r"), A("l2t"), Op.add)
+    tt(A("l2s"), A("l2r"), A("li2"), Op.add)
 
-    mm(A("pb", 0, 80, p1=64), A("n2", 64, 128), A("r80"))
-    aff(A("nt", p1=64), A("pb", 0, 80, p1=64))
+    for d in range(3):
+        p = (32 * d, 32 * d + 32)
+        tt(A("lf", p[0], p[1], 1, *p), rows(plf, *p), A("l2s", 0, 32, 1, *p), Op.min)
+    glue(3)
+    mm(A(BK["r3"], 128, 224), A("r3", p1=96), A("lf", p1=96))
+    ts(A("lfu"), A(BK["r3"], 128, 224), float(TB), Op.add)
 
     wrap8(A("pz", 0, 16), "c2", A("tmb"), 128)
     wrap8(A("pz", 16, 32), "c5", A("tmb"), 128)
     scan(A("sb"), A("sel", 0, 32), A("pz", 0, 32), Op.add, Op.max)
-    tt(A("pv", 0, 64), ind(A("sb"), A("lq", 0, 4)), A("b64"), Op.add)
-    aff(A("pv", 64, 128), ind(A("sb"), A("lq", 4, 8)), None, rsb)
+    tt(A("pv", 0, 64), ind(A("sb"), A("lq", 0, 4)), A("k2", 0, 64), Op.add)
+    tt(A("pv", 64, 128), ind(A("sb"), A("lq", 4, 8)), A("k2", 128, 192), Op.add)
     tt(A("pv", 128, 192), A("pv", 0, 64), A("pv", 64, 128), Op.min)
     ts(A("lvb"), A("pv", 128, 192), ROOT + 511.0, Op.min)
 
-    asel(A("t1", TB + ROOT, TB + ROOT + 512), gw, [[0, 512]], Op.is_ge, 0, 0)
-    for d in range(3):
-        for f in range(8):
-            q = 2 * d + 1 - ((f ^ 2) >> d & 1)
-            src = A("t1", TB + ROOT, TB + ROOT + 512, 1, 16 * q, 16 * q + 16)
-            c = TB + ROOT + RS * (d + 1)
-            load("s", A("t1", c, c + 512, 1, 16 * f, 16 * f + 16), ap(src), "lrt", 3.0, [src])
-        glue(8)
-    for h in range((NDMA + 3) // 4):
-        mm(A(banks[2 - h]), A("wo", 512 * h, 512 * h + 128), gw)
-        aff(A("yt", 512 * h, 512 * h + 512), A(banks[2 - h]))
     for o in range(8):
-        c = TB + ST * o
-        if o < NDMA:
-            src = A("yt", 512 * (o // 4), 512 * (o // 4) + 512, 1, o % 4, 128, 4)
-            for f in range(0, 128, 32):
-                load("s", A("t1", c, c + 512, 1, f, f + 32), ap(src), "lt1", 1.6, [src], DMAC)
-            glue(4)
-            store("s", T.y1[16 * o:16 * o + 16, :], src[:5] + (64, 4), "oy1")
-            continue
-        mm(A(banks[o % 3]), wo(o), gw)
-        aff(A("t1", c, c + 512), A(banks[o % 3]))
-        store("s", T.y1[16 * o:16 * o + 16, :], A("t1", c, c + 512, 1, 16 * o, 16 * o + 16), "oy1")
-    for o in range(8):
-        mm(A(("pz", "pb")[o // 4], 128 + 96 * (o % 4), 224 + 96 * (o % 4)), wo(o), A("gg", 0, 96))
+        mm(A(("pz", "pb")[o // 4], 128 + 96 * (o % 4), 224 + 96 * (o % 4)), wo(o), A("gg"))
         glue(1 + o % 4)
     for o in range(8):
         c = TB + 512 + ST * o
@@ -938,32 +843,14 @@ def rank_program(g, core, T, topo):
             mm(A(banks[i], 0, 256), A("wc"), o)
             o = A("vc", 256 * i, 256 * i + 256)
             aff(o, A(banks[i], 0, 256))
-        rid, pid = topo.addr(cores[q])[:2]
         s = slot(q, rank)
-        m = sum(1 << e for e in share(rank, q, CENG))
         land = A("t1", 512 + 256 * s, 768 + 256 * s) if i >= RAW else A("vg", 256 * s, 256 * s + 256)
-        sent.append(add("g", lambda x, o=o, s=s, rid=rid, pid=pid, m=m, land=land: x.remote_dma(
-            ap(land), ap(o), T.sem["arrc%d" % s], T.sem.sent, pid, rid, m),
-            [], [o], 0.4, "sent", CENG, lat=2.3))
+        sent.append(fused([(o, q, land, "arrc%d" % s, share(rank, q, CENG))], CCALL))
 
-    for a in range(2):
-        mm(A("pd", 400 + 8 * a, 408 + 8 * a, p1=64), A("gg", 64 * a, 64 * a + 64), A("b2", 7, 64, 8))
-    glue(2)
-    ts(A("nfg", p1=64), A("pd", 400, 416, p1=64), 100.0, Op.is_le, float(DUM), Op.mult)
-    for a in range(2):
-        tt(A("nt", 8 + a, 80, 10, p1=64), A("nfg", 8 * a, 8 * a + 8, p1=64), A("cc", 8 * a, 8 * a + 8, p1=64), Op.add)
-    glue(2)
-    for j in range(4):
-        lo = (32 * (j // 2), 32 * (j // 2) + 32)
-        mm(A("pd", j, 320, 4), A("ee", 128 * (j % 2), 128 * (j % 2) + 128, 1, *lo), A("nt", 0, 80, 1, *lo))
-        glue(1 + j % 2)
-    aff(A("nw2", 0, 320), A("pd", 0, 320))
-
-    for h in range(2):
-        c = (256 * h, 256 * h + 256)
-        aff(A("v", *c), ind(t1, A("l2u", 16 * h, 16 * h + 16)))
-        mm(A(("pa", "pb")[h], 0, 256), A("wc"), A("v", *c))
-        aff(A("t1", *c), A(("pa", "pb")[h], 0, 256))
+    for h, c in enumerate(zip(VCUT, VCUT[1:])):
+        aff(A("v", *c), ind(t1, A("l2u", c[0] // 16, c[1] // 16)))
+        mm(A(BK["v"][h], 0, c[1] - c[0]), A("wc"), A("v", *c))
+        aff(A("t1", *c), A(BK["v"][h], 0, c[1] - c[0]))
     for i in range(3):
         q = [p for p in peers if turns(p)[i] == rank][0]
         s = slot(rank, q)
@@ -974,18 +861,9 @@ def rank_program(g, core, T, topo):
         mm(A(banks[i], 0, 256), A("wc"), A("vg", 256 * s, 256 * s + 256))
         aff(A("t1", 512 + 256 * s, 768 + 256 * s), A(banks[i], 0, 256))
 
-    digits("li2", "lcr2", "lcu2", 32)
-    for h in range(2):
-        c = (256 * h, 256 * h + 256)
-        aff(A("mk2", *c), ind(A("i16"), A("lcu2", 32 + 16 * h, 48 + 16 * h)))
-        tt(A("tm2", *c), ind(A("nw2"), A("lcu2", 16 * h, 16 * h + 16)), A("mk2", *c), Op.mult)
-    wrap16(A("pc", 0, 32), "tm2", True)
-    for d in range(3):
-        p = (32 * d, 32 * d + 32)
-        tt(A("lf", p[0], p[1], 1, *p), A("pc", 0, 32, 1, *p), A("l2s", 0, 32, 1, *p), Op.min)
-    glue(3)
-    mm(A("pc", 128, 224), A("r3", p1=96), A("lf", p1=96))
-    copy(A("lfu"), A("pc", 128, 224))
+    for o in range(8):
+        c = TB + ST * o
+        store("s", T.y1[16 * o:16 * o + 16, :], A("t1", c, c + 512, 1, 16 * o, 16 * o + 16), "oy1", [A("l2s")])
     zb = ["pz", "pd", "pa", "pb"]
     cuts = list(zip(CUTS, CUTS[1:]))
     for h, (a, b) in enumerate(cuts):
@@ -1000,29 +878,29 @@ def rank_program(g, core, T, topo):
         tt(A("yo", a, b), A(zb[h], 0, b - a), gd, Op.add)
         store("sa"[h % 2], T.y2[:, a:b], A("yo", a, b), "oy2")
 
-    total = emit(g, T, arrange(ops, rank))
+    total = emit(g, T, arrange(ops))
     g.sync.wait_ge(T.sem.oy1, total["oy1"])
     g.sync.wait_ge(T.sem.oy2, total["oy2"])
     g.wait_ge(T.sem.sent, total["sent"])
 
 
-TRIES = 100
-MOVES = 400000
-SHARE = False
-MOVES2 = 40000
-HEAT, HEAT2 = 0.5, 0.15
-MIX = 0.6
-PULL = 0.0
-AIM = {("yt", 0): 8.2, ("gs", 0): 7.3, ("st", 0): 9.2, ("ls", 0): 10.8, ("l2u", 0): 12.5, ("lfu", 0): 16.4}
 NDMA = 4
-DMAC = 0.12
-FIRST, BCALL = 1.3, 0.7
-KCALL, KENG = 1.5, 8
-KSEND, KARR = (5.0, 6.9, 6.9, 5.0), (10.0, 12.0, 11.4, 10.0)
-STEP, AENG, BENG, CENG = 1, 2, 2, 16
-BSEND = 8.9
-SPLIT = (0, 32)
-PACK = 2000
-LX, LQ = 3.7, 5.5
-RAW = 1
-CUTS = (0, 160, 320, 448, 512)
+AENG, BENG, CENG = 2, 2, 16
+RAW = 0
+VCUT = (0, 160, 352, 512)
+CUTS = (0, 192, 384, 512)
+BK = {"nf": "pd", "lm": "p2", "tb": ("p2", "pd"), "ls": "pc", "li": "pc", "lf": "pd", "r3": "pc",
+      "v": ("pa", "pb", "pz", "pa")}
+GAP, GAP2 = 0.24, 0.32
+VEC = 0.0009
+PE = 0.00045
+SLOW = (1.3, 1.6, 1.8)
+MIX = 1.0
+EARLY = 0.85
+LOCAL, REMOTE = 1.7, 0.9
+DMAC = 0.13
+FIRST, BCALL, CCALL = 1.3, 0.7, 0.4
+ROUNDS = ((100000, 0.35, True),) * 5 + ((200000, 0.3, False), (80000, 0.1, False))
+PACK = 400
+MEAN = 0.03
+SEED = 5

from concourse.bass import DstId, RemoteDMATransfer
from concourse.mybir import AluOpType, ActivationFunctionType

F32, BF, F16, I32, U16 = "float32", "bfloat16", "float16", "int32", "uint16"
ST = 640
ROOT = 8 * ST
TB = 1280
DUM = 8576
BIG = 16384
RS = 528

SB = {
    "xw": (4224, BF), "x0": (32, BF), "xt": (32, BF), "d1": (544, I32), "idb": (64, I32),
    "bdi": (8, I32), "bdg": (8, F32), "eef": (128, F32), "lx": (16, U16), "xs": (4112, BF), "xa": (128, BF), "xb": (128, BF), "gs": (128, BF), "th8": (8, F32),
    "nfb": (8, BF), "w1": (14208, F32), "gw": (512, BF), "gg": (96, BF), "onesb": (144, BF),
    "pk": (24, I32), "col": (40, F32), "iog": (144, BF), "iom": (128, BF), "iob": (128, BF), "bo": (136, BF),
    "trb": (128, BF), "prev": (128, BF), "io128": (136, BF), "prev1": (128, BF), "rf": (128, BF), "rfb": (128, BF),
    "idw": (136, BF), "tri": (128, BF), "dc": (32, F32), "i16": (16, F32), "qw": (1128, F32), "tq": (512, F16),
    "mq": (512, BF), "un": (512, F16), "ix": (112, BF), "e1": (96, BF), "dd": (96, BF), "th": (128, BF),
    "i8": (8, F32), "xi": (96, F32), "xg": (96, F16), "tw": (1128, F32), "tg": (512, F16), "lm": (32, U16),
    "nfs": (64, BF), "k2": (192, F32), "th64": (64, F32), "yt": (512, F32), "offh": (32, F16), "ee": (256, BF),
    "c1": (136, F32), "sel": (80, F32), "ioo": (128, BF), "obi": (12, I32), "obt": (12, F32), "m8": (32, F32),
    "lj": (16, U16), "fw": (288, BF), "ew": (144, BF), "wt": (800, BF), "c2": (136, BF), "c3": (144, BF),
    "c5": (136, BF), "b2": (136, BF), "dw": (128, BF), "rr": (32, F32), "wc": (128, F32), "wz": (128, F32), "r3": (128, F32), "b64": (64, F32),
    "sto": (64, F32), "pm": (256, F32), "lf": (96, F32), "uu": (256, F16), "l2r": (32, F32),
    "st": (256, BF), "cm": (256, BF), "la": (256, BF), "xr": (24, F16), "ls": (32, U16), "tmb": (128, F16),
    "wo": (1024, BF), "jn": (8, F32), "nw": (264, F32), "nf": (32, BF), "sc": (104, BF), "nd": (32, F16),
    "fl": (64, BF), "n2": (64, F16), "back": (128, BF), "off": (32, U16), "lq": (8, U16), "lp": (4, U16),
    "pv": (192, F32), "lvb": (64, U16), "sw": (80, F32), "sb": (32, F32), "l1u": (40, U16), "l2u": (32, U16),
    "li": (40, I32), "lcr": (80, I32), "lcu": (80, U16), "li2": (32, I32), "mk": (640, BF), "tm": (512, F16),
    "l2s": (32, F32), "lfu": (96, U16), "t1": (TB + ROOT + 4 * RS, F32), "v": (512, F32), "vb": (768, F32),
    "vg": (768, F32), "vc": (768, F32), "gd": (1536, F32), "yo": (512, F32),
}
SCRATCH = {k: ("sbuf", [128, v[0]], v[1]) for k, v in SB.items()}
PSUM = ["pa", "pb", "pc", "pd", "p0", "p1", "p2", "pz"]
for _p in PSUM:
    SCRATCH[_p] = ("psum", [128, 512], F32)
SEMAPHORES = ["cv", "ca", "ct", "cg", "lx0", "lbd", "lnb", "lx", "lxs", "lrt", "lt1", "oy1", "oy2", "arra", "arrb",
              "arrc0", "arrc1", "arrc2", "sent"]
ENG_SEM = {"v": "cv", "a": "ca", "t": "ct", "g": "cg"}
QUEUES = "vatgs-"
PLAN = []


def A(name, c0=0, c1=None, cs=1, p0=0, p1=128, ps=1):
    if c1 is None:
        c1 = SB[name][0] if name in SB else 512
    return (name, c0, c1, cs, p0, p1, ps)


def overlap(a, b):
    if a[0] != b[0] or a[1] >= b[2] or b[1] >= a[2] or a[4] >= b[5] or b[4] >= a[5]:
        return False
    if a[3] == b[3]:
        return not (a[1] - b[1]) % a[3]
    if a[3] == 1:
        a, b = b, a
    return b[3] > 1 or any(b[1] <= c < b[2] for c in range(a[1], a[2], a[3]))


def conflict(o, p):
    if p["sem"] and p["sem"] == o["sem"]:
        return False
    if o["names"].isdisjoint(p["names"]):
        return False
    if any(overlap(a, b) for a in o["w"] for b in p["w"] + p["r"]) or any(overlap(a, b) for a in o["r"] for b in p["w"]):
        return True
    return (p["e"] != o["e"] or o["e"] in "t*") and not o["banks"].isdisjoint(p["banks"])


def unfenced(o, p):
    return p["e"] == "t" and o["e"] == "t" and p["tile"] == o["tile"]


def pack(key, alt, lat, before, behind):
    n = len(alt)
    lo, hi = [[] for e in QUEUES], [[] for e in QUEUES]
    start, end, pick = [0.0] * n, [0.0] * n, [0] * n
    left = [len(p) for p in before]
    ready = [(key[i], i) for i in range(n) if not left[i]]
    while ready:
        ready.sort()
        i = ready.pop()[1]
        t0 = max([end[j] + gap for j, gap in before[i]] + [0.0])
        top = None
        for e, c in alt[i]:
            t, a, b = t0, lo[e], hi[e]
            k = len(a)
            while k and b[k - 1] > t:
                k -= 1
            while k < len(a) and t + c > a[k] + 1e-9:
                t = b[k]
                k += 1
            if top is None or t + c < top[0]:
                top = (t + c, t, e, k)
        t, start[i], e, k = top
        end[i], pick[i] = t + lat[i], e
        if e != 5:
            lo[e].insert(k, start[i])
            hi[e].insert(k, t)
        for k, gap in behind[i]:
            left[k] -= 1
            if not left[k]:
                ready.append((key[k], k))
    return sorted(range(n), key=lambda x: (start[x], x)), pick


def improve(ops):
    n = len(ops)
    pred = [[j for j in range(i) if conflict(ops[i], ops[j]) or j in ops[i]["after"]] for i in range(n)]
    above, before, behind = [0] * n, [], [[] for _ in range(n)]
    for i in range(n):
        keep = []
        for j in reversed(pred[i]):
            if not above[i] >> j & 1:
                queued = ops[i]["dma"] and j in ops[i]["after"]
                keep.append((j, -ops[j]["lat"] if queued else 0.0 if unfenced(ops[i], ops[j]) else GAP))
                behind[j].append((i, keep[-1][1]))
            above[i] |= above[j] | 1 << j
        before.append(keep)
    alt = [[(QUEUES.index(e), c) for e, f, c in o["alt"]] for o in ops]
    lat = [o["lat"] for o in ops]
    c1 = [dict(a) for a in alt]
    c2 = [{e: c * o["slow"] for e, c in a} for o, a in zip(ops, alt)]
    wait = [tuple((j, gap + lat[j], gap + lat[j] + (GAP2 - GAP) * (gap > 0)) for j, gap in b) for b in before]
    r1, r2 = lat[:], lat[:]
    for i in range(n - 1, -1, -1):
        r1[i] += max([r1[k] + gap + min(c1[k].values()) for k, gap in behind[i]] + [0.0])
        r2[i] += max([r2[k] + gap + min(c2[k].values()) for k, gap in behind[i]] + [0.0])
    seed = [SEED]

    def rand(m=1.0):
        seed[0] = (seed[0] * 1103515245 + 12345) % 2147483648
        return m * seed[0] / 2147483648

    def run(order, pick, a, old, bar):
        e1, e2 = old[0][:], old[1][:]
        f1, f2 = [0.0] * 6, [0.0] * 6
        k, left = a, 31
        while k and left:
            k -= 1
            i = order[k]
            if left >> pick[i] & 1:
                left ^= 1 << pick[i]
                f1[pick[i]], f2[pick[i]] = e1[i], e2[i]
        m1 = m2 = 0.0
        for i in order[a:]:
            e = pick[i]
            t, u = f1[e], f2[e]
            for j, gap, gap2 in wait[i]:
                x = e1[j] + gap
                if x > t:
                    t = x
                x = e2[j] + gap2
                if x > u:
                    u = x
            t += c1[i][e]
            u += c2[i][e]
            e1[i], e2[i] = t, u
            if e != 5:
                f1[e], f2[e] = t, u
            t += r1[i]
            u += r2[i]
            if t > m1 or u > m2:
                m1, m2 = max(t, m1), max(u, m2)
                if m1 + MIX * m2 > bar:
                    return None
        return m1 + MIX * m2 + MEAN * sum(e1) / n, order, pick, (e1, e2), m1, m2

    def waits(now, w):
        order, pick, end = now[1], now[2], now[3][w]
        prior, last = [None] * n, [None] * 6
        for i in order:
            prior[i], last[pick[i]] = last[pick[i]], i
        i, chain = max(range(n), key=lambda x: end[x] + lat[x]), []
        while i is not None:
            begin = end[i] - (c1, c2)[w][i][pick[i]] - 1e-7
            up = [x[0] for x in wait[i] if end[x[0]] + x[1 + w] >= begin]
            j = up[0] if up else prior[i] if pick[i] != 5 else None
            if not up and j is not None and not above[i] >> j & 1:
                chain.append((i, j))
            i = j
        return chain

    none = ([0.0] * n, [0.0] * n)
    start = best = run(*pack([r1[i] + min(c1[i].values()) for i in range(n)], alt, lat, before, behind), 0, none, 999.0)
    for moves, heat, anew in ROUNDS:
        now, chains = start if anew else best, None
        for trial in range(moves):
            order, pick = now[1:3]
            if trial % PACK == 0:
                key = [0.0] * n
                for k, x in enumerate(order):
                    key[x] = -k
                some = [a if rand() < 0.1 else [(pick[i], c1[i][pick[i]])] for i, a in enumerate(alt)]
                new = run(*pack(key, some, lat, before, behind), 0, none, 999.0)
                if new[0] <= now[0] + 0.1 * heat * (1 - trial / moves):
                    now, chains = new, None
                    best = min(best, now)
                continue
            if not chains:
                chains = [waits(now, 0), waits(now, 1)]
                place = {x: k for k, x in enumerate(order)}
            chain, u = chains[trial & 1], rand()
            if u < 0.06 or not chain:
                a = int(rand(n - 12))
                j, i = order[a], order[a + 1 + int(rand(11))]
                if above[i] >> j & 1:
                    continue
            else:
                i, j = chain[int(rand(len(chain)))]
            if u > 0.7:
                x = i if rand() < 0.5 else j
                if len(alt[x]) < 2:
                    continue
                pick = list(pick)
                pick[x] = [e for e, c in alt[x] if e != pick[x]][int(rand(len(alt[x]) - 1))]
                a = place[x]
            else:
                a, b, far = place[j], place[i], int(rand() ** 3 * 80)
                if rand() < 0.5:
                    a = max(0, a - far)
                    part, mask = order[a:b + 1], above[i] | 1 << i
                    order = (order[:a] + [x for x in part if mask >> x & 1]
                             + [x for x in part if not mask >> x & 1] + order[b + 1:])
                else:
                    b = min(n - 1, b + far)
                    part = order[a:b + 1]
                    order = (order[:a] + [x for x in part if x != j and not above[x] >> j & 1]
                             + [x for x in part if x == j or above[x] >> j & 1] + order[b + 1:])
            bar = now[0] + heat * rand() ** 3 * (1 - trial / moves)
            new = run(order, pick, a, now[3], bar - 7.0 * MEAN)
            if new and new[0] <= bar:
                end, pick = new[3][0], new[2]
                now, chains = (new[0], sorted(order, key=lambda x: end[x] - c1[x][pick[x]])) + new[2:], None
                if now[0] < best[0]:
                    best = now
    return best


def arrange(calls):
    ops, home = [], []
    for o in calls:
        if o["glue"]:
            p = ops[-1]
            c = GAP if o["e"] == "t" and o["tile"] != p["last"] else 0.0
            p.update(w=p["w"] + o["w"], r=p["r"] + o["r"], names=p["names"] | o["names"], last=o["tile"],
                     banks=p["banks"] | o["banks"],
                     alt=[(x[0], None, x[2] + y[2] + c) for x, y in zip(p["alt"], o["alt"])],
                     tile=p["tile"] if p["tile"] == o["tile"] else len(ops))
        else:
            ops.append(dict(o, last=o["tile"], after=[home[j] for j in o["after"]]))
        home.append(len(ops) - 1)
    if not PLAN:
        PLAN.extend([improve(ops), ops])
    order, pick = PLAN[0][1:3]
    place = {x: k for k, x in enumerate(order)}
    for o, i in zip(calls, home):
        o["e"], o["f"] = [x[:2] for x in o["alt"] if x[0] == QUEUES[pick[i]]][0]
    return [calls[i] for i in sorted(range(len(calls)), key=lambda x: (place[home[x]], x))]


def emit(g, T, ops):
    queue = {"v": g.vector, "a": g.scalar, "t": g.tensor, "g": g, "s": g.sync}
    n = len(ops)
    total = {}
    for o in ops:
        if o["sem"]:
            total[o["sem"]] = total.get(o["sem"], 0) + o["inc"]
    known = {e: {} for e in queue}
    clock = [{} for _ in range(n)]
    waits = [[] for _ in range(n)]
    needed = set()
    for i, o in enumerate(ops):
        e = o["e"]
        if e == "-":
            continue
        dep = {}
        for j in range(i):
            p = ops[j]
            if not unfenced(o, p) and conflict(o, p):
                dep[p["sem"] or p["e"]] = j
        k = known[e]
        for src, j in sorted(dep.items(), key=lambda t: -t[1]):
            if k.get(src, -1) >= j:
                continue
            waits[i].append(j)
            needed.add(j)
            k[src] = n if ops[j]["sem"] else j
            for s2, j2 in clock[j].items():
                if k.get(s2, -1) < j2:
                    k[s2] = j2
        clock[i] = dict(k)
    count = {}
    value = {}
    for i, o in enumerate(ops):
        if not o["sem"] and i in needed:
            count[o["e"]] = count.get(o["e"], 0) + 1
            value[i] = count[o["e"]]
    for i, o in enumerate(ops):
        if o["e"] == "-":
            continue
        q = queue[o["e"]]
        for j in waits[i]:
            if ops[j]["sem"]:
                q.wait_ge(T.sem[ops[j]["sem"]], total[ops[j]["sem"]])
            else:
                q.wait_ge(T.sem[ENG_SEM[ops[j]["e"]]], value[j])
        ins = o["f"](q)
        if o["dma"]:
            ins.then_inc(T.sem[o["sem"]], 16)
        elif i in value:
            ins.then_inc(T.sem[ENG_SEM[o["e"]]], 1)
    return total


def rank_program(g, core, T, topo):
    rank = T.rank_of(core)
    if rank is None:
        return
    cores = list(T.cores)
    peers = [q for q in range(len(cores)) if q != rank]
    Op, Fn = AluOpType, ActivationFunctionType
    ops = []
    ZC = 4096 + 32 * rank

    def ap(r):
        if r[0] == "ind":
            return ap(r[1]).indirect(ap(r[2]))
        return T[r[0]][r[4]:r[5]:r[6], r[1]:r[2]:r[3]]

    def width(r):
        return len(range(r[1], r[2], r[3]))

    def rows(r, p0, p1):
        return r[:4] + (p0, p1, 1)

    def add(e, f, w, r, c, sem=None, inc=0, dma=False, lat=0.0, after=(), alt=None, tile=None):
        ww, rr = [], []
        for x in r:
            if isinstance(x, tuple):
                rr += [x[1], x[2]] if x[0] == "ind" else [x]
        for x in w:
            if x[0] == "ind":
                ww.append(x[1])
                rr.append(x[2])
            else:
                ww.append(x)
        names = set(x[0] for x in ww + rr)
        ops.append({"e": e, "f": f, "w": ww, "r": rr, "sem": sem, "inc": inc, "dma": dma, "c": c, "lat": lat,
                    "after": after, "names": names, "banks": names & set(PSUM), "tile": tile,
                    "alt": alt or [(e, f, c)], "glue": False,
                    "slow": 1.0 if sem else SLOW[2] if len(rr) > len(r) and w[0][0] == "ind" else
                    SLOW[1] if any(isinstance(x, tuple) and x[0] == "ind" for x in r) else SLOW[0]})
        return len(ops) - 1

    def glue(n):
        for o in ops[len(ops) - n + 1:]:
            o["glue"] = True

    def narrow(r):
        return r[0] in SB and SB[r[0]][1] in (BF, F16, U16)

    def cost(o, i, cyc=1.0):
        if o[0] == "ind":
            return 0.06 + 16 * width(o[2]) * 3.8 * VEC
        if i[0] == "ind":
            return 0.06 + 16 * width(i[2]) * 1.56 * VEC
        return max(64, width(o) * cyc) * VEC

    def half(o, i):
        return cost(o, i, 0.5 if narrow(o) and narrow(i) else 1.0)

    def sc(s):
        return ap(s) if isinstance(s, tuple) else s

    def ind(win, off):
        return ("ind", win, off)

    def memset(o, c):
        add("v", lambda q: q.memset(ap(o), c), [o], [], half(o, o))

    def copy(o, i):
        add("v", lambda q: q.tensor_copy(ap(o), ap(i)), [o], [i], half(o, i))

    def ts(o, i, s1, op0, s2=None, op1=None):
        if op1 is None:
            add("v", lambda q: q.tensor_scalar(ap(o), ap(i), sc(s1), None, op0), [o], [i, s1], half(o, i))
        else:
            add("v", lambda q: q.tensor_scalar(ap(o), ap(i), sc(s1), sc(s2), op0, op1), [o], [i, s1, s2], half(o, i))

    def tt(o, a, b, op):
        add("v", lambda q: q.tensor_tensor(ap(o), ap(a), ap(b), op), [o], [a, b],
            cost(o, a, 1.0 if a[0] in PSUM or b[0] in PSUM else 2.0))

    def scan(o, a, b, op0, op1, first=0.0):
        add("v", lambda q: q.tensor_tensor_scan(ap(o), ap(a), ap(b), sc(first), op0, op1), [o], [a, b, first], half(o, a))

    def aff(o, i, scale=None, bias=None):
        kw = {}
        if bias is not None:
            kw["bias"] = bias
        if scale is not None:
            kw["scale"] = scale

        def on_a(q):
            return q.activation(ap(o), ap(i), Fn.Identity if kw else Fn.Copy, **{k: sc(x) for k, x in kw.items()})

        def on_v(q):
            if not kw:
                return q.tensor_copy(ap(o), ap(i))
            if scale is None:
                return q.tensor_scalar(ap(o), ap(i), sc(bias), None, Op.add)
            if bias is None:
                return q.tensor_scalar(ap(o), ap(i), sc(scale), None, Op.mult)
            return q.tensor_scalar(ap(o), ap(i), sc(scale), sc(bias), Op.mult, Op.add)
        alt = [("a", on_a, cost(o, i) + 0.015), ("v", on_v, half(o, i))]
        add("*", on_a, [o], [i, scale, bias], alt[0][2], alt=alt)

    def step(o, i, at, size=1.0):
        s = size if at else -size
        alt = [("a", lambda q: q.activation(ap(o), ap(i), Fn.Relu, scale=s, bias=size - s * at), cost(o, i) + 0.015),
               ("v", lambda q: q.tensor_scalar(ap(o), ap(i), float(at), size, Op.is_equal, Op.mult), half(o, i))]
        add("*", alt[0][1], [o], [i], alt[0][2], alt=alt)

    def fill(o, c):
        src = A("onesb", 0, width(o), 1, o[4], o[5])
        alt = [("a", lambda q: q.activation(ap(o), ap(src), Fn.Identity, scale=float(c)), cost(o, o) + 0.015),
               ("v", lambda q: q.memset(ap(o), c), half(o, o)),
               ("g", lambda q: q.iota(ap(o), [[0, width(o)]], int(c), 0, allow_small_or_imprecise_dtypes=True),
                0.16 + width(o) * 2 * VEC)]
        if SB[o[0]][1] == I32:
            return add("*", alt[1][1], [o], [], alt[1][2], alt=alt[1:])
        add("*", alt[0][1], [o], [src], alt[0][2], alt=alt)

    def mm(o, l, r, start=True, stop=True):
        add("t", lambda q: q.matmul(ap(o), ap(l), ap(r), start, stop), [o], [l, r],
            max(64, width(r)) * PE * (4 if SB[l[0]][1] == F32 else 1), tile=(l[4], l[5]))

    def iota(o, pat, base, cm):
        kw = {} if SB[o[0]][1] == I32 else {"allow_small_or_imprecise_dtypes": True}
        add("g", lambda q: q.iota(ap(o), pat, base, cm, **kw), [o], [], 0.16 + width(o) * 2 * VEC)

    def asel(o, i, pat, cmp, base, cm):
        add("g", lambda q: q.affine_select(ap(o), ap(i), pat, cmp, 0.0, base, cm), [o], [i],
            0.21 + width(o) * 2 * VEC)

    def move(o, i):
        asel(o, i, [[0, width(o)]], Op.is_ge, 0, 0)
        on_g = ops.pop()["alt"]
        aff(o, i)
        ops[-1]["alt"] += on_g

    def load(e, o, src, sem, lat, r=()):
        def f(q):
            return q.dma_start(ap(o), src)
        return add(e[0], f, [o], list(r), DMAC, sem, 16, True, lat, alt=[(x, f, DMAC) for x in e])

    def store(e, dst, i, sem, behind=()):
        add(e, lambda q: q.dma_start(dst, ap(i)), [], [i] + list(behind), DMAC, sem, 16, True, LOCAL)

    def slot(at, q):
        return q if q < at else q - 1

    def share(at, q, w):
        en = topo.engines(cores[at], cores[q])
        return en[:w] if 3 * w > len(en) else en[slot(at, q):3 * w:3]

    def fused(trs, c):
        tr = [RemoteDMATransfer(dst_ids=[DstId(rid=topo.addr(cores[q])[0], pnc=topo.addr(cores[q])[1])],
                                dma_engine_mask=sum(1 << e for e in en), remote_sem=T.sem[sem],
                                srcs=[ap(src)], dsts=[ap(dst)]) for src, q, dst, sem, en in trs]
        return add("g", lambda x: x.remote_dma_fused(tr, local_sem=T.sem.sent), [], [t[0] for t in trs], c,
                   "sent", sum(len(t[4]) for t in trs), lat=REMOTE)

    def wrap8(o, c, src, n):
        for b in range(8):
            mm(o, A(c, 7 - b, 135 - b), A(src[0], src[1] + b, src[1] + n, 8), b == 0, b == 7)
        glue(8)

    def wrap4(o, c, c0, src, start):
        for b in range(8):
            mm(o, A(c, c0 + 14 - 2 * b, c0 + 142 - 2 * b), A(src, b, 256, 8), start and b == 0, not start and b == 7)
            glue(1 + b % 4)

    def wrap16(o, src, start):
        for b in range(16):
            mm(o, A("c3", 15 - b, 143 - b), A(src, b, 512, 16), start and b == 0, b == 15)
        glue(16)

    def wo(o):
        return A("wo", 512 * (o // 4) + o % 4, 512 * (o // 4) + 512, 4)

    def block(gr):
        return 4 * (gr % 2) + gr // 2

    (g8col, rcol, kcol, hcol, acol, jcol, code, pcol, ccol, b1col, k6col, zc0, zc, h35, bcol, lxcol, ecol, q0col,
     q1col, gcol, onec, rhalf, nsb, sbz, pw, k67, hp, xt, x1, x2, d32, d33, wcol, r1col, e63, m63, rdcol,
     rsb) = [A("col", i, i + 1) for i in range(38)]
    ident, pi = A("idw", 1, 129), A("pk", 23, 24)

    iota(pi, [[0, 1]], 0, 1)
    iota(A("idb"), [[32, 2], [1, 32]], 0, 32)
    for h in range(2):
        load("sa", A("x0", 16 * h, 16 * h + 16), T.x[0, 2048 * h:2048 * h + 2048], "lx0", LOCAL - 0.2)
    load("sa", A("bdi", p1=16), T.bd[:, :], "lbd", LOCAL - 0.3)
    for k in range(8):
        c = 512 * block(k)
        load("sa", A("d1", 16, 528, 1, 16 * k, 16 * k + 12, 2), T.nb[:, c:c + 512], "lnb", LOCAL)
    for h in range(2):
        load("s", A("d1", 16, 528, 1, 12 + 2 * h, 128, 16), ap(A("idb", 32 * h, 32 * h + 32)), "lnb", LOCAL - 0.2,
             [A("idb")])
        load("sa", A("d1", 16, 528, 1, 64 * h + 1, 64 * h + 64, 2), T.nb[0:4, :], "lnb", LOCAL)
    load("sa", A("xs", 16, 4112, p1=16), T.x[:, :], "lxs", LOCAL + 0.2)
    small = [i for i, o in enumerate(ops) if o["dma"]]
    for k in range(7):
        ops[load("sa", A("xw", 0, 4096, 1, 16 * k, 16 * k + 16), T.x[:, :], "lx", LOCAL + 1.5)]["after"] = small

    memset(A("onesb"), 1.0)
    for c in (0, 528):
        fill(A("d1", c, c + 16), 0)
    iota(A("iom"), [[0, 8], [1, 16]], 0, 0)
    iota(A("iog"), [[1, 9], [0, 16]], 0, 0)
    iota(A("iob"), [[1, 4], [4, 2], [0, 16]], 0, 0)
    iota(A("dc"), [[128, 32]], DUM, 8)
    for c in range(128, 640, 128):
        fill(A("w1", c, c + 128), 0.0)
    fill(A("sc", 0, 40, 39), 0.0)
    fill(A("sel"), -49152.0)
    fill(A("xw", ZC, ZC + 32), 0.0)
    for c in ("c1", "b2", "lf", "dw", "ew", "c2", "c3", "c5"):
        fill(A(c), 0.0)
    for c in (0, 144):
        fill(A("fw", c, c + 144), 0.0)
    fill(A("t1", TB + ROOT + 512, TB + ROOT + 4 * RS, RS), 0.0)
    ts(A("pk", 16, 17), pi, 7, Op.bitwise_and)
    ts(A("pk", 17, 18), pi, 15, Op.bitwise_and)
    ts(A("pk", 18, 19), pi, 4, Op.logical_shift_right)
    ts(A("pk", 19, 20), pi, 4, Op.logical_shift_right, 1, Op.bitwise_and)
    ts(A("pk", 20, 21), pi, 6, Op.logical_shift_right)
    ts(A("pk", 21, 22), pi, 63, Op.bitwise_and)
    ts(A("pk", 22, 23), pi, 3, Op.logical_shift_right)
    aff(A("col", 0, 8), A("pk", 16, 24))
    iota(A("pk", 0, 8), [[4, 2], [-2, 2], [1, 2]], 2, 0)
    iota(A("pk", 8, 16), [[1, 8]], 0, 0)
    ts(A("bo"), A("iog", 0, 136), kcol, Op.is_equal)
    ts(A("prev"), A("iog", 0, 128), kcol, Op.is_gt)
    scan(A("io128"), A("onesb", 0, 136), A("onesb", 0, 136), Op.add, Op.mult, -2.0)
    ts(A("trb"), A("io128", 1, 129), pcol, Op.is_gt, -1.0, Op.mult)
    ts(A("idw"), A("io128"), pcol, Op.is_equal)
    aff(h35, hcol, 3.5)
    aff(bcol, kcol, 0.5, h35)
    ts(A("prev1"), A("iob"), bcol, Op.is_gt)
    aff(lxcol, bcol, -512.0, 16.0)
    ts(A("rf"), A("iom"), rcol, Op.is_equal)
    asel(A("tri"), A("onesb", 0, 128), [[0, 2], [1, 64]], Op.is_gt, 0, -1)
    ts(A("ee", 0, 128), A("rf"), hcol, Op.subtract, 0.0, Op.max)
    aff(A("ee", 128, 256), A("rf"), hcol)
    ts(A("i16"), A("iom", 0, 16), rcol, Op.is_equal)
    ts(onec, A("i16", 14, 15), A("i16", 12, 13), Op.subtract, 16.0, Op.mult)
    aff(ccol, onec, -ZC / 512.0)
    aff(rhalf, rcol, 0.5)
    ts(A("c1", 7, 112, 8), A("iog", 0, 112, 8), rhalf, Op.is_equal, ccol, Op.add)
    ts(ecol, bcol, kcol, Op.subtract, onec, Op.mult)
    aff(A("c1", 103, 112, 8), A("c1", 103, 112, 8), None, ecol)
    memset(A("obi", 0, 9, p0=96), 0)
    for d in range(3):
        ts(A("obi", 0, 9, 1, 32 * d, 32 * d + 32), A("pk", 8, 17, 1, 32 * d, 32 * d + 32), 1 << d, Op.bitwise_and)
    ts(b1col, rcol, 8.0, Op.is_lt, 65536.0, Op.mult)
    aff(A("sel", 1, 80, 2), A("sel", 0, 80, 2), None, b1col)
    aff(sbz, b1col, 0.25, -float(ZC))
    aff(pw, A("obi", 7, 8), float(ST))
    aff(k67, A("prev", 96, 97), -1.0, 1.0)
    aff(hp, pw, hcol, k67)
    ts(A("obt", 0, 9), A("obi", 0, 9), float(ST), Op.mult, hp, Op.is_equal)
    aff(k6col, A("bo", 96, 97), 0.625)
    fill(A("xs", 0, 16), 0.0)
    memset(A("lx", 8, 16), 0)
    aff(A("eef", p1=16), A("rf", p1=16))
    aff(A("m8", 0, 8), A("obt", 0, 8), 0.125, k6col)
    step(e63, jcol, 63, float(BIG))
    aff(m63, e63, 1.0 / BIG, -1.0)
    aff(A("back"), A("idw", 0, 128), m63)
    for c in range(0, 512, 128):
        aff(A("un", c, c + 128), A("io128", 1, 129), None, float(c))
        aff(A("tw", 512 + c, 640 + c), A("un", c, c + 128), 1.0 / 16)
    aff(A("uu"), A("un", 0, 512, 2), None, acol)
    asel(A("pm", 0, 128), A("onesb", 0, 128), [[-64, 2], [16, 4], [-1, 16]], Op.is_equal, -48, 1)
    asel(A("pm", 128, 256), A("onesb", 0, 128), [[64, 2], [32, 2], [-1, 32]], Op.is_equal, -96, 1)
    aff(A("rfb"), A("rf"), float(DUM))
    aff(A("th8"), A("bo", 0, 128, 16), 1000.0, -1000.0)
    aff(A("th64"), A("bo", 0, 128, 2), 1100.0, -1000.0)
    ts(A("i8"), A("iom", 0, 8), g8col, Op.is_equal)
    for c in (7, 71):
        aff(A("b2", c, c + 57, 8), A("m8", 0, 8), A("i16", 0, 1))
    for o in range(8):
        aff(wo(o), A("rf"), A("m8", o, o + 1))
    cut = min(2 + 2 * rank, 6)
    aff(A("jn", 0, cut), A("io128", 33, 33 + cut), 16.0, rcol)
    aff(A("jn", cut, 8), A("io128", 31 + cut, 39), 16.0, rcol)
    iota(A("ioo"), [[0, 2], [1, 8], [32, 8]], 0, 0)
    aff(xt, A("obi", 8, 9), -2.0 * ST, pw)
    aff(x2, g8col, float(ST), xt)
    aff(x1, A("obt", 8, 9), -512.0, 512.0)
    for i, x in enumerate((x1, x2)):
        aff(A("xr", 9 * i, 9 * i + 9), A("bo", 0, 136, 16), x)
    aff(r1col, rcol, None, 1.0)
    ts(A("la", 0, 128), A("ioo"), rcol, Op.is_equal)
    ts(A("la", 128, 256), A("ioo"), r1col, Op.is_equal, -1.0, Op.mult)
    mm(A("p1", 0, 18), A("la", 0, 128), A("xr", 0, 18), True, False)
    mm(A("p1", 0, 18), A("la", 128, 256), A("xr", 0, 18), False, True)
    aff(d33, A("i8", 0, 1), -512.0, 64.0)
    step(wcol, jcol, 0)
    aff(d32, wcol, 448.0, d33)
    for h in range(2):
        p = (64 * h, 64 * h + 64)
        aff(A("fw", 14 + h, 144, 16, *p), A("p1", 0, 9, 1, *p), None, rows(d32, *p))
        aff(A("fw", 158 + h, 288, 16, *p), A("p1", 9, 18, 1, *p))
    glue(4)
    for h in range(2):
        p = (64 * h, 64 * h + 64)
        aff(A("ew", 14 + h, 128, 16, *p), A("onesb", 0, 8, 1, *p), rows(e63, *p), 1.0)
    aff(A("c2", 7, 128, 8), A("bo", 0, 128, 8))
    aff(A("c3", 15, 128, 16), A("bo", 0, 128, 16))
    aff(A("c5", 7, 128, 8), A("bo", 96, 112))
    iota(A("ix", 0, 32), [[0, 2], [2, 8], [-1, 2]], 1, 0)
    for k in range(2, 6):
        iota(A("ix", 16 * k, 16 * k + 16), [[[4, 4], [-2, 2], [1, 2]], [[8, 2], [-4, 2], [1, 4]]][k // 4], 1 << k // 2, 0)
    aff(A("ix", 96, 104), A("iom", 0, 8))
    ts(A("e1"), A("ix", 0, 96), code, Op.is_equal)
    tt(A("dd", 1, 96), A("e1", 1, 96), A("e1", 0, 95), Op.subtract)
    aff(A("dd", 0, 96, 8), A("e1", 0, 96, 8))
    fill(A("wt", 768, 800), 0.0)
    for r in range(8):
        aff(A("wt", 96 * r, 96 * r + 96), A("dd"), A("i8", r, r + 1))
    asel(A("th"), A("onesb", 0, 128), [[0, 16], [8, 8]], Op.is_gt, 0, -1)
    for c in ("qw", "tw"):
        aff(A(c, 1120, 1121), A("i8", 0, 1), float(DUM))
    iota(A("xi", p1=64), [[128, 6], [1, 16]], 512 - TB, 2)
    aff(A("xg", p1=64), A("xi", p1=64))
    copy(A("lj"), A("pk", 0, 16))
    aff(zc0, A("prev", 96, 97), 1.0 / 64)
    aff(zc, k6col, 0.625, zc0)
    aff(A("m8", 16, 24), A("obt", 0, 8), 3.0 / 64, zc)
    tt(A("wc"), ind(A("m8", 0, 8), A("lj", 0, 8)), A("rf"), Op.mult)
    tt(A("wz"), ind(A("m8", 16, 24), A("lj", 8, 16)), A("rf"), Op.mult)
    aff(A("m8", 24, 32), A("obt", 0, 8), -1.0, 1.0)
    aff(A("m8", 24, 32, 1, 32, 64), A("obt", 0, 8, 1, 32, 64))
    tt(A("r3"), ind(A("m8", 24, 32), A("lj", 8, 16)), A("rf"), Op.mult)
    ts(gcol, kcol, hcol, Op.subtract, 16.0, Op.mult)
    aff(rsb, b1col, -0.25, float(ROOT))
    aff(rdcol, gcol, RS / 32.0, float(RS))
    aff(q1col, b1col, -2.0 / 65536, 19.0)
    aff(q0col, A("obt", 8, 9), -16.0, q1col)
    aff(nsb, b1col, -0.25)
    ts(A("lq", 0, 4), A("iom", 0, 4), 4.0, Op.mult, q0col, Op.add)
    ts(A("lq", 4, 8), A("iom", 0, 4), 4.0, Op.mult, q1col, Op.add)
    ts(A("lp"), A("onesb", 0, 4), g8col, Op.mult, gcol, Op.add)
    aff(A("b64"), ind(A("ix"), A("lp")), float(ST), nsb)
    aff(A("sto"), A("iom", 0, 128, 2), ST / 2.0, nsb)
    for o in ops:
        if not o["dma"]:
            o["alt"] = [(e, f, c * (EARLY if e in "va" else 1.0)) for e, f, c in o["alt"]]
            o["slow"] /= EARLY

    add("v", lambda q: q.transpose(ap(A("xt")), ap(A("x0"))), [A("xt")], [A("x0")], 64 * VEC)
    ts(A("nf"), A("xt"), 0.0, Op.is_le)
    scan(A("sc", 1, 33), A("onesb", 0, 32), A("nf"), Op.add, Op.subtract)
    tt(A("nd"), A("nf"), A("dc"), Op.mult)
    p1, pc = A("pb", 0, 32), A("pb", 32, 33)
    mm(p1, A("trb"), A("nf"), True, False)
    mm(p1, A("prev"), A("nf"), False, False)
    glue(2)
    mm(p1, ident, A("nd"), False, False)
    mm(p1, A("bo", 0, 128), A("sc", 0, 32), False, True)
    mm(pc, A("prev1"), A("sc", 32, 33))
    glue(2)
    ts(A("off"), p1, pc, Op.add, rcol, Op.add)
    ts(A("offh"), p1, pc, Op.add, rcol, Op.add)

    aff(A("bdg", p1=16), A("bdi", p1=16))
    mm(A("pz", 0, 8), A("eef", p1=16), A("bdg", p1=16))
    ts(A("lx", 0, 8), A("pz", 0, 8), lxcol, Op.add, 528.0, Op.min)
    ts(A("lx", 8, 16, p1=16), A("bdi", p1=16), 16.0, Op.add)
    aff(A("xa"), ind(A("xs"), A("lx", 8, 16)))
    mm(A("p0", 0, 128), A("rf", p1=16), A("xa", p1=16))
    aff(A("xb"), A("p0", 0, 128))
    sa = fused([(A("xb", 32 * q, 32 * q + 32), q, A("xw", ZC, ZC + 32), "arra", share(rank, q, AENG)) for q in peers],
               FIRST)
    add("-", None, [A("xw", 4096 + 32 * q, 4128 + 32 * q) for q in peers], [], 0.0, "arra", 3 * AENG, after=(sa,))
    banks = ["p0", "p1", "p2"]

    mm(A("pz", 0, 8), A("xw", 4096, 4224, p1=16), A("rf", 0, 128, 16, p1=16))
    tt(A("nfb"), A("pz", 0, 8), A("th8"), Op.is_le)
    mm(A("pz", 8, 16), A("rfb"), A("nfb"))
    tt(A("nw", 256, 264), A("pz", 8, 16), A("jn"), Op.add)

    aff(A("w1", 0, 128), ind(A("d1"), A("lx", 0, 8)))
    wrap8(A("pc", 0, 16), "c1", A("w1"), 128)
    copy(ind(A("w1", 128), A("off")), A("d1", 16, 528))
    for gr in range(8):
        lo, c = (32 * (gr // 2), 32 * (gr // 2) + 32), 128 * (gr % 2)
        mm(A("pd", 32 * block(gr), 32 * block(gr) + 32), A("ee", c, c + 128, 1, *lo), A("offh", 0, 32, 1, *lo))
        glue(1 + gr % 2)
    aff(A("nw", 0, 256), A("pd", 0, 256))
    wrap8(A("pc", 16, 80), "c1", A("w1", 128), 512)
    scan(A("sw"), A("sel"), A("pc", 0, 80), Op.add, Op.max)
    ts(A("l1u"), A("sw", 1, 80, 2), sbz, Op.subtract)
    aff(A("gs"), ind(A("xw"), A("l1u", 0, 8)))
    ts(A("li"), A("sw", 1, 80, 2), sbz, Op.subtract)
    ts(A("lcr", 40, 80), A("li"), 15, Op.bitwise_and)
    ts(A("lcr", 0, 40), A("li"), 4, Op.logical_shift_right)
    copy(A("lcu"), A("lcr"))
    for h in range(2):
        aff(A("gw", 256 * h, 256 * h + 256), ind(A("xw"), A("l1u", 8 + 16 * h, 24 + 16 * h)))
    gw = A("gw")

    sb = fused([(A("gs", 32 * q, 32 * q + 32), q, A("gg", 32 * slot(q, rank), 32 * slot(q, rank) + 32), "arrb",
                 share(rank, q, BENG)) for q in peers], BCALL)
    add("-", None, [A("gg")], [], 0.0, "arrb", 3 * BENG, after=(sb,))

    asel(A("t1", TB + ROOT, TB + ROOT + 512), gw, [[0, 512]], Op.is_ge, 0, 0)
    for d in range(3):
        for f in range(8):
            q = 2 * d + 1 - ((f ^ 2) >> d & 1)
            src = A("t1", TB + ROOT, TB + ROOT + 512, 1, 16 * q, 16 * q + 16)
            c = TB + ROOT + RS * (d + 1)
            load("sa", A("t1", c, c + 512, 1, 16 * f, 16 * f + 16), ap(src), "lrt", LOCAL + 1.0, [src])
            glue(1 + f % 2)
    mm(A(banks[2]), A("wo", 0, 128), gw)
    aff(A("yt"), A(banks[2]))
    for o in range(8):
        c = TB + ST * o
        if o < NDMA:
            src = A("yt", 0, 512, 1, o, 128, 4)
            for f in range(0, 128, 32):
                load("s", A("t1", c, c + 512, 1, f, f + 32), ap(src), "lt1", LOCAL - 0.2, [src])
            glue(4)
            continue
        mm(A(banks[o % 2]), wo(o), gw)
        aff(A("t1", c, c + 512), A(banks[o % 2]))

    for i in range(4):
        mm(A(BK["nf"], 16 * i, 16 * i + 16), A("gs"), A("b2", 7, 135, 8))
    glue(4)
    tt(A("nfs"), A(BK["nf"], 0, 64), A("th64"), Op.is_le)
    mm(A(BK["nf"], 64, 128), A("rfb"), A("nfs"))
    tt(A("k2", 0, 64), A(BK["nf"], 64, 128), A("b64"), Op.add)
    aff(A("k2", 64, 128), A(BK["nf"], 64, 128), -1.0, rsb)
    tt(A("k2", 128, 192), A("k2", 64, 128), A("sto"), Op.max)

    aff(A("mk", 0, 128), ind(A("i16"), A("lcu", 40, 48)))
    tt(A("tmb"), ind(A("nw"), A("lcu", 0, 8)), A("mk", 0, 128), Op.mult)
    for h in range(2):
        a = 256 * h
        aff(A("mk", a + 128, a + 384), ind(A("i16"), A("lcu", 48 + 16 * h, 64 + 16 * h)))
        tt(A("tm", a, a + 256), ind(A("nw"), A("lcu", 8 + 16 * h, 24 + 16 * h)), A("mk", a + 128, a + 384), Op.mult)
        move(A("tw", a, a + 256), A("tm", a, a + 256))

    for r in range(8):
        mm(A("pa", 64, 128), A("b2", 7 - r, 135 - r), A("gw", 64 * r, 64 * r + 64), r == 0, r == 7)
    glue(8)
    wrap16(A(BK["lm"], 224, 256), "tm", True)
    ts(A("lm"), A(BK["lm"], 224, 256), 608.0, Op.min)
    cnt, before, bound = A("sc", 40, 104), A("pb", 80, 81), A("pb", 81, 82)
    ts(A("fl"), A("pa", 64, 128), 100.0, Op.is_gt)
    ts(A("n2", p0=64), A("pa", 64, 128, p0=64), 100.0, Op.is_le, float(DUM), Op.mult)
    scan(cnt, A("onesb", 0, 64), A("fl"), Op.mult, Op.add)
    mm(before, A("tri"), A("sc", 103, 104))
    mm(bound, A("th"), A("sc", 103, 104))
    glue(2)
    ts(A("st"), A("uu"), before, Op.is_ge)
    ts(A("n2", p1=64), A("sc", 39, 103, p1=64), rows(before, 0, 64), Op.add, -float(TB), Op.add)
    ts(A("mq"), A("un"), bound, Op.is_ge)
    mm(A("pc", 320, 384), ident, cnt, True, False)
    mm(A("pc", 320, 384), A("back"), cnt, False, True)
    mm(A("pc", 384, 385), A("back"), A("sc", 103, 104))
    glue(3)
    for h in (0, 64):
        ts(A("dw", h, h + 64, 1, h, h + 64), A("pc", 320, 384, 1, h, h + 64), A("pc", 384, 385, 1, h, h + 64), Op.subtract)
    glue(2)
    mm(A("pa", 128, 384), A("dw"), A("st"))
    for h in range(2):
        bank = BK["tb"][h]
        if h:
            mm(A(bank, 256, 352), A("wt", 0, 128, p1=64), A("xg", p1=64))
        for r in range(4 * h, 4 * h + 4):
            mm(A(bank, 64 * (r % 4), 64 * (r % 4) + 64), A("wt", 96 * r, 96 * r + 128), A("n2"))
        glue(4)
        aff(A("qw", 512 + 256 * h, 768 + 352 * h), A(bank, 0, 256 + 96 * h))
    for h in range(2):
        aff(A("qw", 256 * h, 256 * h + 256), ind(A("qw", 512), A("lm", 16 * h, 16 * h + 16)))
    tt(A("cm"), A("pa", 128, 384), A("uu"), Op.is_le)
    pls, pli, plf = A(BK["ls"], 320, 352), A(BK["li"], 192, 224), A(BK["lf"], 0, 32)
    wrap4(pls, "fw", 0, "st", True)
    wrap4(pls, "ew", 0, "cm", False)
    ts(A("ls"), pls, 1120.0, Op.min)
    ts(A("rr"), pls, 512.0, Op.min, float(ROOT), Op.add)
    wrap4(pli, "fw", 144, "st", True)
    for h in range(2):
        aff(A("tg", 256 * h, 256 * h + 256), ind(A("tw"), A("ls", 16 * h, 16 * h + 16)))
    wrap16(pli, "tg", False)
    for h in range(2):
        c = (256 * h, 256 * h + 256)
        tt(A("tq", *c), ind(A("qw"), A("ls", 16 * h, 16 * h + 16)), A("mq", *c), Op.mult)
    wrap16(plf, "tq", True)
    tt(A("li2"), pli, A("rr"), Op.min)
    copy(A("l2u"), A("li2"))
    ts(A("l2r"), A("li2"), float(ROOT), Op.is_ge, rdcol, Op.mult)
    tt(A("l2s"), A("l2r"), A("li2"), Op.add)

    for d in range(3):
        p = (32 * d, 32 * d + 32)
        tt(A("lf", p[0], p[1], 1, *p), rows(plf, *p), A("l2s", 0, 32, 1, *p), Op.min)
    glue(3)
    mm(A(BK["r3"], 128, 224), A("r3", p1=96), A("lf", p1=96))
    ts(A("lfu"), A(BK["r3"], 128, 224), float(TB), Op.add)

    wrap8(A("pz", 0, 16), "c2", A("tmb"), 128)
    wrap8(A("pz", 16, 32), "c5", A("tmb"), 128)
    scan(A("sb"), A("sel", 0, 32), A("pz", 0, 32), Op.add, Op.max)
    tt(A("pv", 0, 64), ind(A("sb"), A("lq", 0, 4)), A("k2", 0, 64), Op.add)
    tt(A("pv", 64, 128), ind(A("sb"), A("lq", 4, 8)), A("k2", 128, 192), Op.add)
    tt(A("pv", 128, 192), A("pv", 0, 64), A("pv", 64, 128), Op.min)
    ts(A("lvb"), A("pv", 128, 192), ROOT + 511.0, Op.min)

    for o in range(8):
        mm(A(("pz", "pb")[o // 4], 128 + 96 * (o % 4), 224 + 96 * (o % 4)), wo(o), A("gg"))
        glue(1 + o % 4)
    for o in range(8):
        c = TB + 512 + ST * o
        aff(A("t1", c, c + 96), A(("pz", "pb")[o // 4], 128 + 96 * (o % 4), 224 + 96 * (o % 4)))
        glue(1 + o % 4)
    t1 = A("t1", TB, TB + ROOT + RS)

    def turns(at):
        return sorted((at ^ k for k in range(1, len(cores))), key=lambda q: topo.die(cores[q]) == topo.die(cores[at]))
    sent = []
    for i, q in enumerate(turns(rank)):
        o = A("vb", 256 * i, 256 * i + 256)
        aff(o, ind(t1, A("lvb", 16 * q, 16 * q + 16)))
        if i >= RAW:
            mm(A(banks[i], 0, 256), A("wc"), o)
            o = A("vc", 256 * i, 256 * i + 256)
            aff(o, A(banks[i], 0, 256))
        s = slot(q, rank)
        land = A("t1", 512 + 256 * s, 768 + 256 * s) if i >= RAW else A("vg", 256 * s, 256 * s + 256)
        sent.append(fused([(o, q, land, "arrc%d" % s, share(rank, q, CENG))], CCALL))

    for h, c in enumerate(zip(VCUT, VCUT[1:])):
        aff(A("v", *c), ind(t1, A("l2u", c[0] // 16, c[1] // 16)))
        mm(A(BK["v"][h], 0, c[1] - c[0]), A("wc"), A("v", *c))
        aff(A("t1", *c), A(BK["v"][h], 0, c[1] - c[0]))
    for i in range(3):
        q = [p for p in peers if turns(p)[i] == rank][0]
        s = slot(rank, q)
        land = A("t1", 512 + 256 * s, 768 + 256 * s) if i >= RAW else A("vg", 256 * s, 256 * s + 256)
        add("-", None, [land], [], 0.0, "arrc%d" % s, CENG, after=(sent[i],))
        if i >= RAW:
            continue
        mm(A(banks[i], 0, 256), A("wc"), A("vg", 256 * s, 256 * s + 256))
        aff(A("t1", 512 + 256 * s, 768 + 256 * s), A(banks[i], 0, 256))

    for o in range(8):
        c = TB + ST * o
        store("s", T.y1[16 * o:16 * o + 16, :], A("t1", c, c + 512, 1, 16 * o, 16 * o + 16), "oy1", [A("l2s")])
    zb = ["pz", "pd", "pa", "pb"]
    cuts = list(zip(CUTS, CUTS[1:]))
    for h, (a, b) in enumerate(cuts):
        mm(A(zb[h], 0, b - a), A("wz"), A("v", a, b), True, False)

    for h, (a, b) in enumerate(cuts):
        for j, d in enumerate((0, 2, 1)):
            gd = A("gd", 512 * d + a, 512 * d + b)
            aff(gd, ind(A("t1"), A("lfu", gd[1] // 16, gd[2] // 16)), 0.125)
            if j < 2:
                mm(A(zb[h], 0, b - a), A("pm", 128 * j, 128 * j + 128), gd, False, j == 1)
        tt(A("yo", a, b), A(zb[h], 0, b - a), gd, Op.add)
        store("sa"[h % 2], T.y2[:, a:b], A("yo", a, b), "oy2")

    total = emit(g, T, arrange(ops))
    g.sync.wait_ge(T.sem.oy1, total["oy1"])
    g.sync.wait_ge(T.sem.oy2, total["oy2"])
    g.wait_ge(T.sem.sent, total["sent"])


NDMA = 4
AENG, BENG, CENG = 2, 2, 16
RAW = 0
VCUT = (0, 160, 352, 512)
CUTS = (0, 192, 384, 512)
BK = {"nf": "pd", "lm": "p2", "tb": ("p2", "pd"), "ls": "pc", "li": "pc", "lf": "pd", "r3": "pc",
      "v": ("pa", "pb", "pz", "pa")}
GAP, GAP2 = 0.24, 0.32
VEC = 0.0009
PE = 0.00045
SLOW = (1.3, 1.6, 1.8)
MIX = 1.0
EARLY = 0.85
LOCAL, REMOTE = 1.7, 0.9
DMAC = 0.13
FIRST, BCALL, CCALL = 1.3, 0.7, 0.4
ROUNDS = ((100000, 0.35, True),) * 5 + ((200000, 0.3, False), (80000, 0.1, False))
PACK = 400
MEAN = 0.03
SEED = 5
